import numpy as np
import ml_dtypes


def mxq(x, axis, fmt="e4m3"):
    dtype, down = {"e4m3": (ml_dtypes.float8_e4m3fn, 7), "e5m2": (ml_dtypes.float8_e5m2, 14)}[fmt]
    v = np.moveaxis(np.asarray(x, np.float32).astype(ml_dtypes.bfloat16).astype(np.float64), axis, -1)
    blocks = v.reshape(v.shape[:-1] + (-1, 32))
    amax = np.abs(blocks).max(-1, keepdims=True)
    byte = np.maximum(np.where(amax > 0, np.frexp(amax)[1] - 1 + 127, 0) - down, 1)
    scale = np.exp2(byte - 127.0)
    codes = (blocks / scale).astype(np.float32).astype(dtype).astype(np.float64)
    return np.moveaxis((codes * scale).reshape(v.shape), -1, axis)


WIDE = False


def mx_kscale(k):
    if not WIDE:
        return np.ones(k)
    levels = np.array([10, -10, 5, -5, 0])
    if k % 512:
        return np.exp2(np.random.permutation(np.resize(levels, k // 32))).repeat(32)
    a = np.empty((k // 512, 16))
    for p in range(k // 512):
        a[p, :8] = np.random.permutation(np.resize(levels, 8))
        for g in range(8):
            far = levels[np.abs(levels - a[p, g]) >= 10]
            a[p, g + 8] = far[np.random.randint(len(far))]
    return np.exp2(a.ravel()).repeat(32)


def f64(x):
    return np.asarray(x).astype(np.float64)


def striped(idx):
    return np.tile(idx.reshape(-1, 16).T, (8, 1)).astype(np.uint16)


def unstriped(offs):
    return offs[:16].T.reshape(-1).astype(np.int64)


E2M1 = np.array([0.0, 0.5, 1.0, 1.5, 2.0, 3.0, 4.0, 6.0, -0.0, -0.5, -1.0, -1.5, -2.0, -3.0, -4.0, -6.0])


def pack_weight(w, fmt):
    k, n = w.shape
    w = f64(np.asarray(w, np.float32).astype(ml_dtypes.bfloat16)).reshape(k // 32, 32, n)
    amax = np.abs(w).max(1)
    if fmt == "e4m3":
        byte = np.frexp(amax)[1] - 1 + 127 - 7
    else:
        mant, ex = np.frexp(amax / 6.0)
        byte = np.where(mant > 0.5, ex, ex - 1) + 127
    byte = np.clip(np.where(amax > 0, byte, 1), 1, 254)
    scaled = (w * np.exp2(127.0 - byte)[:, None, :]).reshape(k, n).astype(np.float32)
    by_word = np.ascontiguousarray(scaled.reshape(k // 512, 128, 4, n).transpose(0, 1, 3, 2))
    if fmt == "e4m3":
        words = by_word.astype(ml_dtypes.float8_e4m3fn).view(np.uint8)
    else:
        c = by_word.astype(ml_dtypes.float4_e2m1fn).view(np.uint8) & 0xF
        words = (c[..., 0::2] | (c[..., 1::2] << 4)).reshape(k // 512, 128, 2 * n)
    return np.ascontiguousarray(words), np.ascontiguousarray(byte.astype(np.uint8).reshape(k // 512, 16, n))


def unpack_weight(words, scales, fmt):
    g, _, n = scales.shape
    words = np.ascontiguousarray(words).reshape(g, 128, n, -1)
    if fmt == "e4m3":
        vals = words.view(ml_dtypes.float8_e4m3fn).astype(np.float64)
    else:
        nib = np.empty((g, 128, n, 4), np.uint8)
        nib[..., 0::2] = words & 0xF
        nib[..., 1::2] = words >> 4
        vals = E2M1[nib]
    vals = vals * np.repeat(np.exp2(scales.astype(np.float64) - 127.0), 8, axis=1)[..., None]
    return vals.transpose(0, 1, 3, 2).reshape(g * 512, n)


def gelu(v):
    return 0.5 * v * (1.0 + np.tanh(np.sqrt(2.0 / np.pi) * (v + 0.044715 * v**3)))


K, H, N, T, S = 512, 1024, 512, 4096, 1024

def setup_inputs():
    n = np.random.standard_normal
    s = mx_kscale(K)[:, None]
    u = mx_kscale(H)[:, None]
    tab_words, tab_scales = pack_weight(n((K, T)) * s, "e4m3")
    wg_words, wg_scales = pack_weight(n((K, H)) / np.sqrt(K) / s, "e2m1")
    wb_words, wb_scales = pack_weight(n((K, H)) / np.sqrt(K) / s, "e4m3")
    wr_words, wr_scales = pack_weight(n((K, N)) / np.sqrt(K) / s, "e2m1")
    return {
        "tab_words": tab_words, "tab_scales": tab_scales,
        "offs": striped(np.random.permutation(T)[:S]),
        "offs2": striped(np.random.permutation(T)[:S]),
        "offs3": striped(np.random.permutation(T)[:S]),
        "wg_words": wg_words, "wg_scales": wg_scales,
        "wa": (n((K, H)) / np.sqrt(K) / s * u.T).astype(np.float32),
        "wb_words": wb_words, "wb_scales": wb_scales,
        "wr_words": wr_words, "wr_scales": wr_scales,
        "wo": (1.5 * n((H, N)) / np.sqrt(H) / u).astype(np.float32),
        "bo": (0.5 * n(N)).astype(np.float32),
    }

def reference(tab_words, tab_scales, offs, offs2, offs3, wg_words, wg_scales, wa, wb_words, wb_scales,
              wr_words, wr_scales, wo, bo):
    v_ij = unpack_weight(tab_words, tab_scales, "e4m3")[:, unstriped(offs)]
    v_ik = unpack_weight(tab_words, tab_scales, "e4m3")[:, unstriped(offs2)]
    v_jk = unpack_weight(tab_words, tab_scales, "e4m3")[:, unstriped(offs3)]
    wg = unpack_weight(wg_words, wg_scales, "e2m1")
    wb = unpack_weight(wb_words, wb_scales, "e4m3")
    wr = unpack_weight(wr_words, wr_scales, "e2m1")
    gate = 1.0 / (1.0 + np.exp(-(wg.T @ v_ij)))
    a = mxq(f64(wa), 0, "e4m3").T @ v_ik
    b = wb.T @ v_jk
    h = gate * a * b
    y = wr.T @ v_ij + mxq(f64(wo), 0, "e4m3").T @ mxq(h, 0, "e4m3")
    return y + f64(bo)[:, None]

@@ -1,0 +1,279 @@
+from contextlib import ExitStack
+
+import concourse.mybir as mybir
+
+K, H, N, T, S = 512, 1024, 512, 4096, 1024
+FLOPS = 2 * S * (3 * K * H + K * N + H * N)
+
+F32 = mybir.dt.float32
+BF16 = mybir.dt.bfloat16
+I32 = mybir.dt.int32
+U32 = mybir.dt.uint32
+U16 = mybir.dt.uint16
+U8 = mybir.dt.uint8
+FP8X4 = mybir.dt.float8_e4m3fn_x4
+FP4X4 = mybir.dt.float4_e2m1fn_x4
+ACT = mybir.ActivationFunctionType
+ALU = mybir.AluOpType
+
+P = 128
+HALF = 512
+TOK = 128
+
+
+def tile_list_triangle_edge_update_kernel(
+    tc, tab_words, tab_scales, offs, offs2, offs3, wg_words, wg_scales, wa, wb_words, wb_scales,
+    wr_words, wr_scales, wo, bo, out,
+):
+    nc = tc.nc
+    with ExitStack() as ctx:
+        held = ctx.enter_context(tc.tile_pool(name="held", bufs=1))
+        stage = ctx.enter_context(tc.tile_pool(name="stage", bufs=2))
+        work = ctx.enter_context(tc.tile_pool(name="work", bufs=3))
+        psum = ctx.enter_context(tc.psum_pool(name="psum", bufs=2))
+
+        lists = []
+        for i, src in enumerate((offs, offs2, offs3)):
+            lst = held.tile([P, S // 16], U16, name=f"list{i}")
+            nc.sync.dma_start(lst[:], src)
+            lists.append(lst)
+
+        tab_w = held.tile([P, T], I32, name="tab_w", align_bytes=64)
+        tab_s = held.tile([P, T // 4], I32, name="tab_s", align_bytes=64)
+        w_s = held.tile([P, (2 * H + N) // 4], I32, name="w_s", align_bytes=64)
+        warm_in = held.tile([P, 1], F32, name="warm_in")
+        warm_out = held.tile([P, 1], F32, name="warm_out")
+
+        nc.vector.memset(tab_s[:], 0)
+        nc.vector.memset(w_s[:], 0)
+        nc.vector.memset(warm_in[:], 0.0)
+        nc.scalar.activation(warm_out[:], warm_in[:], ACT.Sigmoid)
+
+        def load_scale_rows(queue, dst, src):
+            for q in range(4):
+                queue.dma_start(dst[32 * q : 32 * q + 4, :], src[0, 4 * q : 4 * q + 4, :].bitcast(I32))
+
+        load_scale_rows(nc.sync, tab_s, tab_scales)
+        nc.sync.dma_start(tab_w[:], tab_words[0].rearrange("p t i -> p (t i)").bitcast(I32))
+
+        wg_raw = held.tile([P, H // 2], I32, name="wg_raw")
+        wb_raw = held.tile([P, H], I32, name="wb_raw")
+        wr_w = held.tile([P, 2 * N], U8, name="wr_w", align_bytes=64)
+        bias = held.tile([P, N // P], F32, name="bias")
+        nc.sync.dma_start(wg_raw[:], wg_words[0].bitcast(I32))
+        nc.sync.dma_start(wb_raw[:], wb_words[0].rearrange("p c i -> p (c i)").bitcast(I32))
+        wa_raw = []
+        for b in range(2):
+            raw = stage.tile([P, 4, HALF], F32, name="raw")
+            nc.sync.dma_start(raw[:], wa.rearrange("(p j) c -> p j c", j=4)[:, :, b * HALF : (b + 1) * HALF])
+            wa_raw.append(raw)
+        load_scale_rows(nc.gpsimd, w_s[:, 0 : H // 4], wg_scales)
+        load_scale_rows(nc.gpsimd, w_s[:, H // 4 : H // 2], wb_scales)
+        load_scale_rows(nc.gpsimd, w_s[:, H // 2 :], wr_scales)
+        nc.sync.dma_start(wr_w[:].bitcast(I32), wr_words[0].bitcast(I32))
+        with nc.allow_non_contiguous_dma(reason="one bias value a partition"):
+            nc.sync.dma_start(bias[:], bo.rearrange("(c p) -> p c", p=P))
+        wr_s = w_s[:, H // 2 :].bitcast(U8)
+
+        v_w = {}
+        v_s = {}
+
+        def gather_scales(i, h):
+            v_s[i, h] = held.tile([P, HALF], U8, name=f"v_s{i}{h}", align_bytes=64)
+            nc.vector.tensor_copy(v_s[i, h][:], tab_s[:].bitcast(U8).indirect(lists[i][:, 32 * h : 32 * h + 32]))
+
+        def gather_words(i, h):
+            v_w[i, h] = held.tile([P, HALF], U32, name=f"v_w{i}{h}", align_bytes=64)
+            nc.vector.tensor_copy(v_w[i, h][:], tab_w[:].bitcast(U32).indirect(lists[i][:, 32 * h : 32 * h + 32]))
+
+        for h in range(2):
+            for i in range(3):
+                gather_scales(i, h)
+        for i in (0, 2, 1):
+            gather_words(i, 0)
+
+        wg_w = held.tile([P, 2 * H], U8, name="wg_w", align_bytes=64)
+        wb_w = held.tile([P, H], U32, name="wb_w", align_bytes=64)
+        gb_s = held.tile([P, 2 * H], U8, name="gb_s", align_bytes=64)
+        nc.vector.tensor_copy(
+            gb_s[:].bitcast(I32).rearrange("p (c t q) -> p c q t", c=4, t=4),
+            w_s[:, 0 : H // 2].rearrange("p (c q t) -> p c q t", c=4, t=4),
+        )
+
+        def permute_words(b):
+            nc.vector.tensor_copy(
+                wg_w[:, b * 2 * HALF : (b + 1) * 2 * HALF].bitcast(I32).rearrange("p (t q i) -> p t q i", t=4, i=2),
+                wg_raw[:, b * HALF // 2 : (b + 1) * HALF // 2].rearrange("p (q t i) -> p t q i", t=4, i=2),
+            )
+            nc.vector.tensor_copy(
+                wb_w[:, b * HALF : (b + 1) * HALF].bitcast(I32).rearrange("p (t q i) -> p t q i", t=4, i=4),
+                wb_raw[:, b * HALF : (b + 1) * HALF].rearrange("p (q t i) -> p t q i", t=4, i=4),
+            )
+
+        wa_w = held.tile([P, H], U32, name="wa_w", align_bytes=64)
+        wa_s = held.tile([P, H], U8, name="wa_s", align_bytes=64)
+        wo_w = held.tile([P, 2 * N], U32, name="wo_w", align_bytes=64)
+        wo_s = held.tile([P, 2 * N], U8, name="wo_s", align_bytes=64)
+        w_bf = {}
+
+        def round_wa(b):
+            w_bf["a", b] = held.tile([P, 4, TOK, 4], BF16, name=f"wa_bf{b}", align_bytes=64)
+            for t in range(4):
+                nc.scalar.copy(
+                    w_bf["a", b][:, t].rearrange("p (q i) j -> p q j i", i=4),
+                    wa_raw[b][:].rearrange("p j (q t i) -> p t q j i", t=4, i=4)[:, t],
+                )
+
+        def quantize_wa(b, part):
+            cols = slice(b * HALF + part * 256, b * HALF + (part + 1) * 256)
+            nc.vector.quantize_mx(
+                out=wa_w[:, cols].bitcast(FP8X4),
+                scales=wa_s[:, cols],
+                in_=w_bf["a", b][:, 2 * part : 2 * part + 2].rearrange("p t m j -> p (t m j)"),
+            )
+
+        wo_raw = {}
+
+        def load_wo(b):
+            wo_raw[b] = stage.tile([P, 4, HALF], F32, name="raw")
+            rows = wo.rearrange("(b g t e) n -> b e g t n", b=2, t=4, e=4)
+            for e in range(4):
+                (nc.sync if e % 2 == 0 else nc.scalar).dma_start(wo_raw[b][e:P:4, :, :], rows[b, e])
+
+        def round_wo(b, c):
+            if c == 0:
+                w_bf["o", b] = held.tile([P, N, 4], BF16, name=f"wo_bf{b}", align_bytes=64)
+            cols = slice(c * P, (c + 1) * P)
+            nc.scalar.copy(
+                w_bf["o", b][:, cols, :].rearrange("p (c i) t -> p c t i", i=4),
+                wo_raw[b][:, :, cols].rearrange("p t (c i) -> p c t i", i=4),
+            )
+
+        def quantize_wo(b):
+            cols = slice(b * N, (b + 1) * N)
+            nc.vector.quantize_mx(
+                out=wo_w[:, cols].bitcast(FP8X4),
+                scales=wo_s[:, cols],
+                in_=w_bf["o", b][:].rearrange("p n t -> p (n t)"),
+            )
+
+        permute_words(0)
+        round_wa(0)
+        quantize_wa(0, 0)
+        quantize_wa(0, 1)
+        load_wo(0)
+        permute_words(1)
+        round_wa(1)
+        load_wo(1)
+
+        units = [(h, b, k) for h in range(2) for b in range(2) for k in range(HALF // TOK)]
+        h_bf = {}
+        h_w = {}
+        h_s = {}
+        ga = {}
+        b_bank = {}
+
+        def first_products(u):
+            h, b, k = units[u]
+            tok = slice(k * TOK, (k + 1) * TOK)
+            banks = []
+            for name, i in (("g_bank", 0), ("a_bank", 1), ("b_bank", 2)):
+                bank = psum.tile([P, 4, TOK], F32, name=name)
+                for t in range(4):
+                    c0 = b * HALF + t * P
+                    if i == 0:
+                        lhsT, lhsT_s = wg_w[:, 2 * c0 : 2 * c0 + 2 * P].bitcast(FP4X4), gb_s[:, c0 : c0 + P]
+                    elif i == 1:
+                        lhsT, lhsT_s = wa_w[:, c0 : c0 + P].bitcast(FP8X4), wa_s[:, c0 : c0 + P]
+                    else:
+                        lhsT, lhsT_s = wb_w[:, c0 : c0 + P].bitcast(FP8X4), gb_s[:, H + c0 : H + c0 + P]
+                    nc.tensor.matmul_mx(
+                        out=bank[:, t, :], lhsT=lhsT, lhsT_scale=lhsT_s,
+                        rhs=v_w[i, h][:, tok].bitcast(FP8X4), rhs_scale=v_s[i, h][:, tok],
+                        start=True, stop=True,
+                    )
+                banks.append(bank)
+            gate = work.tile([P, TOK, 4], F32, name="gate")
+            nc.scalar.activation(gate[:], banks[0][:].rearrange("p t n -> p n t"), ACT.Sigmoid)
+            ga[u] = work.tile([P, TOK, 4], F32, name="ga")
+            nc.vector.tensor_tensor(ga[u][:], banks[1][:].rearrange("p t n -> p n t"), gate[:], ALU.mult)
+            b_bank[u] = banks[2]
+
+        def message(u):
+            h, b, k = units[u]
+            if k == 0:
+                h_bf[h, b] = held.tile([P, HALF, 4], BF16, name=f"h_bf{h}{b}", align_bytes=64)
+                h_w[h, b] = held.tile([P, HALF], U32, name=f"h_w{h}{b}", align_bytes=64)
+                h_s[h, b] = held.tile([P, HALF], U8, name=f"h_s{h}{b}", align_bytes=64)
+            nc.vector.tensor_tensor(
+                h_bf[h, b][:, k * TOK : (k + 1) * TOK, :], b_bank[u][:].rearrange("p t n -> p n t"), ga[u][:], ALU.mult
+            )
+
+        def quantize_h(h, b, lo, hi):
+            nc.vector.quantize_mx(
+                out=h_w[h, b][:, lo:hi].bitcast(FP8X4),
+                scales=h_s[h, b][:, lo:hi],
+                in_=h_bf[h, b][:, lo:hi, :].rearrange("p n t -> p (n t)"),
+            )
+
+        y_bank = {}
+
+        def y_pass(h, c, step, tag):
+            if step == 0:
+                y_bank[h, c] = psum.tile([P, HALF], F32, name=tag)
+                nc.tensor.matmul_mx(
+                    out=y_bank[h, c][:], lhsT=wr_w[:, 2 * c * P : 2 * (c + 1) * P].bitcast(FP4X4),
+                    lhsT_scale=wr_s[:, c * P : (c + 1) * P],
+                    rhs=v_w[0, h][:].bitcast(FP8X4), rhs_scale=v_s[0, h][:], start=True, stop=False,
+                )
+            else:
+                b = step - 1
+                cols = slice(b * N + c * P, b * N + (c + 1) * P)
+                nc.tensor.matmul_mx(
+                    out=y_bank[h, c][:], lhsT=wo_w[:, cols].bitcast(FP8X4), lhsT_scale=wo_s[:, cols],
+                    rhs=h_w[h, b][:].bitcast(FP8X4), rhs_scale=h_s[h, b][:], start=False, stop=(b == 1),
+                )
+
+        def y_out(h, c, on_vector):
+            y = work.tile([P, HALF], F32, name="y", bufs=4)
+            if on_vector:
+                nc.vector.tensor_scalar(y[:], y_bank[h, c][:], bias[:, c : c + 1], None, ALU.add)
+            else:
+                nc.scalar.activation(y[:], y_bank[h, c][:], ACT.Identity, bias=bias[:, c : c + 1])
+            nc.sync.dma_start(out[c * P : (c + 1) * P, h * HALF : (h + 1) * HALF], y[:])
+
+        def y_whole(c):
+            for step in range(3):
+                y_pass(0, c, step, "y_bank")
+            y_out(0, c, False)
+
+        extra = {
+            1: [lambda: gather_words(0, 1), lambda: quantize_wa(1, 0)],
+            2: [lambda: quantize_wa(1, 1)],
+            3: [lambda: gather_words(2, 1), lambda: round_wo(0, 0), lambda: round_wo(0, 1)],
+            4: [lambda: round_wo(0, 2), lambda: round_wo(0, 3)],
+            5: [lambda: quantize_h(0, 0, 0, HALF), lambda: gather_words(1, 1), lambda: round_wo(1, 0), lambda: round_wo(1, 1)],
+            6: [lambda: quantize_wo(0), lambda: round_wo(1, 2), lambda: round_wo(1, 3)],
+            8: [lambda: quantize_wo(1)],
+            9: [lambda: quantize_h(0, 1, 0, HALF)],
+            10: [lambda: y_whole(0)],
+            11: [lambda: y_whole(1)],
+            12: [lambda: y_whole(2)],
+            13: [lambda: quantize_h(1, 0, 0, HALF), lambda: y_whole(3)],
+            15: [lambda: quantize_h(1, 1, 0, 256)],
+        }
+        for u in range(len(units)):
+            first_products(u)
+            for step in extra.get(u, []):
+                step()
+            if u > 0:
+                message(u - 1)
+        for c in range(4):
+            for step in range(2):
+                y_pass(1, c, step, "y_bank" if c < 2 else "g_bank")
+        quantize_h(1, 1, 256, 384)
+        message(len(units) - 1)
+        quantize_h(1, 1, 384, 512)
+        for c in range(4):
+            y_pass(1, c, 2, None)
+            y_out(1, c, c % 2 == 1)

@@ -54,7 +54,6 @@ def tile_list_triangle_edge_update_kernel(
                 queue.dma_start(dst[32 * q : 32 * q + 4, :], src[0, 4 * q : 4 * q + 4, :].bitcast(I32))
 
         load_scale_rows(nc.sync, tab_s, tab_scales)
-        nc.sync.dma_start(tab_w[:], tab_words[0].rearrange("p t i -> p (t i)").bitcast(I32))
 
         wg_raw = held.tile([P, H // 2], I32, name="wg_raw")
         wb_raw = held.tile([P, H], I32, name="wb_raw")
@@ -67,6 +66,8 @@ def tile_list_triangle_edge_update_kernel(
             raw = stage.tile([P, 4, HALF], F32, name="raw")
             nc.sync.dma_start(raw[:], wa.rearrange("(p j) c -> p j c", j=4)[:, :, b * HALF : (b + 1) * HALF])
             wa_raw.append(raw)
+            if b == 0:
+                nc.sync.dma_start(tab_w[:], tab_words[0].rearrange("p t i -> p (t i)").bitcast(I32))
         load_scale_rows(nc.gpsimd, w_s[:, 0 : H // 4], wg_scales)
         load_scale_rows(nc.gpsimd, w_s[:, H // 4 : H // 2], wb_scales)
         load_scale_rows(nc.gpsimd, w_s[:, H // 2 :], wr_scales)
@@ -89,8 +90,6 @@ def tile_list_triangle_edge_update_kernel(
         for h in range(2):
             for i in range(3):
                 gather_scales(i, h)
-        for i in (0, 2, 1):
-            gather_words(i, 0)
 
         wg_w = held.tile([P, 2 * H], U8, name="wg_w", align_bytes=64)
         wb_w = held.tile([P, H], U32, name="wb_w", align_bytes=64)
@@ -138,7 +137,7 @@ def tile_list_triangle_edge_update_kernel(
             wo_raw[b] = stage.tile([P, 4, HALF], F32, name="raw")
             rows = wo.rearrange("(b g t e) n -> b e g t n", b=2, t=4, e=4)
             for e in range(4):
-                (nc.sync if e % 2 == 0 else nc.scalar).dma_start(wo_raw[b][e:P:4, :, :], rows[b, e])
+                (nc.sync if e < 2 else nc.gpsimd).dma_start(wo_raw[b][e:P:4, :, :], rows[b, e])
 
         def round_wo(b, c):
             if c == 0:
@@ -163,6 +162,8 @@ def tile_list_triangle_edge_update_kernel(
         quantize_wa(0, 1)
         load_wo(0)
         permute_words(1)
+        for i in (0, 2, 1):
+            gather_words(i, 0)
         round_wa(1)
         load_wo(1)
 
@@ -216,36 +217,49 @@ def tile_list_triangle_edge_update_kernel(
                 in_=h_bf[h, b][:, lo:hi, :].rearrange("p n t -> p (n t)"),
             )
 
-        y_bank = {}
-
-        def y_pass(h, c, step, tag):
+        def y_pass(dst, h, tok, c, step):
             if step == 0:
-                y_bank[h, c] = psum.tile([P, HALF], F32, name=tag)
                 nc.tensor.matmul_mx(
-                    out=y_bank[h, c][:], lhsT=wr_w[:, 2 * c * P : 2 * (c + 1) * P].bitcast(FP4X4),
+                    out=dst, lhsT=wr_w[:, 2 * c * P : 2 * (c + 1) * P].bitcast(FP4X4),
                     lhsT_scale=wr_s[:, c * P : (c + 1) * P],
-                    rhs=v_w[0, h][:].bitcast(FP8X4), rhs_scale=v_s[0, h][:], start=True, stop=False,
+                    rhs=v_w[0, h][:, tok].bitcast(FP8X4), rhs_scale=v_s[0, h][:, tok], start=True, stop=False,
                 )
             else:
                 b = step - 1
                 cols = slice(b * N + c * P, b * N + (c + 1) * P)
                 nc.tensor.matmul_mx(
-                    out=y_bank[h, c][:], lhsT=wo_w[:, cols].bitcast(FP8X4), lhsT_scale=wo_s[:, cols],
-                    rhs=h_w[h, b][:].bitcast(FP8X4), rhs_scale=h_s[h, b][:], start=False, stop=(b == 1),
+                    out=dst, lhsT=wo_w[:, cols].bitcast(FP8X4), lhsT_scale=wo_s[:, cols],
+                    rhs=h_w[h, b][:, tok].bitcast(FP8X4), rhs_scale=h_s[h, b][:, tok], start=False, stop=(b == 1),
                 )
 
-        def y_out(h, c, on_vector):
-            y = work.tile([P, HALF], F32, name="y", bufs=4)
+        def add_bias(dst, src, c, on_vector):
             if on_vector:
-                nc.vector.tensor_scalar(y[:], y_bank[h, c][:], bias[:, c : c + 1], None, ALU.add)
+                nc.vector.tensor_scalar(dst, src, bias[:, c : c + 1], None, ALU.add)
             else:
-                nc.scalar.activation(y[:], y_bank[h, c][:], ACT.Identity, bias=bias[:, c : c + 1])
-            nc.sync.dma_start(out[c * P : (c + 1) * P, h * HALF : (h + 1) * HALF], y[:])
+                nc.scalar.activation(dst, src, ACT.Identity, bias=bias[:, c : c + 1])
 
-        def y_whole(c):
+        def y_wide(c):
+            bank = psum.tile([P, HALF], F32, name="y_bank")
             for step in range(3):
-                y_pass(0, c, step, "y_bank")
-            y_out(0, c, False)
+                y_pass(bank[:], 0, slice(0, HALF), c, step)
+            y = work.tile([P, HALF], F32, name="y")
+            add_bias(y[:], bank[:], c, False)
+            nc.sync.dma_start(out[c * P : (c + 1) * P, 0:HALF], y[:])
+
+        def store_narrow(k, y):
+            dst = out.rearrange("(c p) s -> p c s", p=P)[:, :, HALF + k * TOK : HALF + (k + 1) * TOK]
+            nc.sync.dma_start(dst, y[:])
+
+        def y_narrow(k):
+            tok = slice(k * TOK, (k + 1) * TOK)
+            bank = psum.tile([P, 4, TOK], F32, name="y_bank")
+            for c in range(4):
+                for step in range(3):
+                    y_pass(bank[:, c, :], 1, tok, c, step)
+            y = work.tile([P, 4, TOK], F32, name="y")
+            for c in range(4):
+                add_bias(y[:, c, :], bank[:, c, :], c, False)
+            store_narrow(k, y)
 
         extra = {
             1: [lambda: gather_words(0, 1), lambda: quantize_wa(1, 0)],
@@ -256,11 +270,12 @@ def tile_list_triangle_edge_update_kernel(
             6: [lambda: quantize_wo(0), lambda: round_wo(1, 2), lambda: round_wo(1, 3)],
             8: [lambda: quantize_wo(1)],
             9: [lambda: quantize_h(0, 1, 0, HALF)],
-            10: [lambda: y_whole(0)],
-            11: [lambda: y_whole(1)],
-            12: [lambda: y_whole(2)],
-            13: [lambda: quantize_h(1, 0, 0, HALF), lambda: y_whole(3)],
-            15: [lambda: quantize_h(1, 1, 0, 256)],
+            10: [lambda: y_wide(0)],
+            11: [lambda: y_wide(1)],
+            12: [lambda: y_wide(2)],
+            13: [lambda: quantize_h(1, 0, 0, HALF), lambda: y_wide(3)],
+            14: [lambda: quantize_h(1, 1, 0, TOK)],
+            15: [lambda: y_narrow(0), lambda: quantize_h(1, 1, TOK, 2 * TOK)],
         }
         for u in range(len(units)):
             first_products(u)
@@ -268,12 +283,20 @@ def tile_list_triangle_edge_update_kernel(
                 step()
             if u > 0:
                 message(u - 1)
-        for c in range(4):
-            for step in range(2):
-                y_pass(1, c, step, "y_bank" if c < 2 else "g_bank")
-        quantize_h(1, 1, 256, 384)
         message(len(units) - 1)
-        quantize_h(1, 1, 384, 512)
+        y_narrow(1)
+        quantize_h(1, 1, 2 * TOK, 3 * TOK)
+        last = slice(3 * TOK, HALF)
+        banks = []
         for c in range(4):
-            y_pass(1, c, 2, None)
-            y_out(1, c, c % 2 == 1)
+            bank = psum.tile([P, TOK], F32, name="g_bank" if c < 2 else "a_bank")
+            for step in range(2):
+                y_pass(bank[:], 1, last, c, step)
+            banks.append(bank)
+        y_narrow(2)
+        quantize_h(1, 1, 3 * TOK, HALF)
+        y = work.tile([P, 4, TOK], F32, name="y")
+        for c in range(4):
+            y_pass(banks[c][:], 1, last, c, 2)
+            add_bias(y[:, c, :], banks[c][:], c, c % 2 == 1)
+        store_narrow(3, y)

@@ -45,15 +45,15 @@ def tile_list_triangle_edge_update_kernel(
         warm_out = held.tile([P, 1], F32, name="warm_out")
 
         nc.vector.memset(tab_s[:], 0)
-        nc.vector.memset(w_s[:], 0)
         nc.vector.memset(warm_in[:], 0.0)
-        nc.scalar.activation(warm_out[:], warm_in[:], ACT.Sigmoid)
+        nc.vector.memset(w_s[:], 0)
 
-        def load_scale_rows(queue, dst, src):
+        def load_scale_rows(queues, dst, src):
             for q in range(4):
-                queue.dma_start(dst[32 * q : 32 * q + 4, :], src[0, 4 * q : 4 * q + 4, :].bitcast(I32))
+                queues[q // 2].dma_start(dst[32 * q : 32 * q + 4, :], src[0, 4 * q : 4 * q + 4, :].bitcast(I32))
 
-        load_scale_rows(nc.sync, tab_s, tab_scales)
+        load_scale_rows((nc.sync, nc.scalar), tab_s, tab_scales)
+        nc.scalar.activation(warm_out[:], warm_in[:], ACT.Sigmoid)
 
         wg_raw = held.tile([P, H // 2], I32, name="wg_raw")
         wb_raw = held.tile([P, H], I32, name="wb_raw")
@@ -68,9 +68,8 @@ def tile_list_triangle_edge_update_kernel(
             wa_raw.append(raw)
             if b == 0:
                 nc.sync.dma_start(tab_w[:], tab_words[0].rearrange("p t i -> p (t i)").bitcast(I32))
-        load_scale_rows(nc.gpsimd, w_s[:, 0 : H // 4], wg_scales)
-        load_scale_rows(nc.gpsimd, w_s[:, H // 4 : H // 2], wb_scales)
-        load_scale_rows(nc.gpsimd, w_s[:, H // 2 :], wr_scales)
+        load_scale_rows((nc.scalar, nc.scalar), w_s[:, 0 : H // 4], wg_scales)
+        load_scale_rows((nc.scalar, nc.scalar), w_s[:, H // 4 : H // 2], wb_scales)
         nc.sync.dma_start(wr_w[:].bitcast(I32), wr_words[0].bitcast(I32))
         with nc.allow_non_contiguous_dma(reason="one bias value a partition"):
             nc.sync.dma_start(bias[:], bo.rearrange("(c p) -> p c", p=P))
@@ -79,34 +78,35 @@ def tile_list_triangle_edge_update_kernel(
         v_w = {}
         v_s = {}
 
-        def gather_scales(i, h):
-            v_s[i, h] = held.tile([P, HALF], U8, name=f"v_s{i}{h}", align_bytes=64)
-            nc.vector.tensor_copy(v_s[i, h][:], tab_s[:].bitcast(U8).indirect(lists[i][:, 32 * h : 32 * h + 32]))
+        def gather_scales(i):
+            both = held.tile([P, S], U8, name=f"v_s{i}", align_bytes=64)
+            nc.vector.tensor_copy(both[:], tab_s[:].bitcast(U8).indirect(lists[i][:]))
+            for h in range(2):
+                v_s[i, h] = both[:, h * HALF : (h + 1) * HALF]
 
         def gather_words(i, h):
             v_w[i, h] = held.tile([P, HALF], U32, name=f"v_w{i}{h}", align_bytes=64)
             nc.vector.tensor_copy(v_w[i, h][:], tab_w[:].bitcast(U32).indirect(lists[i][:, 32 * h : 32 * h + 32]))
 
-        for h in range(2):
-            for i in range(3):
-                gather_scales(i, h)
+        for i in range(3):
+            gather_scales(i)
 
         wg_w = held.tile([P, 2 * H], U8, name="wg_w", align_bytes=64)
         wb_w = held.tile([P, H], U32, name="wb_w", align_bytes=64)
         gb_s = held.tile([P, 2 * H], U8, name="gb_s", align_bytes=64)
         nc.vector.tensor_copy(
-            gb_s[:].bitcast(I32).rearrange("p (c t q) -> p c q t", c=4, t=4),
-            w_s[:, 0 : H // 2].rearrange("p (c q t) -> p c q t", c=4, t=4),
+            gb_s[:].bitcast(U16).rearrange("p (c t g) -> p c t g", c=4, t=4),
+            w_s[:, 0 : H // 2].bitcast(U16).rearrange("p (c g t) -> p c t g", c=4, t=4),
         )
 
         def permute_words(b):
             nc.vector.tensor_copy(
-                wg_w[:, b * 2 * HALF : (b + 1) * 2 * HALF].bitcast(I32).rearrange("p (t q i) -> p t q i", t=4, i=2),
-                wg_raw[:, b * HALF // 2 : (b + 1) * HALF // 2].rearrange("p (q t i) -> p t q i", t=4, i=2),
+                wg_w[:, b * 2 * HALF : (b + 1) * 2 * HALF].bitcast(I32).rearrange("p (t g) -> p t g", t=4),
+                wg_raw[:, b * HALF // 2 : (b + 1) * HALF // 2].rearrange("p (g t) -> p t g", t=4),
             )
             nc.vector.tensor_copy(
-                wb_w[:, b * HALF : (b + 1) * HALF].bitcast(I32).rearrange("p (t q i) -> p t q i", t=4, i=4),
-                wb_raw[:, b * HALF : (b + 1) * HALF].rearrange("p (q t i) -> p t q i", t=4, i=4),
+                wb_w[:, b * HALF : (b + 1) * HALF].bitcast(I32).rearrange("p (t g i) -> p t g i", t=4, i=2),
+                wb_raw[:, b * HALF : (b + 1) * HALF].rearrange("p (g t i) -> p t g i", t=4, i=2),
             )
 
         wa_w = held.tile([P, H], U32, name="wa_w", align_bytes=64)
@@ -119,25 +119,25 @@ def tile_list_triangle_edge_update_kernel(
             w_bf["a", b] = held.tile([P, 4, TOK, 4], BF16, name=f"wa_bf{b}", align_bytes=64)
             for t in range(4):
                 nc.scalar.copy(
-                    w_bf["a", b][:, t].rearrange("p (q i) j -> p q j i", i=4),
-                    wa_raw[b][:].rearrange("p j (q t i) -> p t q j i", t=4, i=4)[:, t],
+                    w_bf["a", b][:, t].rearrange("p (g i) j -> p g j i", i=2),
+                    wa_raw[b][:].rearrange("p j (g t i) -> p t g j i", t=4, i=2)[:, t],
                 )
 
-        def quantize_wa(b, part):
-            cols = slice(b * HALF + part * 256, b * HALF + (part + 1) * 256)
+        def quantize_wa(b):
+            cols = slice(b * HALF, (b + 1) * HALF)
             nc.vector.quantize_mx(
                 out=wa_w[:, cols].bitcast(FP8X4),
                 scales=wa_s[:, cols],
-                in_=w_bf["a", b][:, 2 * part : 2 * part + 2].rearrange("p t m j -> p (t m j)"),
+                in_=w_bf["a", b][:].rearrange("p t m j -> p (t m j)"),
             )
 
         wo_raw = {}
 
-        def load_wo(b):
-            wo_raw[b] = stage.tile([P, 4, HALF], F32, name="raw")
-            rows = wo.rearrange("(b g t e) n -> b e g t n", b=2, t=4, e=4)
-            for e in range(4):
-                (nc.sync if e < 2 else nc.gpsimd).dma_start(wo_raw[b][e:P:4, :, :], rows[b, e])
+        def load_wo(b, e):
+            if e == 0:
+                wo_raw[b] = stage.tile([P, 4, HALF], F32, name="raw")
+            rows = wo.rearrange("(b g t e) n -> b e g t n", b=2, t=4, e=2)
+            (nc.scalar if (b, e) == (1, 1) else nc.sync).dma_start(wo_raw[b][e:P:2, :, :], rows[b, e])
 
         def round_wo(b, c):
             if c == 0:
@@ -158,16 +158,17 @@ def tile_list_triangle_edge_update_kernel(
 
         permute_words(0)
         round_wa(0)
-        quantize_wa(0, 0)
-        quantize_wa(0, 1)
-        load_wo(0)
+        quantize_wa(0)
+        load_scale_rows((nc.scalar, nc.scalar), w_s[:, H // 2 :], wr_scales)
+        for e in range(2):
+            load_wo(0, e)
         permute_words(1)
         for i in (0, 2, 1):
             gather_words(i, 0)
         round_wa(1)
-        load_wo(1)
 
-        units = [(h, b, k) for h in range(2) for b in range(2) for k in range(HALF // TOK)]
+        units = [(0, b, k) for b in range(2) for k in range(HALF // TOK)]
+        units += [(1, b, k) for k in range(HALF // TOK) for b in range(2)]
         h_bf = {}
         h_w = {}
         h_s = {}
@@ -217,6 +218,10 @@ def tile_list_triangle_edge_update_kernel(
                 in_=h_bf[h, b][:, lo:hi, :].rearrange("p n t -> p (n t)"),
             )
 
+        def quantize_unit(u):
+            h, b, k = units[u]
+            quantize_h(h, b, k * TOK, (k + 1) * TOK)
+
         def y_pass(dst, h, tok, c, step):
             if step == 0:
                 nc.tensor.matmul_mx(
@@ -238,13 +243,17 @@ def tile_list_triangle_edge_update_kernel(
             else:
                 nc.scalar.activation(dst, src, ACT.Identity, bias=bias[:, c : c + 1])
 
-        def y_wide(c):
-            bank = psum.tile([P, HALF], F32, name="y_bank")
-            for step in range(3):
-                y_pass(bank[:], 0, slice(0, HALF), c, step)
-            y = work.tile([P, HALF], F32, name="y")
-            add_bias(y[:], bank[:], c, False)
-            nc.sync.dma_start(out[c * P : (c + 1) * P, 0:HALF], y[:])
+        wide_bank = {}
+
+        def y_wide(c, steps):
+            for step in steps:
+                if step == 0:
+                    wide_bank[c] = psum.tile([P, HALF], F32, name="y_bank")
+                y_pass(wide_bank[c][:], 0, slice(0, HALF), c, step)
+            if steps[-1] == 2:
+                y = work.tile([P, HALF], F32, name="y", bufs=8)
+                add_bias(y[:], wide_bank[c][:], c, False)
+                nc.sync.dma_start(out[c * P : (c + 1) * P, 0:HALF], y[:])
 
         def store_narrow(k, y):
             dst = out.rearrange("(c p) s -> p c s", p=P)[:, :, HALF + k * TOK : HALF + (k + 1) * TOK]
@@ -256,26 +265,27 @@ def tile_list_triangle_edge_update_kernel(
             for c in range(4):
                 for step in range(3):
                     y_pass(bank[:, c, :], 1, tok, c, step)
-            y = work.tile([P, 4, TOK], F32, name="y")
+            y = work.tile([P, 4, TOK], F32, name="y", bufs=8)
             for c in range(4):
                 add_bias(y[:, c, :], bank[:, c, :], c, False)
             store_narrow(k, y)
 
         extra = {
-            1: [lambda: gather_words(0, 1), lambda: quantize_wa(1, 0)],
-            2: [lambda: quantize_wa(1, 1)],
+            0: [lambda: load_wo(1, 0), lambda: load_wo(1, 1)],
+            1: [lambda: gather_words(0, 1), lambda: quantize_wa(1)],
             3: [lambda: gather_words(2, 1), lambda: round_wo(0, 0), lambda: round_wo(0, 1)],
             4: [lambda: round_wo(0, 2), lambda: round_wo(0, 3)],
             5: [lambda: quantize_h(0, 0, 0, HALF), lambda: gather_words(1, 1), lambda: round_wo(1, 0), lambda: round_wo(1, 1)],
             6: [lambda: quantize_wo(0), lambda: round_wo(1, 2), lambda: round_wo(1, 3)],
+            7: [lambda: y_wide(0, [0, 1]), lambda: y_wide(1, [0, 1])],
             8: [lambda: quantize_wo(1)],
-            9: [lambda: quantize_h(0, 1, 0, HALF)],
-            10: [lambda: y_wide(0)],
-            11: [lambda: y_wide(1)],
-            12: [lambda: y_wide(2)],
-            13: [lambda: quantize_h(1, 0, 0, HALF), lambda: y_wide(3)],
-            14: [lambda: quantize_h(1, 1, 0, TOK)],
-            15: [lambda: y_narrow(0), lambda: quantize_h(1, 1, TOK, 2 * TOK)],
+            9: [lambda: quantize_h(0, 1, 0, HALF), lambda: y_wide(0, [2]), lambda: y_wide(1, [2])],
+            10: [lambda: quantize_unit(8), lambda: y_wide(2, [0, 1, 2])],
+            11: [lambda: quantize_unit(9), lambda: y_wide(3, [0, 1, 2])],
+            12: [lambda: quantize_unit(10), lambda: y_narrow(0)],
+            13: [lambda: quantize_unit(11), lambda: y_narrow(1)],
+            14: [lambda: quantize_unit(12)],
+            15: [lambda: quantize_unit(13), lambda: y_narrow(2)],
         }
         for u in range(len(units)):
             first_products(u)
@@ -284,19 +294,18 @@ def tile_list_triangle_edge_update_kernel(
             if u > 0:
                 message(u - 1)
         message(len(units) - 1)
-        y_narrow(1)
-        quantize_h(1, 1, 2 * TOK, 3 * TOK)
         last = slice(3 * TOK, HALF)
         banks = []
         for c in range(4):
             bank = psum.tile([P, TOK], F32, name="g_bank" if c < 2 else "a_bank")
-            for step in range(2):
-                y_pass(bank[:], 1, last, c, step)
+            y_pass(bank[:], 1, last, c, 0)
             banks.append(bank)
-        y_narrow(2)
-        quantize_h(1, 1, 3 * TOK, HALF)
-        y = work.tile([P, 4, TOK], F32, name="y")
+        for b in range(2):
+            quantize_unit(14 + b)
+        for c in range(4):
+            y_pass(banks[c][:], 1, last, c, 1)
+        y = work.tile([P, 4, TOK], F32, name="y", bufs=8)
         for c in range(4):
             y_pass(banks[c][:], 1, last, c, 2)
-            add_bias(y[:, c, :], banks[c][:], c, c % 2 == 1)
+            add_bias(y[:, c, :], banks[c][:], c, c < 3)
         store_narrow(3, y)

@@ -29,7 +29,7 @@ def tile_list_triangle_edge_update_kernel(
     with ExitStack() as ctx:
         held = ctx.enter_context(tc.tile_pool(name="held", bufs=1))
         stage = ctx.enter_context(tc.tile_pool(name="stage", bufs=2))
-        work = ctx.enter_context(tc.tile_pool(name="work", bufs=3))
+        work = ctx.enter_context(tc.tile_pool(name="work", bufs=4))
         psum = ctx.enter_context(tc.psum_pool(name="psum", bufs=2))
 
         lists = []
@@ -116,7 +116,7 @@ def tile_list_triangle_edge_update_kernel(
         w_bf = {}
 
         def round_wa(b):
-            w_bf["a", b] = held.tile([P, 4, TOK, 4], BF16, name=f"wa_bf{b}", align_bytes=64)
+            w_bf["a", b] = held.tile([P, 4, TOK, 4], BF16, name="w_bf", align_bytes=64)
             for t in range(4):
                 nc.scalar.copy(
                     w_bf["a", b][:, t].rearrange("p (g i) j -> p g j i", i=2),
@@ -139,14 +139,14 @@ def tile_list_triangle_edge_update_kernel(
             rows = wo.rearrange("(b g t e) n -> b e g t n", b=2, t=4, e=2)
             (nc.scalar if (b, e) == (1, 1) else nc.sync).dma_start(wo_raw[b][e:P:2, :, :], rows[b, e])
 
-        def round_wo(b, c):
-            if c == 0:
-                w_bf["o", b] = held.tile([P, N, 4], BF16, name=f"wo_bf{b}", align_bytes=64)
-            cols = slice(c * P, (c + 1) * P)
-            nc.scalar.copy(
-                w_bf["o", b][:, cols, :].rearrange("p (c i) t -> p c t i", i=4),
-                wo_raw[b][:, :, cols].rearrange("p t (c i) -> p c t i", i=4),
-            )
+        def round_wo(b):
+            w_bf["o", b] = held.tile([P, N, 4], BF16, name="w_bf", align_bytes=64)
+            for c in range(4):
+                cols = slice(c * P, (c + 1) * P)
+                nc.gpsimd.tensor_scalar(
+                    w_bf["o", b][:, cols, :], wo_raw[b][:, :, cols].rearrange("p t n -> p n t"),
+                    1.0, 0.0, ALU.mult, ALU.add,
+                )
 
         def quantize_wo(b):
             cols = slice(b * N, (b + 1) * N)
@@ -272,11 +272,10 @@ def tile_list_triangle_edge_update_kernel(
 
         extra = {
             0: [lambda: load_wo(1, 0), lambda: load_wo(1, 1)],
-            1: [lambda: gather_words(0, 1), lambda: quantize_wa(1)],
-            3: [lambda: gather_words(2, 1), lambda: round_wo(0, 0), lambda: round_wo(0, 1)],
-            4: [lambda: round_wo(0, 2), lambda: round_wo(0, 3)],
-            5: [lambda: quantize_h(0, 0, 0, HALF), lambda: gather_words(1, 1), lambda: round_wo(1, 0), lambda: round_wo(1, 1)],
-            6: [lambda: quantize_wo(0), lambda: round_wo(1, 2), lambda: round_wo(1, 3)],
+            1: [lambda: gather_words(0, 1), lambda: quantize_wa(1), lambda: round_wo(0)],
+            3: [lambda: gather_words(2, 1)],
+            4: [lambda: gather_words(1, 1), lambda: quantize_wo(0), lambda: round_wo(1)],
+            5: [lambda: quantize_h(0, 0, 0, HALF)],
             7: [lambda: y_wide(0, [0, 1]), lambda: y_wide(1, [0, 1])],
             8: [lambda: quantize_wo(1)],
             9: [lambda: quantize_h(0, 1, 0, HALF), lambda: y_wide(0, [2]), lambda: y_wide(1, [2])],
@@ -304,8 +303,10 @@ def tile_list_triangle_edge_update_kernel(
             quantize_unit(14 + b)
         for c in range(4):
             y_pass(banks[c][:], 1, last, c, 1)
-        y = work.tile([P, 4, TOK], F32, name="y", bufs=8)
-        for c in range(4):
-            y_pass(banks[c][:], 1, last, c, 2)
-            add_bias(y[:, c, :], banks[c][:], c, c < 3)
-        store_narrow(3, y)
+        for c0 in (0, 2):
+            y = work.tile([P, 2, TOK], F32, name="y", bufs=8)
+            for c in (c0, c0 + 1):
+                y_pass(banks[c][:], 1, last, c, 2)
+                add_bias(y[:, c - c0, :], banks[c][:], c, c < 3)
+            dst = out.rearrange("(c p) s -> p c s", p=P)[:, c0 : c0 + 2, S - TOK :]
+            nc.sync.dma_start(dst, y[:])

@@ -195,7 +195,7 @@ def tile_list_triangle_edge_update_kernel(
                         start=True, stop=True,
                     )
                 banks.append(bank)
-            gate = work.tile([P, TOK, 4], F32, name="gate")
+            gate = work.tile([P, TOK, 4], F32, name="gate", bufs=16)
             nc.scalar.activation(gate[:], banks[0][:].rearrange("p t n -> p n t"), ACT.Sigmoid)
             ga[u] = work.tile([P, TOK, 4], F32, name="ga")
             nc.vector.tensor_tensor(ga[u][:], banks[1][:].rearrange("p t n -> p n t"), gate[:], ALU.mult)

@@ -17,8 +17,12 @@ ACT = mybir.ActivationFunctionType
 ALU = mybir.AluOpType
 
 P = 128
+PASS = 512
 HALF = 512
+PAIR = 256
 TOK = 128
+IJ, IK, JK = 0, 1, 2
+GROUPS = [(0, 512), (512, 256), (768, 128), (896, 128)]
 
 
 def tile_list_triangle_edge_update_kernel(
@@ -28,285 +32,285 @@ def tile_list_triangle_edge_update_kernel(
     nc = tc.nc
     with ExitStack() as ctx:
         held = ctx.enter_context(tc.tile_pool(name="held", bufs=1))
-        stage = ctx.enter_context(tc.tile_pool(name="stage", bufs=2))
-        work = ctx.enter_context(tc.tile_pool(name="work", bufs=4))
+        work = ctx.enter_context(tc.tile_pool(name="work", bufs=16))
+        reuse = ctx.enter_context(tc.tile_pool(name="reuse", bufs=1))
         psum = ctx.enter_context(tc.psum_pool(name="psum", bufs=2))
 
-        lists = []
-        for i, src in enumerate((offs, offs2, offs3)):
-            lst = held.tile([P, S // 16], U16, name=f"list{i}")
-            nc.sync.dma_start(lst[:], src)
-            lists.append(lst)
-
+        lists = [held.tile([P, S // 16], U16, name=f"list{i}") for i in range(3)]
         tab_w = held.tile([P, T], I32, name="tab_w", align_bytes=64)
         tab_s = held.tile([P, T // 4], I32, name="tab_s", align_bytes=64)
-        w_s = held.tile([P, (2 * H + N) // 4], I32, name="w_s", align_bytes=64)
-        warm_in = held.tile([P, 1], F32, name="warm_in")
-        warm_out = held.tile([P, 1], F32, name="warm_out")
-
-        nc.vector.memset(tab_s[:], 0)
-        nc.vector.memset(warm_in[:], 0.0)
-        nc.vector.memset(w_s[:], 0)
-
-        def load_scale_rows(queues, dst, src):
-            for q in range(4):
-                queues[q // 2].dma_start(dst[32 * q : 32 * q + 4, :], src[0, 4 * q : 4 * q + 4, :].bitcast(I32))
-
-        load_scale_rows((nc.sync, nc.scalar), tab_s, tab_scales)
-        nc.scalar.activation(warm_out[:], warm_in[:], ACT.Sigmoid)
-
-        wg_raw = held.tile([P, H // 2], I32, name="wg_raw")
-        wb_raw = held.tile([P, H], I32, name="wb_raw")
+        w_s = held.tile([P, (H + N) // 4], I32, name="w_s", align_bytes=64)
+        wg_raw = reuse.tile([P, H // 2], I32, name="wg_raw", align_bytes=64, offset=0)
+        wb_raw = reuse.tile([P, H], I32, name="wb_raw", align_bytes=64, offset=2 * H)
+        wb_s_raw = reuse.tile([P, H // 4], I32, name="wb_s_raw", align_bytes=64, offset=6 * H)
         wr_w = held.tile([P, 2 * N], U8, name="wr_w", align_bytes=64)
         bias = held.tile([P, N // P], F32, name="bias")
+        wa_raw = [held.tile([P, 4, PASS], F32, name=f"wa_raw{b}") for b in range(2)]
+        wo_raw = [held.tile([P, 4, N], F32, name=f"wo_raw{b}") for b in range(2)]
+
+        def load_scale_rows(dst, src):
+            for r in range(4):
+                nc.sync.dma_start(dst[r:P:32, :], src[0, r:16:4, :].bitcast(I32))
+
+        def load_wa(b):
+            nc.sync.dma_start(wa_raw[b][:], wa.rearrange("(p j) c -> p j c", j=4)[:, :, b * PASS : (b + 1) * PASS])
+
+        nc.vector.memset(tab_s[:], 0)
+        nc.vector.memset(w_s[:], 0)
+        nc.vector.memset(wb_s_raw[:], 0)
+        for i, src in ((IJ, offs), (JK, offs3), (IK, offs2)):
+            nc.sync.dma_start(lists[i][:], src)
+        load_scale_rows(tab_s, tab_scales)
+        load_wa(0)
+        nc.sync.dma_start(tab_w[:], tab_words[0].rearrange("p t i -> p (t i)").bitcast(I32))
+        load_scale_rows(w_s[:, 0 : H // 4], wg_scales)
         nc.sync.dma_start(wg_raw[:], wg_words[0].bitcast(I32))
         nc.sync.dma_start(wb_raw[:], wb_words[0].rearrange("p c i -> p (c i)").bitcast(I32))
-        wa_raw = []
+        load_wa(1)
+        load_scale_rows(wb_s_raw, wb_scales)
+        wo_rows = wo.rearrange("(b g t e) n -> b t g e n", b=2, t=4, e=8)
         for b in range(2):
-            raw = stage.tile([P, 4, HALF], F32, name="raw")
-            nc.sync.dma_start(raw[:], wa.rearrange("(p j) c -> p j c", j=4)[:, :, b * HALF : (b + 1) * HALF])
-            wa_raw.append(raw)
-            if b == 0:
-                nc.sync.dma_start(tab_w[:], tab_words[0].rearrange("p t i -> p (t i)").bitcast(I32))
-        load_scale_rows((nc.scalar, nc.scalar), w_s[:, 0 : H // 4], wg_scales)
-        load_scale_rows((nc.scalar, nc.scalar), w_s[:, H // 4 : H // 2], wb_scales)
+            for t in range(4):
+                nc.sync.dma_start(wo_raw[b][:, t, :], wo_rows[b, t])
         nc.sync.dma_start(wr_w[:].bitcast(I32), wr_words[0].bitcast(I32))
+        load_scale_rows(w_s[:, H // 4 :], wr_scales)
         with nc.allow_non_contiguous_dma(reason="one bias value a partition"):
             nc.sync.dma_start(bias[:], bo.rearrange("(c p) -> p c", p=P))
-        wr_s = w_s[:, H // 2 :].bitcast(U8)
+        wr_s = w_s[:, H // 4 :].bitcast(U8)
 
         v_w = {}
         v_s = {}
 
-        def gather_scales(i):
-            both = held.tile([P, S], U8, name=f"v_s{i}", align_bytes=64)
-            nc.vector.tensor_copy(both[:], tab_s[:].bitcast(U8).indirect(lists[i][:]))
-            for h in range(2):
-                v_s[i, h] = both[:, h * HALF : (h + 1) * HALF]
+        def gather_scales(i, halves, dst):
+            for h in halves:
+                v_s[i, h] = dst[:, (h - halves[0]) * HALF : (h - halves[0] + 1) * HALF]
+            nc.vector.tensor_copy(dst, tab_s[:].bitcast(U8).indirect(lists[i][:, 32 * halves[0] : 32 * halves[-1] + 32]))
 
-        def gather_words(i, h):
-            v_w[i, h] = held.tile([P, HALF], U32, name=f"v_w{i}{h}", align_bytes=64)
-            nc.vector.tensor_copy(v_w[i, h][:], tab_w[:].bitcast(U32).indirect(lists[i][:, 32 * h : 32 * h + 32]))
+        def gather_words(i, h, dst):
+            v_w[i, h] = dst
+            nc.vector.tensor_copy(dst, tab_w[:].bitcast(U32).indirect(lists[i][:, 32 * h : 32 * h + 32]))
 
-        for i in range(3):
-            gather_scales(i)
+        def picked(i, tok0, ntok):
+            h, lo = divmod(tok0, HALF)
+            return v_w[i, h][:, lo : lo + ntok].bitcast(FP8X4), v_s[i, h][:, lo : lo + ntok]
 
-        wg_w = held.tile([P, 2 * H], U8, name="wg_w", align_bytes=64)
-        wb_w = held.tile([P, H], U32, name="wb_w", align_bytes=64)
-        gb_s = held.tile([P, 2 * H], U8, name="gb_s", align_bytes=64)
-        nc.vector.tensor_copy(
-            gb_s[:].bitcast(U16).rearrange("p (c t g) -> p c t g", c=4, t=4),
-            w_s[:, 0 : H // 2].bitcast(U16).rearrange("p (c g t) -> p c t g", c=4, t=4),
-        )
+        wg_w = held.tile([P, H // 2], I32, name="wg_w", align_bytes=64)
+        wb_w = held.tile([P, H], I32, name="wb_w", align_bytes=64)
+        gb_s = held.tile([P, H // 2], I32, name="gb_s", align_bytes=64)
+        wg_s = gb_s[:, 0 : H // 4].bitcast(U8)
+        wb_s = gb_s[:, H // 4 :].bitcast(U8)
 
-        def permute_words(b):
+        def deal_columns(dst, src):
             nc.vector.tensor_copy(
-                wg_w[:, b * 2 * HALF : (b + 1) * 2 * HALF].bitcast(I32).rearrange("p (t g) -> p t g", t=4),
-                wg_raw[:, b * HALF // 2 : (b + 1) * HALF // 2].rearrange("p (g t) -> p t g", t=4),
-            )
-            nc.vector.tensor_copy(
-                wb_w[:, b * HALF : (b + 1) * HALF].bitcast(I32).rearrange("p (t g i) -> p t g i", t=4, i=2),
-                wb_raw[:, b * HALF : (b + 1) * HALF].rearrange("p (g t i) -> p t g i", t=4, i=2),
+                dst.rearrange("p (b t g e) -> p b t g e", b=2, t=4, g=16),
+                src.rearrange("p (b g t e) -> p b t g e", b=2, t=4, g=16),
             )
 
         wa_w = held.tile([P, H], U32, name="wa_w", align_bytes=64)
         wa_s = held.tile([P, H], U8, name="wa_s", align_bytes=64)
         wo_w = held.tile([P, 2 * N], U32, name="wo_w", align_bytes=64)
         wo_s = held.tile([P, 2 * N], U8, name="wo_s", align_bytes=64)
-        w_bf = {}
+        wa_bf = [held.tile([P, 4, P, 4], BF16, name=f"wa_bf{b}", align_bytes=64) for b in range(2)]
+        wo_bf = [held.tile([P, N, 4], BF16, name=f"wo_bf{b}", align_bytes=64) for b in range(2)]
 
         def round_wa(b):
-            w_bf["a", b] = held.tile([P, 4, TOK, 4], BF16, name="w_bf", align_bytes=64)
             for t in range(4):
                 nc.scalar.copy(
-                    w_bf["a", b][:, t].rearrange("p (g i) j -> p g j i", i=2),
-                    wa_raw[b][:].rearrange("p j (g t i) -> p t g j i", t=4, i=2)[:, t],
+                    wa_bf[b][:, t].rearrange("p (g e i) j -> p g e j i", e=2, i=4),
+                    wa_raw[b][:].rearrange("p j (g t e i) -> p t g e j i", t=4, e=2, i=4)[:, t],
                 )
 
-        def quantize_wa(b):
-            cols = slice(b * HALF, (b + 1) * HALF)
-            nc.vector.quantize_mx(
-                out=wa_w[:, cols].bitcast(FP8X4),
-                scales=wa_s[:, cols],
-                in_=w_bf["a", b][:].rearrange("p t m j -> p (t m j)"),
+        def round_wo(b, c):
+            cols = slice(c * P, (c + 1) * P)
+            nc.scalar.copy(
+                wo_bf[b][:, cols, :].rearrange("p (m i) t -> p m t i", i=4),
+                wo_raw[b][:, :, cols].rearrange("p t (m i) -> p m t i", i=4),
             )
 
-        wo_raw = {}
+        def quantize(codes, scales, values):
+            nc.vector.quantize_mx(out=codes.bitcast(FP8X4), scales=scales, in_=values)
 
-        def load_wo(b, e):
-            if e == 0:
-                wo_raw[b] = stage.tile([P, 4, HALF], F32, name="raw")
-            rows = wo.rearrange("(b g t e) n -> b e g t n", b=2, t=4, e=2)
-            (nc.scalar if (b, e) == (1, 1) else nc.sync).dma_start(wo_raw[b][e:P:2, :, :], rows[b, e])
-
-        def round_wo(b):
-            w_bf["o", b] = held.tile([P, N, 4], BF16, name="w_bf", align_bytes=64)
-            for c in range(4):
-                cols = slice(c * P, (c + 1) * P)
-                nc.gpsimd.tensor_scalar(
-                    w_bf["o", b][:, cols, :], wo_raw[b][:, :, cols].rearrange("p t n -> p n t"),
-                    1.0, 0.0, ALU.mult, ALU.add,
-                )
+        def quantize_wa(b):
+            cols = slice(b * PASS, (b + 1) * PASS)
+            quantize(wa_w[:, cols], wa_s[:, cols], wa_bf[b][:].rearrange("p t m j -> p (t m j)"))
 
         def quantize_wo(b):
             cols = slice(b * N, (b + 1) * N)
-            nc.vector.quantize_mx(
-                out=wo_w[:, cols].bitcast(FP8X4),
-                scales=wo_s[:, cols],
-                in_=w_bf["o", b][:].rearrange("p n t -> p (n t)"),
+            quantize(wo_w[:, cols], wo_s[:, cols], wo_bf[b][:].rearrange("p n t -> p (n t)"))
+
+        def lone_pass(dst, codes, scales, rhs):
+            nc.tensor.matmul_mx(
+                out=dst, lhsT=codes, lhsT_scale=scales, rhs=rhs[0], rhs_scale=rhs[1], start=True, stop=True
             )
 
-        permute_words(0)
-        round_wa(0)
-        quantize_wa(0)
-        load_scale_rows((nc.scalar, nc.scalar), w_s[:, H // 2 :], wr_scales)
-        for e in range(2):
-            load_wo(0, e)
-        permute_words(1)
-        for i in (0, 2, 1):
-            gather_words(i, 0)
-        round_wa(1)
+        gate = {}
+        gb = {}
 
-        units = [(0, b, k) for b in range(2) for k in range(HALF // TOK)]
-        units += [(1, b, k) for k in range(HALF // TOK) for b in range(2)]
+        def gate_pair(tok0, b, s):
+            bank = psum.tile([P, 2, PAIR], F32, name="g_bank")
+            for u in range(2):
+                c0 = b * PASS + (2 * s + u) * P
+                lone_pass(
+                    bank[:, u, :], wg_w[:].bitcast(U8)[:, 2 * c0 : 2 * c0 + 2 * P].bitcast(FP4X4),
+                    wg_s[:, c0 : c0 + P], picked(IJ, tok0, PAIR),
+                )
+            gate[tok0, b, s] = work.tile([P, PAIR, 2], F32, name="gate")
+            nc.scalar.activation(gate[tok0, b, s][:], bank[:].rearrange("p u n -> p n u"), ACT.Sigmoid)
+
+        def gate_times_b(tok0, b, s):
+            bank = psum.tile([P, 2, PAIR], F32, name="b_bank")
+            for u in range(2):
+                c0 = b * PASS + (2 * s + u) * P
+                lone_pass(
+                    bank[:, u, :], wb_w[:, c0 : c0 + P].bitcast(FP8X4),
+                    wb_s[:, c0 : c0 + P], picked(JK, tok0, PAIR),
+                )
+            if s == 0:
+                gb[tok0, b] = work.tile([P, 2, PAIR, 2], F32, name="gb", bufs=8)
+            nc.vector.tensor_tensor(
+                gb[tok0, b][:, s], bank[:].rearrange("p u n -> p n u"), gate[tok0, b, s][:], ALU.mult
+            )
+
         h_bf = {}
         h_w = {}
         h_s = {}
-        ga = {}
-        b_bank = {}
+        for tok0, ntok in GROUPS:
+            h_bf[tok0] = held.tile([P, 2, ntok, 4], BF16, name=f"h_bf{tok0}", align_bytes=64)
+            h_w[tok0] = held.tile([P, 2 * ntok], U32, name=f"h_w{tok0}", align_bytes=64)
+            h_s[tok0] = held.tile([P, 2 * ntok], U8, name=f"h_s{tok0}", align_bytes=64)
 
-        def first_products(u):
-            h, b, k = units[u]
-            tok = slice(k * TOK, (k + 1) * TOK)
-            banks = []
-            for name, i in (("g_bank", 0), ("a_bank", 1), ("b_bank", 2)):
-                bank = psum.tile([P, 4, TOK], F32, name=name)
-                for t in range(4):
-                    c0 = b * HALF + t * P
-                    if i == 0:
-                        lhsT, lhsT_s = wg_w[:, 2 * c0 : 2 * c0 + 2 * P].bitcast(FP4X4), gb_s[:, c0 : c0 + P]
-                    elif i == 1:
-                        lhsT, lhsT_s = wa_w[:, c0 : c0 + P].bitcast(FP8X4), wa_s[:, c0 : c0 + P]
-                    else:
-                        lhsT, lhsT_s = wb_w[:, c0 : c0 + P].bitcast(FP8X4), gb_s[:, H + c0 : H + c0 + P]
-                    nc.tensor.matmul_mx(
-                        out=bank[:, t, :], lhsT=lhsT, lhsT_scale=lhsT_s,
-                        rhs=v_w[i, h][:, tok].bitcast(FP8X4), rhs_scale=v_s[i, h][:, tok],
-                        start=True, stop=True,
-                    )
-                banks.append(bank)
-            gate = work.tile([P, TOK, 4], F32, name="gate", bufs=16)
-            nc.scalar.activation(gate[:], banks[0][:].rearrange("p t n -> p n t"), ACT.Sigmoid)
-            ga[u] = work.tile([P, TOK, 4], F32, name="ga")
-            nc.vector.tensor_tensor(ga[u][:], banks[1][:].rearrange("p t n -> p n t"), gate[:], ALU.mult)
-            b_bank[u] = banks[2]
-
-        def message(u):
-            h, b, k = units[u]
-            if k == 0:
-                h_bf[h, b] = held.tile([P, HALF, 4], BF16, name=f"h_bf{h}{b}", align_bytes=64)
-                h_w[h, b] = held.tile([P, HALF], U32, name=f"h_w{h}{b}", align_bytes=64)
-                h_s[h, b] = held.tile([P, HALF], U8, name=f"h_s{h}{b}", align_bytes=64)
+        def message(tok0, b, k):
+            tok = tok0 + k * TOK
+            bank = psum.tile([P, 4, TOK], F32, name="a_bank")
+            for t in range(4):
+                c0 = b * PASS + t * P
+                lone_pass(bank[:, t, :], wa_w[:, c0 : c0 + P].bitcast(FP8X4), wa_s[:, c0 : c0 + P], picked(IK, tok, TOK))
+            first = max(g0 for g0, ntok in GROUPS if g0 <= tok)
             nc.vector.tensor_tensor(
-                h_bf[h, b][:, k * TOK : (k + 1) * TOK, :], b_bank[u][:].rearrange("p t n -> p n t"), ga[u][:], ALU.mult
+                h_bf[first][:, b, tok - first : tok - first + TOK, :].rearrange("p n (s u) -> p n s u", s=2),
+                bank[:].rearrange("p (s u) n -> p n s u", s=2),
+                gb[tok0, b][:, :, k * TOK : (k + 1) * TOK, :].rearrange("p s n u -> p n s u"),
+                ALU.mult,
             )
 
-        def quantize_h(h, b, lo, hi):
-            nc.vector.quantize_mx(
-                out=h_w[h, b][:, lo:hi].bitcast(FP8X4),
-                scales=h_s[h, b][:, lo:hi],
-                in_=h_bf[h, b][:, lo:hi, :].rearrange("p n t -> p (n t)"),
-            )
+        def quantize_h(group, passes):
+            tok0, ntok = group
+            cols = slice(passes[0] * ntok, (passes[-1] + 1) * ntok)
+            values = h_bf[tok0][:].rearrange("p b n t -> p (b n t)")[:, 4 * cols.start : 4 * cols.stop]
+            quantize(h_w[tok0][:, cols], h_s[tok0][:, cols], values)
 
-        def quantize_unit(u):
-            h, b, k = units[u]
-            quantize_h(h, b, k * TOK, (k + 1) * TOK)
+        y_bank = {}
 
-        def y_pass(dst, h, tok, c, step):
-            if step == 0:
-                nc.tensor.matmul_mx(
-                    out=dst, lhsT=wr_w[:, 2 * c * P : 2 * (c + 1) * P].bitcast(FP4X4),
-                    lhsT_scale=wr_s[:, c * P : (c + 1) * P],
-                    rhs=v_w[0, h][:, tok].bitcast(FP8X4), rhs_scale=v_s[0, h][:, tok], start=True, stop=False,
-                )
-            else:
-                b = step - 1
+        def open_y(group, cs, tag="y_bank"):
+            tok0, ntok = group
+            y_bank[tok0, cs[0]] = psum.tile([P, len(cs), ntok], F32, name=tag)
+            width = ntok if ntok == HALF else TOK
+            for c in cs:
+                for lo in range(0, ntok, width):
+                    rhs = picked(IJ, tok0 + lo, width)
+                    nc.tensor.matmul_mx(
+                        out=y_bank[tok0, cs[0]][:, c - cs[0], lo : lo + width],
+                        lhsT=wr_w[:, 2 * c * P : 2 * (c + 1) * P].bitcast(FP4X4), lhsT_scale=wr_s[:, c * P : (c + 1) * P],
+                        rhs=rhs[0], rhs_scale=rhs[1], start=(c == cs[0] and lo == 0), stop=False,
+                    )
+
+        def add_to_y(group, cs, b):
+            tok0, ntok = group
+            for c in cs:
                 cols = slice(b * N + c * P, b * N + (c + 1) * P)
                 nc.tensor.matmul_mx(
-                    out=dst, lhsT=wo_w[:, cols].bitcast(FP8X4), lhsT_scale=wo_s[:, cols],
-                    rhs=h_w[h, b][:, tok].bitcast(FP8X4), rhs_scale=h_s[h, b][:, tok], start=False, stop=(b == 1),
+                    out=y_bank[tok0, cs[0]][:, c - cs[0], :], lhsT=wo_w[:, cols].bitcast(FP8X4), lhsT_scale=wo_s[:, cols],
+                    rhs=h_w[tok0][:, b * ntok : (b + 1) * ntok].bitcast(FP8X4), rhs_scale=h_s[tok0][:, b * ntok : (b + 1) * ntok],
+                    start=False, stop=(b == 1 and c == cs[-1]),
                 )
 
-        def add_bias(dst, src, c, on_vector):
-            if on_vector:
-                nc.vector.tensor_scalar(dst, src, bias[:, c : c + 1], None, ALU.add)
-            else:
-                nc.scalar.activation(dst, src, ACT.Identity, bias=bias[:, c : c + 1])
-
-        wide_bank = {}
-
-        def y_wide(c, steps):
-            for step in steps:
-                if step == 0:
-                    wide_bank[c] = psum.tile([P, HALF], F32, name="y_bank")
-                y_pass(wide_bank[c][:], 0, slice(0, HALF), c, step)
-            if steps[-1] == 2:
-                y = work.tile([P, HALF], F32, name="y", bufs=8)
-                add_bias(y[:], wide_bank[c][:], c, False)
-                nc.sync.dma_start(out[c * P : (c + 1) * P, 0:HALF], y[:])
-
-        def store_narrow(k, y):
-            dst = out.rearrange("(c p) s -> p c s", p=P)[:, :, HALF + k * TOK : HALF + (k + 1) * TOK]
+        def store_y(group, cs, on_vector=False):
+            tok0, ntok = group
+            y = work.tile([P, len(cs), ntok], F32, name="y", bufs=9)
+            for c in cs:
+                src = y_bank[tok0, cs[0]][:, c - cs[0], :]
+                if on_vector:
+                    nc.vector.tensor_scalar(y[:, c - cs[0], :], src, bias[:, c : c + 1], None, ALU.add)
+                else:
+                    nc.scalar.activation(y[:, c - cs[0], :], src, ACT.Identity, bias=bias[:, c : c + 1])
+            dst = out.rearrange("(c p) s -> p c s", p=P)[:, cs[0] : cs[-1] + 1, tok0 : tok0 + ntok]
             nc.sync.dma_start(dst, y[:])
 
-        def y_narrow(k):
-            tok = slice(k * TOK, (k + 1) * TOK)
-            bank = psum.tile([P, 4, TOK], F32, name="y_bank")
-            for c in range(4):
-                for step in range(3):
-                    y_pass(bank[:, c, :], 1, tok, c, step)
-            y = work.tile([P, 4, TOK], F32, name="y", bufs=8)
-            for c in range(4):
-                add_bias(y[:, c, :], bank[:, c, :], c, False)
-            store_narrow(k, y)
+        def whole_y(group, cs):
+            open_y(group, cs)
+            for b in range(2):
+                add_to_y(group, cs, b)
+            store_y(group, cs)
 
-        extra = {
-            0: [lambda: load_wo(1, 0), lambda: load_wo(1, 1)],
-            1: [lambda: gather_words(0, 1), lambda: quantize_wa(1), lambda: round_wo(0)],
-            3: [lambda: gather_words(2, 1)],
-            4: [lambda: gather_words(1, 1), lambda: quantize_wo(0), lambda: round_wo(1)],
-            5: [lambda: quantize_h(0, 0, 0, HALF)],
-            7: [lambda: y_wide(0, [0, 1]), lambda: y_wide(1, [0, 1])],
-            8: [lambda: quantize_wo(1)],
-            9: [lambda: quantize_h(0, 1, 0, HALF), lambda: y_wide(0, [2]), lambda: y_wide(1, [2])],
-            10: [lambda: quantize_unit(8), lambda: y_wide(2, [0, 1, 2])],
-            11: [lambda: quantize_unit(9), lambda: y_wide(3, [0, 1, 2])],
-            12: [lambda: quantize_unit(10), lambda: y_narrow(0)],
-            13: [lambda: quantize_unit(11), lambda: y_narrow(1)],
-            14: [lambda: quantize_unit(12)],
-            15: [lambda: quantize_unit(13), lambda: y_narrow(2)],
-        }
-        for u in range(len(units)):
-            first_products(u)
-            for step in extra.get(u, []):
-                step()
-            if u > 0:
-                message(u - 1)
-        message(len(units) - 1)
-        last = slice(3 * TOK, HALF)
-        banks = []
-        for c in range(4):
-            bank = psum.tile([P, TOK], F32, name="g_bank" if c < 2 else "a_bank")
-            y_pass(bank[:], 1, last, c, 0)
-            banks.append(bank)
+        for i, halves in ((IJ, [0, 1]), (JK, [0, 1]), (IK, [0])):
+            picked_s = held.tile([P, len(halves) * HALF], U8, name=f"picked_s{i}", align_bytes=64)
+            gather_scales(i, halves, picked_s[:])
+        round_wa(0)
+        quantize_wa(0)
+        first_w = held.tile([P, HALF], U32, name="first_w", align_bytes=64)
+        gather_words(IJ, 0, first_w[:])
+        deal_columns(gb_s[:, 0 : H // 4], w_s[:, 0 : H // 4])
+        deal_columns(wg_w[:], wg_raw[:])
+        second_w = reuse.tile([P, HALF], U32, name="second_w", align_bytes=64, offset=0)
+        gather_words(JK, 0, second_w[:])
+        deal_columns(wb_w[:], wb_raw[:])
+        third_w = reuse.tile([P, HALF], U32, name="third_w", align_bytes=64, offset=2 * H)
+        gather_words(IK, 0, third_w[:])
+        deal_columns(gb_s[:, H // 4 :], wb_s_raw[:])
+        late_s = reuse.tile([P, HALF], U8, name="late_s", align_bytes=64, offset=6 * H)
+        late_w = reuse.tile([P, 3 * HALF], U32, name="late_w", align_bytes=64, offset=6 * H + HALF)
+        gather_words(IJ, 1, late_w[:, 0:HALF])
+        gather_words(JK, 1, late_w[:, HALF : 2 * HALF])
+        gather_scales(IK, [1], late_s[:])
+        gather_words(IK, 1, late_w[:, 2 * HALF :])
+
+        def gates(tok0, b):
+            for s in range(2):
+                gate_pair(tok0, b, s)
+
+        def products(tok0, b):
+            for s in range(2):
+                gate_times_b(tok0, b, s)
+
+        units = [(0, 0), (256, 0), (0, 1), (256, 1), (512, 0), (512, 1), (768, 0), (768, 1)]
+        for unit in units[:4]:
+            gates(*unit)
+        round_wa(1)
+        for unit in units[4:]:
+            gates(*unit)
         for b in range(2):
-            quantize_unit(14 + b)
-        for c in range(4):
-            y_pass(banks[c][:], 1, last, c, 1)
-        for c0 in (0, 2):
-            y = work.tile([P, 2, TOK], F32, name="y", bufs=8)
-            for c in (c0, c0 + 1):
-                y_pass(banks[c][:], 1, last, c, 2)
-                add_bias(y[:, c - c0, :], banks[c][:], c, c < 3)
-            dst = out.rearrange("(c p) s -> p c s", p=P)[:, c0 : c0 + 2, S - TOK :]
-            nc.sync.dma_start(dst, y[:])
+            for c in range(4):
+                round_wo(b, c)
+        extra = {
+            (1, 0): [lambda: quantize_wa(1)],
+            (3, 0): [lambda: quantize_h(GROUPS[0], [0]), lambda: quantize_wo(0)],
+            (3, 1): [lambda: quantize_wo(1)],
+            (5, 0): [lambda: quantize_h(GROUPS[0], [1]), lambda: whole_y(GROUPS[0], [0])],
+            (5, 1): [lambda: whole_y(GROUPS[0], [1])],
+            (6, 0): [lambda: whole_y(GROUPS[0], [2])],
+            (6, 1): [lambda: whole_y(GROUPS[0], [3])],
+            (7, 0): [lambda: quantize_h(GROUPS[1], [0, 1]), lambda: whole_y(GROUPS[1], [0, 1])],
+            (7, 1): [lambda: whole_y(GROUPS[1], [2, 3])],
+        }
+        for u, (tok0, b) in enumerate(units):
+            for s in range(2):
+                gate_times_b(tok0, b, s)
+                for step in extra.get((u, s), []):
+                    step()
+                if u > 0 and (u, s) != (7, 1):
+                    message(units[u - 1][0], units[u - 1][1], s)
+        tail = GROUPS[3]
+        tail_banks = ([0, 1], [2, 3])
+        message(768, 1, 0)
+        message(768, 0, 1)
+        quantize_h(GROUPS[2], [0, 1])
+        whole_y(GROUPS[2], [0, 1, 2, 3])
+        message(768, 1, 1)
+        quantize_h(tail, [0])
+        for cs in tail_banks:
+            open_y(tail, cs, "g_bank")
+            add_to_y(tail, cs, 0)
+        quantize_h(tail, [1])
+        for cs in tail_banks:
+            add_to_y(tail, cs, 1)
+            store_y(tail, cs, on_vector=(cs[0] == 0))

@@ -34,12 +34,22 @@ def tile_list_triangle_edge_update_kernel(
         held = ctx.enter_context(tc.tile_pool(name="held", bufs=1))
         work = ctx.enter_context(tc.tile_pool(name="work", bufs=16))
         reuse = ctx.enter_context(tc.tile_pool(name="reuse", bufs=1))
-        psum = ctx.enter_context(tc.psum_pool(name="psum", bufs=2))
+        psum = ctx.enter_context(tc.psum_pool(name="psum", bufs=1))
+        banks = [psum.tile([P, 512], F32, name=f"bank{i}") for i in range(8)]
+        dealt = {"ring": [0, 1, 2, 3], "a": [4, 5], "y": [6, 7]}
+        turns = {"ring": 0, "a": 0, "y": 0}
+
+        def next_bank(kind, rows):
+            bank = banks[dealt[kind][turns[kind] % len(dealt[kind])]]
+            turns[kind] = turns[kind] + 1
+            return bank[:].rearrange("p (r n) -> p r n", r=rows)
+
 
         lists = [held.tile([P, S // 16], U16, name=f"list{i}") for i in range(3)]
         tab_w = held.tile([P, T], I32, name="tab_w", align_bytes=64)
         tab_s = held.tile([P, T // 4], I32, name="tab_s", align_bytes=64)
-        w_s = held.tile([P, (H + N) // 4], I32, name="w_s", align_bytes=64)
+        wg_s_raw = held.tile([P, H // 4], I32, name="wg_s_raw", align_bytes=64)
+        wr_s_rows = held.tile([P, N // 4], I32, name="wr_s_rows", align_bytes=64)
         wg_raw = reuse.tile([P, H // 2], I32, name="wg_raw", align_bytes=64, offset=0)
         wb_raw = reuse.tile([P, H], I32, name="wb_raw", align_bytes=64, offset=2 * H)
         wb_s_raw = reuse.tile([P, H // 4], I32, name="wb_s_raw", align_bytes=64, offset=6 * H)
@@ -56,14 +66,18 @@ def tile_list_triangle_edge_update_kernel(
             nc.sync.dma_start(wa_raw[b][:], wa.rearrange("(p j) c -> p j c", j=4)[:, :, b * PASS : (b + 1) * PASS])
 
         nc.vector.memset(tab_s[:], 0)
-        nc.vector.memset(w_s[:], 0)
+        nc.vector.memset(wg_s_raw[:], 0)
         nc.vector.memset(wb_s_raw[:], 0)
+        nc.vector.memset(wr_s_rows[:], 0)
+        warm = held.tile([P, 2], F32, name="warm")
+        nc.vector.memset(warm[:, 0:1], 0.0)
+        nc.scalar.activation(warm[:, 1:2], warm[:, 0:1], ACT.Sigmoid)
         for i, src in ((IJ, offs), (JK, offs3), (IK, offs2)):
             nc.sync.dma_start(lists[i][:], src)
         load_scale_rows(tab_s, tab_scales)
         load_wa(0)
         nc.sync.dma_start(tab_w[:], tab_words[0].rearrange("p t i -> p (t i)").bitcast(I32))
-        load_scale_rows(w_s[:, 0 : H // 4], wg_scales)
+        load_scale_rows(wg_s_raw, wg_scales)
         nc.sync.dma_start(wg_raw[:], wg_words[0].bitcast(I32))
         nc.sync.dma_start(wb_raw[:], wb_words[0].rearrange("p c i -> p (c i)").bitcast(I32))
         load_wa(1)
@@ -73,10 +87,10 @@ def tile_list_triangle_edge_update_kernel(
             for t in range(4):
                 nc.sync.dma_start(wo_raw[b][:, t, :], wo_rows[b, t])
         nc.sync.dma_start(wr_w[:].bitcast(I32), wr_words[0].bitcast(I32))
-        load_scale_rows(w_s[:, H // 4 :], wr_scales)
+        load_scale_rows(wr_s_rows, wr_scales)
         with nc.allow_non_contiguous_dma(reason="one bias value a partition"):
             nc.sync.dma_start(bias[:], bo.rearrange("(c p) -> p c", p=P))
-        wr_s = w_s[:, H // 4 :].bitcast(U8)
+        wr_s = wr_s_rows[:].bitcast(U8)
 
         v_w = {}
         v_s = {}
@@ -110,10 +124,12 @@ def tile_list_triangle_edge_update_kernel(
         wa_s = held.tile([P, H], U8, name="wa_s", align_bytes=64)
         wo_w = held.tile([P, 2 * N], U32, name="wo_w", align_bytes=64)
         wo_s = held.tile([P, 2 * N], U8, name="wo_s", align_bytes=64)
-        wa_bf = [held.tile([P, 4, P, 4], BF16, name=f"wa_bf{b}", align_bytes=64) for b in range(2)]
-        wo_bf = [held.tile([P, N, 4], BF16, name=f"wo_bf{b}", align_bytes=64) for b in range(2)]
+        wa_bf = {}
+        wo_bf = {}
+        STAGE = 16 * H
 
-        def round_wa(b):
+        def round_wa(b, place):
+            wa_bf[b] = reuse.tile([P, 4, P, 4], BF16, name=f"wa_bf{b}", align_bytes=64, offset=STAGE + place * 2 * H)
             for t in range(4):
                 nc.scalar.copy(
                     wa_bf[b][:, t].rearrange("p (g e i) j -> p g e j i", e=2, i=4),
@@ -143,11 +159,12 @@ def tile_list_triangle_edge_update_kernel(
                 out=dst, lhsT=codes, lhsT_scale=scales, rhs=rhs[0], rhs_scale=rhs[1], start=True, stop=True
             )
 
+        b_outs = []
         gate = {}
         gb = {}
 
         def gate_pair(tok0, b, s):
-            bank = psum.tile([P, 2, PAIR], F32, name="g_bank")
+            bank = next_bank("ring", 2)
             for u in range(2):
                 c0 = b * PASS + (2 * s + u) * P
                 lone_pass(
@@ -155,10 +172,10 @@ def tile_list_triangle_edge_update_kernel(
                     wg_s[:, c0 : c0 + P], picked(IJ, tok0, PAIR),
                 )
             gate[tok0, b, s] = work.tile([P, PAIR, 2], F32, name="gate")
-            nc.scalar.activation(gate[tok0, b, s][:], bank[:].rearrange("p u n -> p n u"), ACT.Sigmoid)
+            nc.scalar.activation(gate[tok0, b, s][:], bank.rearrange("p u n -> p n u"), ACT.Sigmoid)
 
-        def gate_times_b(tok0, b, s):
-            bank = psum.tile([P, 2, PAIR], F32, name="b_bank")
+        def gate_times_b(tok0, b, s, on_gpsimd=False):
+            bank = next_bank("ring", 2)
             for u in range(2):
                 c0 = b * PASS + (2 * s + u) * P
                 lone_pass(
@@ -167,9 +184,16 @@ def tile_list_triangle_edge_update_kernel(
                 )
             if s == 0:
                 gb[tok0, b] = work.tile([P, 2, PAIR, 2], F32, name="gb", bufs=8)
-            nc.vector.tensor_tensor(
-                gb[tok0, b][:, s], bank[:].rearrange("p u n -> p n u"), gate[tok0, b, s][:], ALU.mult
-            )
+            if on_gpsimd:
+                place = len(b_outs)
+                b_out = reuse.tile([P, PAIR, 2], F32, name=f"b_out{place}", align_bytes=64, offset=STAGE + (place if place < 8 else place + 2) * 2 * H)
+                b_outs.append(b_out)
+                nc.scalar.copy(b_out[:], bank.rearrange("p u n -> p n u"))
+                nc.gpsimd.tensor_tensor(gb[tok0, b][:, s], b_out[:], gate[tok0, b, s][:], ALU.mult)
+            else:
+                nc.vector.tensor_tensor(
+                    gb[tok0, b][:, s], bank.rearrange("p u n -> p n u"), gate[tok0, b, s][:], ALU.mult
+                )
 
         h_bf = {}
         h_w = {}
@@ -181,14 +205,14 @@ def tile_list_triangle_edge_update_kernel(
 
         def message(tok0, b, k):
             tok = tok0 + k * TOK
-            bank = psum.tile([P, 4, TOK], F32, name="a_bank")
+            bank = next_bank("a", 4)
             for t in range(4):
                 c0 = b * PASS + t * P
                 lone_pass(bank[:, t, :], wa_w[:, c0 : c0 + P].bitcast(FP8X4), wa_s[:, c0 : c0 + P], picked(IK, tok, TOK))
             first = max(g0 for g0, ntok in GROUPS if g0 <= tok)
             nc.vector.tensor_tensor(
                 h_bf[first][:, b, tok - first : tok - first + TOK, :].rearrange("p n (s u) -> p n s u", s=2),
-                bank[:].rearrange("p (s u) n -> p n s u", s=2),
+                bank.rearrange("p (s u) n -> p n s u", s=2),
                 gb[tok0, b][:, :, k * TOK : (k + 1) * TOK, :].rearrange("p s n u -> p n s u"),
                 ALU.mult,
             )
@@ -201,9 +225,9 @@ def tile_list_triangle_edge_update_kernel(
 
         y_bank = {}
 
-        def open_y(group, cs, tag="y_bank"):
+        def open_y(group, cs, kind="y"):
             tok0, ntok = group
-            y_bank[tok0, cs[0]] = psum.tile([P, len(cs), ntok], F32, name=tag)
+            y_bank[tok0, cs[0]] = next_bank(kind, 512 // ntok)
             width = ntok if ntok == HALF else TOK
             for c in cs:
                 for lo in range(0, ntok, width):
@@ -236,8 +260,8 @@ def tile_list_triangle_edge_update_kernel(
             dst = out.rearrange("(c p) s -> p c s", p=P)[:, cs[0] : cs[-1] + 1, tok0 : tok0 + ntok]
             nc.sync.dma_start(dst, y[:])
 
-        def whole_y(group, cs):
-            open_y(group, cs)
+        def whole_y(group, cs, kind="y"):
+            open_y(group, cs, kind)
             for b in range(2):
                 add_to_y(group, cs, b)
             store_y(group, cs)
@@ -245,11 +269,11 @@ def tile_list_triangle_edge_update_kernel(
         for i, halves in ((IJ, [0, 1]), (JK, [0, 1]), (IK, [0])):
             picked_s = held.tile([P, len(halves) * HALF], U8, name=f"picked_s{i}", align_bytes=64)
             gather_scales(i, halves, picked_s[:])
-        round_wa(0)
+        round_wa(0, 8)
         quantize_wa(0)
         first_w = held.tile([P, HALF], U32, name="first_w", align_bytes=64)
         gather_words(IJ, 0, first_w[:])
-        deal_columns(gb_s[:, 0 : H // 4], w_s[:, 0 : H // 4])
+        deal_columns(gb_s[:, 0 : H // 4], wg_s_raw[:])
         deal_columns(wg_w[:], wg_raw[:])
         second_w = reuse.tile([P, HALF], U32, name="second_w", align_bytes=64, offset=0)
         gather_words(JK, 0, second_w[:])
@@ -268,47 +292,72 @@ def tile_list_triangle_edge_update_kernel(
             for s in range(2):
                 gate_pair(tok0, b, s)
 
-        def products(tok0, b):
+        def products(tok0, b, on_gpsimd=False):
             for s in range(2):
-                gate_times_b(tok0, b, s)
+                gate_times_b(tok0, b, s, on_gpsimd)
 
-        units = [(0, 0), (256, 0), (0, 1), (256, 1), (512, 0), (512, 1), (768, 0), (768, 1)]
-        for unit in units[:4]:
-            gates(*unit)
-        round_wa(1)
-        for unit in units[4:]:
-            gates(*unit)
-        for b in range(2):
+        def messages(tok0, b):
+            for k in range(2):
+                message(tok0, b, k)
+
+        def round_wo_pass(b, place):
+            wo_bf[b] = reuse.tile([P, N, 4], BF16, name=f"wo_bf{b}", align_bytes=64, offset=STAGE + place * 2 * H)
             for c in range(4):
                 round_wo(b, c)
-        extra = {
-            (1, 0): [lambda: quantize_wa(1)],
-            (3, 0): [lambda: quantize_h(GROUPS[0], [0]), lambda: quantize_wo(0)],
-            (3, 1): [lambda: quantize_wo(1)],
-            (5, 0): [lambda: quantize_h(GROUPS[0], [1]), lambda: whole_y(GROUPS[0], [0])],
-            (5, 1): [lambda: whole_y(GROUPS[0], [1])],
-            (6, 0): [lambda: whole_y(GROUPS[0], [2])],
-            (6, 1): [lambda: whole_y(GROUPS[0], [3])],
-            (7, 0): [lambda: quantize_h(GROUPS[1], [0, 1]), lambda: whole_y(GROUPS[1], [0, 1])],
-            (7, 1): [lambda: whole_y(GROUPS[1], [2, 3])],
-        }
-        for u, (tok0, b) in enumerate(units):
-            for s in range(2):
-                gate_times_b(tok0, b, s)
-                for step in extra.get((u, s), []):
-                    step()
-                if u > 0 and (u, s) != (7, 1):
-                    message(units[u - 1][0], units[u - 1][1], s)
+
+
+        gates(0, 0)
+        gates(256, 0)
+        gates(0, 1)
+        products(0, 0, True)
+        products(256, 0, True)
+        gates(512, 0)
+        round_wa(1, 0)
+        messages(0, 0)
+        products(512, 0)
+        products(0, 1, True)
+        gates(256, 1)
+        products(256, 1, True)
+        messages(256, 0)
+        quantize_wa(1)
+        messages(512, 0)
+        gates(512, 1)
+        round_wo_pass(0, 2)
+        quantize_h(GROUPS[0], [0])
+        messages(0, 1)
+        products(512, 1)
+        gates(768, 0)
+        round_wo_pass(1, 4)
+        messages(256, 1)
+        quantize_wo(0)
+        gates(768, 1)
+        for c in range(2):
+            open_y(GROUPS[0], [c])
+            add_to_y(GROUPS[0], [c], 0)
+        messages(512, 1)
+        quantize_h(GROUPS[0], [1])
+        products(768, 0)
+        quantize_wo(1)
+        for c in range(2):
+            add_to_y(GROUPS[0], [c], 1)
+            store_y(GROUPS[0], [c])
+        products(768, 1)
+        quantize_h(GROUPS[1], [0, 1])
+        for c in range(2, 4):
+            whole_y(GROUPS[0], [c], "ring")
+        message(768, 0, 0)
         tail = GROUPS[3]
         tail_banks = ([0, 1], [2, 3])
         message(768, 1, 0)
         message(768, 0, 1)
+        whole_y(GROUPS[1], [0, 1])
+        whole_y(GROUPS[1], [2, 3])
         quantize_h(GROUPS[2], [0, 1])
         whole_y(GROUPS[2], [0, 1, 2, 3])
         message(768, 1, 1)
         quantize_h(tail, [0])
         for cs in tail_banks:
-            open_y(tail, cs, "g_bank")
+            open_y(tail, cs, "ring")
             add_to_y(tail, cs, 0)
         quantize_h(tail, [1])
         for cs in tail_banks:

@@ -22,7 +22,7 @@ HALF = 512
 PAIR = 256
 TOK = 128
 IJ, IK, JK = 0, 1, 2
-GROUPS = [(0, 512), (512, 256), (768, 128), (896, 128)]
+GROUPS = [(0, 256), (256, 256), (512, 256), (768, 128), (896, 128)]
 
 
 def tile_list_triangle_edge_update_kernel(
@@ -36,7 +36,7 @@ def tile_list_triangle_edge_update_kernel(
         reuse = ctx.enter_context(tc.tile_pool(name="reuse", bufs=1))
         psum = ctx.enter_context(tc.psum_pool(name="psum", bufs=1))
         banks = [psum.tile([P, 512], F32, name=f"bank{i}") for i in range(8)]
-        dealt = {"ring": [0, 1, 2, 3], "a": [4, 5], "y": [6, 7]}
+        dealt = {"ring": [0, 1, 2, 6, 7], "a": [3, 4, 5], "y": [6, 7]}
         turns = {"ring": 0, "a": 0, "y": 0}
 
         def next_bank(kind, rows):
@@ -52,7 +52,7 @@ def tile_list_triangle_edge_update_kernel(
         wr_s_rows = held.tile([P, N // 4], I32, name="wr_s_rows", align_bytes=64)
         wg_raw = reuse.tile([P, H // 2], I32, name="wg_raw", align_bytes=64, offset=0)
         wb_raw = reuse.tile([P, H], I32, name="wb_raw", align_bytes=64, offset=2 * H)
-        wb_s_raw = reuse.tile([P, H // 4], I32, name="wb_s_raw", align_bytes=64, offset=6 * H)
+        wb_s_raw = reuse.tile([P, H // 4], I32, name="wb_s_raw", align_bytes=64, offset=8 * H)
         wr_w = held.tile([P, 2 * N], U8, name="wr_w", align_bytes=64)
         bias = held.tile([P, N // P], F32, name="bias")
         wa_raw = [held.tile([P, 4, PASS], F32, name=f"wa_raw{b}") for b in range(2)]
@@ -120,13 +120,16 @@ def tile_list_triangle_edge_update_kernel(
                 src.rearrange("p (b g t e) -> p b t g e", b=2, t=4, g=16),
             )
 
-        wa_w = held.tile([P, H], U32, name="wa_w", align_bytes=64)
+        wa_w = {0: held.tile([P, PASS], U32, name="wa_w0", align_bytes=64)}
         wa_s = held.tile([P, H], U8, name="wa_s", align_bytes=64)
         wo_w = held.tile([P, 2 * N], U32, name="wo_w", align_bytes=64)
         wo_s = held.tile([P, 2 * N], U8, name="wo_s", align_bytes=64)
         wa_bf = {}
         wo_bf = {}
         STAGE = 16 * H
+        MESSAGES = 44 * H
+        WA_STAGE = 64 * H
+        gb_place = {(0, 0): WA_STAGE + 64, (512, 0): MESSAGES, (768, 0): MESSAGES + 16 * PAIR}
 
         def round_wa(b, place):
             wa_bf[b] = reuse.tile([P, 4, P, 4], BF16, name=f"wa_bf{b}", align_bytes=64, offset=STAGE + place * 2 * H)
@@ -135,6 +138,21 @@ def tile_list_triangle_edge_update_kernel(
                     wa_bf[b][:, t].rearrange("p (g e i) j -> p g e j i", e=2, i=4),
                     wa_raw[b][:].rearrange("p j (g t e i) -> p t g e j i", t=4, e=2, i=4)[:, t],
                 )
+
+        def round_wa_on_gpsimd(b):
+            wa_bf[b] = reuse.tile([P, 4, P, 4], BF16, name=f"wa_bf{b}", align_bytes=64, offset=WA_STAGE)
+            for t in range(4):
+                nc.gpsimd.tensor_scalar(
+                    wa_bf[b][:, t].rearrange("p (g e) j -> p g e j", e=8),
+                    wa_raw[b][:].rearrange("p j (g t e) -> p t g e j", t=4, e=8)[:, t],
+                    1.0, 0.0, ALU.mult, ALU.add,
+                )
+
+        def round_wo_on_gpsimd(b, c):
+            cols = slice(c * P, (c + 1) * P)
+            nc.gpsimd.tensor_scalar(
+                wo_bf[b][:, cols, :], wo_raw[b][:, :, cols].rearrange("p t n -> p n t"), 1.0, 0.0, ALU.mult, ALU.add
+            )
 
         def round_wo(b, c):
             cols = slice(c * P, (c + 1) * P)
@@ -148,7 +166,9 @@ def tile_list_triangle_edge_update_kernel(
 
         def quantize_wa(b):
             cols = slice(b * PASS, (b + 1) * PASS)
-            quantize(wa_w[:, cols], wa_s[:, cols], wa_bf[b][:].rearrange("p t m j -> p (t m j)"))
+            if b == 1:
+                wa_w[1] = reuse.tile([P, PASS], U32, name="wa_w1", align_bytes=64, offset=6 * H + 64)
+            quantize(wa_w[b][:], wa_s[:, cols], wa_bf[b][:].rearrange("p t m j -> p (t m j)"))
 
         def quantize_wo(b):
             cols = slice(b * N, (b + 1) * N)
@@ -183,10 +203,13 @@ def tile_list_triangle_edge_update_kernel(
                     wb_s[:, c0 : c0 + P], picked(JK, tok0, PAIR),
                 )
             if s == 0:
-                gb[tok0, b] = work.tile([P, 2, PAIR, 2], F32, name="gb", bufs=8)
+                if (tok0, b) in gb_place:
+                    gb[tok0, b] = reuse.tile([P, 2, PAIR, 2], F32, name=f"gb{tok0}", align_bytes=64, offset=gb_place[tok0, b])
+                else:
+                    gb[tok0, b] = work.tile([P, 2, PAIR, 2], F32, name="gb", bufs=5)
             if on_gpsimd:
                 place = len(b_outs)
-                b_out = reuse.tile([P, PAIR, 2], F32, name=f"b_out{place}", align_bytes=64, offset=STAGE + (place if place < 8 else place + 2) * 2 * H)
+                b_out = reuse.tile([P, PAIR, 2], F32, name=f"b_out{place}", align_bytes=64, offset=STAGE + place * 2 * H)
                 b_outs.append(b_out)
                 nc.scalar.copy(b_out[:], bank.rearrange("p u n -> p n u"))
                 nc.gpsimd.tensor_tensor(gb[tok0, b][:, s], b_out[:], gate[tok0, b, s][:], ALU.mult)
@@ -199,7 +222,7 @@ def tile_list_triangle_edge_update_kernel(
         h_w = {}
         h_s = {}
         for tok0, ntok in GROUPS:
-            h_bf[tok0] = held.tile([P, 2, ntok, 4], BF16, name=f"h_bf{tok0}", align_bytes=64)
+            h_bf[tok0] = reuse.tile([P, 2, ntok, 4], BF16, name=f"h_bf{tok0}", align_bytes=64, offset=MESSAGES + 16 * tok0)
             h_w[tok0] = held.tile([P, 2 * ntok], U32, name=f"h_w{tok0}", align_bytes=64)
             h_s[tok0] = held.tile([P, 2 * ntok], U8, name=f"h_s{tok0}", align_bytes=64)
 
@@ -208,7 +231,7 @@ def tile_list_triangle_edge_update_kernel(
             bank = next_bank("a", 4)
             for t in range(4):
                 c0 = b * PASS + t * P
-                lone_pass(bank[:, t, :], wa_w[:, c0 : c0 + P].bitcast(FP8X4), wa_s[:, c0 : c0 + P], picked(IK, tok, TOK))
+                lone_pass(bank[:, t, :], wa_w[b][:, t * P : (t + 1) * P].bitcast(FP8X4), wa_s[:, c0 : c0 + P], picked(IK, tok, TOK))
             first = max(g0 for g0, ntok in GROUPS if g0 <= tok)
             nc.vector.tensor_tensor(
                 h_bf[first][:, b, tok - first : tok - first + TOK, :].rearrange("p n (s u) -> p n s u", s=2),
@@ -281,12 +304,15 @@ def tile_list_triangle_edge_update_kernel(
         third_w = reuse.tile([P, HALF], U32, name="third_w", align_bytes=64, offset=2 * H)
         gather_words(IK, 0, third_w[:])
         deal_columns(gb_s[:, H // 4 :], wb_s_raw[:])
-        late_s = reuse.tile([P, HALF], U8, name="late_s", align_bytes=64, offset=6 * H)
-        late_w = reuse.tile([P, 3 * HALF], U32, name="late_w", align_bytes=64, offset=6 * H + HALF)
+        late_s = reuse.tile([P, HALF], U8, name="late_s", align_bytes=64, offset=8 * H + 64)
+        late_w = reuse.tile([P, 2 * HALF], U32, name="late_w", align_bytes=64, offset=8 * H + 64 + HALF)
         gather_words(IJ, 1, late_w[:, 0:HALF])
         gather_words(JK, 1, late_w[:, HALF : 2 * HALF])
         gather_scales(IK, [1], late_s[:])
-        gather_words(IK, 1, late_w[:, 2 * HALF :])
+        round_wa_on_gpsimd(1)
+        quantize_wa(1)
+        last_w = reuse.tile([P, HALF], U32, name="last_w", align_bytes=64, offset=WA_STAGE + 64 - 4 * HALF)
+        gather_words(IK, 1, last_w[:])
 
         def gates(tok0, b):
             for s in range(2):
@@ -300,60 +326,75 @@ def tile_list_triangle_edge_update_kernel(
             for k in range(2):
                 message(tok0, b, k)
 
+        def round_wo_on_vector(b):
+            wo_bf[b] = held.tile([P, N, 4], BF16, name=f"wo_bf{b}", align_bytes=64)
+            nc.vector.tensor_copy(
+                wo_bf[b][:].rearrange("p (m i) t -> p m t i", i=4), wo_raw[b][:].rearrange("p t (m i) -> p m t i", i=4)
+            )
+
         def round_wo_pass(b, place):
             wo_bf[b] = reuse.tile([P, N, 4], BF16, name=f"wo_bf{b}", align_bytes=64, offset=STAGE + place * 2 * H)
             for c in range(4):
                 round_wo(b, c)
 
 
+        def open_quarter(q, kind="y"):
+            for cs in ([0, 1], [2, 3]):
+                open_y(GROUPS[q], cs, kind)
+
+        def close_y(group, cs):
+            for b in range(2):
+                add_to_y(group, cs, b)
+            store_y(group, cs)
+
+        def close_quarter(q):
+            for cs in ([0, 1], [2, 3]):
+                close_y(GROUPS[q], cs)
+
         gates(0, 0)
         gates(256, 0)
         gates(0, 1)
         products(0, 0, True)
         products(256, 0, True)
-        gates(512, 0)
-        round_wa(1, 0)
-        messages(0, 0)
-        products(512, 0)
-        products(0, 1, True)
         gates(256, 1)
-        products(256, 1, True)
-        messages(256, 0)
-        quantize_wa(1)
-        messages(512, 0)
-        gates(512, 1)
-        round_wo_pass(0, 2)
-        quantize_h(GROUPS[0], [0])
+        products(0, 1)
+        products(256, 1)
+        round_wo_pass(0, 10)
+        round_wo_pass(1, 12)
+        dealt["ring"] = [0, 1, 2]
+        messages(0, 0)
+        gates(512, 0)
         messages(0, 1)
-        products(512, 1)
-        gates(768, 0)
-        round_wo_pass(1, 4)
-        messages(256, 1)
+        open_quarter(0)
         quantize_wo(0)
-        gates(768, 1)
-        for c in range(2):
-            open_y(GROUPS[0], [c])
-            add_to_y(GROUPS[0], [c], 0)
-        messages(512, 1)
-        quantize_h(GROUPS[0], [1])
-        products(768, 0)
         quantize_wo(1)
-        for c in range(2):
-            add_to_y(GROUPS[0], [c], 1)
-            store_y(GROUPS[0], [c])
-        products(768, 1)
+        quantize_h(GROUPS[0], [0, 1])
+        products(512, 0, True)
+        messages(256, 0)
+        gates(512, 1)
+        messages(256, 1)
+        gates(768, 0)
+        close_quarter(0)
         quantize_h(GROUPS[1], [0, 1])
-        for c in range(2, 4):
-            whole_y(GROUPS[0], [c], "ring")
-        message(768, 0, 0)
-        tail = GROUPS[3]
-        tail_banks = ([0, 1], [2, 3])
-        message(768, 1, 0)
-        message(768, 0, 1)
-        whole_y(GROUPS[1], [0, 1])
-        whole_y(GROUPS[1], [2, 3])
+        products(768, 0, True)
+        products(512, 1)
+        gates(768, 1)
+        messages(512, 0)
+        open_quarter(1)
+        messages(512, 1)
+        close_quarter(1)
+        products(768, 1)
+        open_quarter(2, "ring")
         quantize_h(GROUPS[2], [0, 1])
-        whole_y(GROUPS[2], [0, 1, 2, 3])
+        tail = GROUPS[4]
+        tail_banks = ([0, 1], [2, 3])
+        message(768, 0, 0)
+        message(768, 1, 0)
+        close_quarter(2)
+        open_y(GROUPS[3], [0, 1, 2, 3])
+        message(768, 0, 1)
+        quantize_h(GROUPS[3], [0, 1])
+        close_y(GROUPS[3], [0, 1, 2, 3])
         message(768, 1, 1)
         quantize_h(tail, [0])
         for cs in tail_banks:

@@ -48,57 +48,69 @@ def tile_list_triangle_edge_update_kernel(
         lists = [held.tile([P, S // 16], U16, name=f"list{i}") for i in range(3)]
         tab_w = held.tile([P, T], I32, name="tab_w", align_bytes=64)
         tab_s = held.tile([P, T // 4], I32, name="tab_s", align_bytes=64)
-        wg_s_raw = held.tile([P, H // 4], I32, name="wg_s_raw", align_bytes=64)
-        wr_s_rows = held.tile([P, N // 4], I32, name="wr_s_rows", align_bytes=64)
-        wg_raw = reuse.tile([P, H // 2], I32, name="wg_raw", align_bytes=64, offset=0)
-        wb_raw = reuse.tile([P, H], I32, name="wb_raw", align_bytes=64, offset=2 * H)
-        wb_s_raw = reuse.tile([P, H // 4], I32, name="wb_s_raw", align_bytes=64, offset=8 * H)
+        raw_s = [held.tile([P, H // 4], I32, name=f"raw_s{i}", align_bytes=64) for i in range(2)]
+        dealt_s = held.tile([P, (2 * H + N) // 4], I32, name="dealt_s", align_bytes=64)
+        w_plane = held.tile([P, (2 * H + N) // 4], I32, name="w_plane", align_bytes=64)
+        planes = {IJ: held.tile([P, S // 4], I32, name="plane_ij", align_bytes=64), JK: held.tile([P, S // 2], I32, name="plane_jk_ik", align_bytes=64)}
+        wg_raw = held.tile([P, H // 2], I32, name="wg_raw")
+        wb_raw = reuse.tile([P, H], I32, name="wb_raw", align_bytes=64, offset=54 * H)
         wr_w = held.tile([P, 2 * N], U8, name="wr_w", align_bytes=64)
         bias = held.tile([P, N // P], F32, name="bias")
         wa_raw = [held.tile([P, 4, PASS], F32, name=f"wa_raw{b}") for b in range(2)]
         wo_raw = [held.tile([P, 4, N], F32, name=f"wo_raw{b}") for b in range(2)]
-
-        def load_scale_rows(dst, src):
-            for r in range(4):
-                nc.sync.dma_start(dst[r:P:32, :], src[0, r:16:4, :].bitcast(I32))
+        ROWS = slice(P - 16, P)
+        REST = slice(0, P - 16)
 
         def load_wa(b):
             nc.sync.dma_start(wa_raw[b][:], wa.rearrange("(p j) c -> p j c", j=4)[:, :, b * PASS : (b + 1) * PASS])
 
-        nc.vector.memset(tab_s[:], 0)
-        nc.vector.memset(wg_s_raw[:], 0)
-        nc.vector.memset(wb_s_raw[:], 0)
-        nc.vector.memset(wr_s_rows[:], 0)
+        def rows_to_plane(plane, rows):
+            for q in range(4):
+                nc.scalar.dma_start(plane[32 * q : 32 * q + 4, :], rows[P - 16 + 4 * q : P - 12 + 4 * q, :])
+
+        nc.scalar.dma_start(tab_s[ROWS, :], tab_scales[0].bitcast(I32))
+        nc.scalar.dma_start(raw_s[0][ROWS, :], wg_scales[0].bitcast(I32))
+        nc.scalar.dma_start(raw_s[1][ROWS, :], wb_scales[0].bitcast(I32))
+        nc.vector.memset(tab_s[REST, :], 0)
+        nc.vector.memset(planes[IJ][:], 0)
+        for i in range(2):
+            nc.vector.memset(raw_s[i][REST, :], 0)
         warm = held.tile([P, 2], F32, name="warm")
         nc.vector.memset(warm[:, 0:1], 0.0)
         nc.scalar.activation(warm[:, 1:2], warm[:, 0:1], ACT.Sigmoid)
-        for i, src in ((IJ, offs), (JK, offs3), (IK, offs2)):
-            nc.sync.dma_start(lists[i][:], src)
-        load_scale_rows(tab_s, tab_scales)
+        nc.vector.memset(w_plane[:], 0)
+        nc.vector.memset(planes[JK][:], 0)
+        nc.sync.dma_start(lists[IJ][:], offs)
+        nc.sync.dma_start(lists[IK][:], offs2)
+        nc.sync.dma_start(dealt_s[ROWS, H // 2 :], wr_scales[0].bitcast(I32))
         load_wa(0)
-        nc.sync.dma_start(tab_w[:], tab_words[0].rearrange("p t i -> p (t i)").bitcast(I32))
-        load_scale_rows(wg_s_raw, wg_scales)
+        nc.sync.dma_start(lists[JK][:], offs3)
         nc.sync.dma_start(wg_raw[:], wg_words[0].bitcast(I32))
+        nc.sync.dma_start(tab_w[:], tab_words[0].rearrange("p t i -> p (t i)").bitcast(I32))
         nc.sync.dma_start(wb_raw[:], wb_words[0].rearrange("p c i -> p (c i)").bitcast(I32))
         load_wa(1)
-        load_scale_rows(wb_s_raw, wb_scales)
         wo_rows = wo.rearrange("(b g t e) n -> b t g e n", b=2, t=4, e=8)
         for b in range(2):
             for t in range(4):
                 nc.sync.dma_start(wo_raw[b][:, t, :], wo_rows[b, t])
         nc.sync.dma_start(wr_w[:].bitcast(I32), wr_words[0].bitcast(I32))
-        load_scale_rows(wr_s_rows, wr_scales)
         with nc.allow_non_contiguous_dma(reason="one bias value a partition"):
             nc.sync.dma_start(bias[:], bo.rearrange("(c p) -> p c", p=P))
-        wr_s = wr_s_rows[:].bitcast(U8)
+        wg_s = w_plane[:].bitcast(U8)[:, 0:H]
+        wb_s = w_plane[:].bitcast(U8)[:, H : 2 * H]
+        wr_s = w_plane[:].bitcast(U8)[:, 2 * H :]
 
         v_w = {}
         v_s = {}
 
-        def gather_scales(i, halves, dst):
-            for h in halves:
-                v_s[i, h] = dst[:, (h - halves[0]) * HALF : (h - halves[0] + 1) * HALF]
-            nc.vector.tensor_copy(dst, tab_s[:].bitcast(U8).indirect(lists[i][:, 32 * halves[0] : 32 * halves[-1] + 32]))
+        picked_s = {
+            IJ: held.tile([P, S], U8, name="picked_ij", align_bytes=64),
+            JK: held.tile([P, 2 * S], U8, name="picked_jk_ik", align_bytes=64),
+        }
+
+        def pick_scales(i, first, n):
+            nc.vector.tensor_copy(picked_s[first][:, n * S : (n + 1) * S], tab_s[:].bitcast(U8).indirect(lists[i][:]))
+            v_s[i] = planes[first][:].bitcast(U8)[:, n * S : (n + 1) * S]
 
         def gather_words(i, h, dst):
             v_w[i, h] = dst
@@ -106,13 +118,13 @@ def tile_list_triangle_edge_update_kernel(
 
         def picked(i, tok0, ntok):
             h, lo = divmod(tok0, HALF)
-            return v_w[i, h][:, lo : lo + ntok].bitcast(FP8X4), v_s[i, h][:, lo : lo + ntok]
+            return v_w[i, h][:, lo : lo + ntok].bitcast(FP8X4), v_s[i][:, tok0 : tok0 + ntok]
 
+        STAGE = 0
+        MESSAGES = 28 * H
+        WA_STAGE = 44 * H
         wg_w = held.tile([P, H // 2], I32, name="wg_w", align_bytes=64)
         wb_w = held.tile([P, H], I32, name="wb_w", align_bytes=64)
-        gb_s = held.tile([P, H // 2], I32, name="gb_s", align_bytes=64)
-        wg_s = gb_s[:, 0 : H // 4].bitcast(U8)
-        wb_s = gb_s[:, H // 4 :].bitcast(U8)
 
         def deal_columns(dst, src):
             nc.vector.tensor_copy(
@@ -120,30 +132,24 @@ def tile_list_triangle_edge_update_kernel(
                 src.rearrange("p (b g t e) -> p b t g e", b=2, t=4, g=16),
             )
 
-        wa_w = {0: held.tile([P, PASS], U32, name="wa_w0", align_bytes=64)}
+        wa_bf = reuse.tile([P, 2, 4, P, 4], BF16, name="wa_bf", align_bytes=64, offset=WA_STAGE)
         wa_s = held.tile([P, H], U8, name="wa_s", align_bytes=64)
         wo_w = held.tile([P, 2 * N], U32, name="wo_w", align_bytes=64)
         wo_s = held.tile([P, 2 * N], U8, name="wo_s", align_bytes=64)
-        wa_bf = {}
         wo_bf = {}
-        STAGE = 16 * H
-        MESSAGES = 44 * H
-        WA_STAGE = 64 * H
-        gb_place = {(0, 0): WA_STAGE + 64, (512, 0): MESSAGES, (768, 0): MESSAGES + 16 * PAIR}
+        gb_place = {(0, 0): WA_STAGE, (256, 0): WA_STAGE + 4 * H, (512, 0): MESSAGES, (768, 0): MESSAGES + 16 * PAIR}
 
-        def round_wa(b, place):
-            wa_bf[b] = reuse.tile([P, 4, P, 4], BF16, name=f"wa_bf{b}", align_bytes=64, offset=STAGE + place * 2 * H)
+        def round_wa(b):
             for t in range(4):
                 nc.scalar.copy(
-                    wa_bf[b][:, t].rearrange("p (g e i) j -> p g e j i", e=2, i=4),
+                    wa_bf[:, b, t].rearrange("p (g e i) j -> p g e j i", e=2, i=4),
                     wa_raw[b][:].rearrange("p j (g t e i) -> p t g e j i", t=4, e=2, i=4)[:, t],
                 )
 
         def round_wa_on_gpsimd(b):
-            wa_bf[b] = reuse.tile([P, 4, P, 4], BF16, name=f"wa_bf{b}", align_bytes=64, offset=WA_STAGE)
             for t in range(4):
                 nc.gpsimd.tensor_scalar(
-                    wa_bf[b][:, t].rearrange("p (g e) j -> p g e j", e=8),
+                    wa_bf[:, b, t].rearrange("p (g e) j -> p g e j", e=8),
                     wa_raw[b][:].rearrange("p j (g t e) -> p t g e j", t=4, e=8)[:, t],
                     1.0, 0.0, ALU.mult, ALU.add,
                 )
@@ -163,12 +169,6 @@ def tile_list_triangle_edge_update_kernel(
 
         def quantize(codes, scales, values):
             nc.vector.quantize_mx(out=codes.bitcast(FP8X4), scales=scales, in_=values)
-
-        def quantize_wa(b):
-            cols = slice(b * PASS, (b + 1) * PASS)
-            if b == 1:
-                wa_w[1] = reuse.tile([P, PASS], U32, name="wa_w1", align_bytes=64, offset=6 * H + 64)
-            quantize(wa_w[b][:], wa_s[:, cols], wa_bf[b][:].rearrange("p t m j -> p (t m j)"))
 
         def quantize_wo(b):
             cols = slice(b * N, (b + 1) * N)
@@ -231,7 +231,7 @@ def tile_list_triangle_edge_update_kernel(
             bank = next_bank("a", 4)
             for t in range(4):
                 c0 = b * PASS + t * P
-                lone_pass(bank[:, t, :], wa_w[b][:, t * P : (t + 1) * P].bitcast(FP8X4), wa_s[:, c0 : c0 + P], picked(IK, tok, TOK))
+                lone_pass(bank[:, t, :], wa_w[:, c0 : c0 + P].bitcast(FP8X4), wa_s[:, c0 : c0 + P], picked(IK, tok, TOK))
             first = max(g0 for g0, ntok in GROUPS if g0 <= tok)
             nc.vector.tensor_tensor(
                 h_bf[first][:, b, tok - first : tok - first + TOK, :].rearrange("p n (s u) -> p n s u", s=2),
@@ -289,30 +289,26 @@ def tile_list_triangle_edge_update_kernel(
                 add_to_y(group, cs, b)
             store_y(group, cs)
 
-        for i, halves in ((IJ, [0, 1]), (JK, [0, 1]), (IK, [0])):
-            picked_s = held.tile([P, len(halves) * HALF], U8, name=f"picked_s{i}", align_bytes=64)
-            gather_scales(i, halves, picked_s[:])
-        round_wa(0, 8)
-        quantize_wa(0)
-        first_w = held.tile([P, HALF], U32, name="first_w", align_bytes=64)
-        gather_words(IJ, 0, first_w[:])
-        deal_columns(gb_s[:, 0 : H // 4], wg_s_raw[:])
+        pick_scales(IJ, IJ, 0)
+        rows_to_plane(planes[IJ], picked_s[IJ][:].bitcast(I32))
+        for i in range(2):
+            deal_columns(dealt_s[:, i * H // 4 : (i + 1) * H // 4], raw_s[i][:])
+        rows_to_plane(w_plane, dealt_s[:])
+        pick_scales(IK, JK, 1)
+        round_wa(0)
+        pick_scales(JK, JK, 0)
+        rows_to_plane(planes[JK], picked_s[JK][:].bitcast(I32))
         deal_columns(wg_w[:], wg_raw[:])
-        second_w = reuse.tile([P, HALF], U32, name="second_w", align_bytes=64, offset=0)
-        gather_words(JK, 0, second_w[:])
+        for i in (IJ, JK):
+            picked_w = held.tile([P, HALF], U32, name=f"picked_w{i}", align_bytes=64)
+            gather_words(i, 0, picked_w[:])
         deal_columns(wb_w[:], wb_raw[:])
-        third_w = reuse.tile([P, HALF], U32, name="third_w", align_bytes=64, offset=2 * H)
-        gather_words(IK, 0, third_w[:])
-        deal_columns(gb_s[:, H // 4 :], wb_s_raw[:])
-        late_s = reuse.tile([P, HALF], U8, name="late_s", align_bytes=64, offset=8 * H + 64)
-        late_w = reuse.tile([P, 2 * HALF], U32, name="late_w", align_bytes=64, offset=8 * H + 64 + HALF)
-        gather_words(IJ, 1, late_w[:, 0:HALF])
-        gather_words(JK, 1, late_w[:, HALF : 2 * HALF])
-        gather_scales(IK, [1], late_s[:])
+        late_w = reuse.tile([P, 4 * HALF], U32, name="late_w", align_bytes=64, offset=54 * H)
+        for n, (i, h) in enumerate(((IJ, 1), (IK, 0), (JK, 1), (IK, 1))):
+            gather_words(i, h, late_w[:, n * HALF : (n + 1) * HALF])
         round_wa_on_gpsimd(1)
-        quantize_wa(1)
-        last_w = reuse.tile([P, HALF], U32, name="last_w", align_bytes=64, offset=WA_STAGE + 64 - 4 * HALF)
-        gather_words(IK, 1, last_w[:])
+        wa_w = held.tile([P, H], U32, name="wa_w", align_bytes=64)
+        quantize(wa_w[:], wa_s[:], wa_bf[:].rearrange("p b t m j -> p (b t m j)"))
 
         def gates(tok0, b):
             for s in range(2):
@@ -351,9 +347,9 @@ def tile_list_triangle_edge_update_kernel(
             for cs in ([0, 1], [2, 3]):
                 close_y(GROUPS[q], cs)
 
+        gates(0, 1)
         gates(0, 0)
         gates(256, 0)
-        gates(0, 1)
         products(0, 0, True)
         products(256, 0, True)
         gates(256, 1)
@@ -362,28 +358,28 @@ def tile_list_triangle_edge_update_kernel(
         round_wo_pass(0, 10)
         round_wo_pass(1, 12)
         dealt["ring"] = [0, 1, 2]
-        messages(0, 0)
-        gates(512, 0)
         messages(0, 1)
-        open_quarter(0)
+        gates(512, 0)
+        messages(0, 0)
+        messages(256, 1)
         quantize_wo(0)
         quantize_wo(1)
         quantize_h(GROUPS[0], [0, 1])
         products(512, 0, True)
-        messages(256, 0)
         gates(512, 1)
-        messages(256, 1)
+        messages(256, 0)
         gates(768, 0)
-        close_quarter(0)
+        products(512, 1)
         quantize_h(GROUPS[1], [0, 1])
         products(768, 0, True)
-        products(512, 1)
         gates(768, 1)
-        messages(512, 0)
-        open_quarter(1)
         messages(512, 1)
-        close_quarter(1)
+        messages(512, 0)
         products(768, 1)
+        open_quarter(0)
+        close_quarter(0)
+        open_quarter(1)
+        close_quarter(1)
         open_quarter(2, "ring")
         quantize_h(GROUPS[2], [0, 1])
         tail = GROUPS[4]

@@ -22,7 +22,8 @@ HALF = 512
 PAIR = 256
 TOK = 128
 IJ, IK, JK = 0, 1, 2
-GROUPS = [(0, 256), (256, 256), (512, 256), (768, 128), (896, 128)]
+RING_FROM = 1024
+GROUPS = [(0, 512), (512, 256), (768, 128), (896, 128)]
 
 
 def tile_list_triangle_edge_update_kernel(
@@ -126,18 +127,18 @@ def tile_list_triangle_edge_update_kernel(
         wg_w = held.tile([P, H // 2], I32, name="wg_w", align_bytes=64)
         wb_w = held.tile([P, H], I32, name="wb_w", align_bytes=64)
 
-        def deal_columns(dst, src):
-            nc.vector.tensor_copy(
+        def deal_columns(dst, src, engine=nc.vector):
+            engine.tensor_copy(
                 dst.rearrange("p (b t g e) -> p b t g e", b=2, t=4, g=16),
                 src.rearrange("p (b g t e) -> p b t g e", b=2, t=4, g=16),
             )
 
         wa_bf = reuse.tile([P, 2, 4, P, 4], BF16, name="wa_bf", align_bytes=64, offset=WA_STAGE)
         wa_s = held.tile([P, H], U8, name="wa_s", align_bytes=64)
-        wo_w = held.tile([P, 2 * N], U32, name="wo_w", align_bytes=64)
+        wo_w = {}
         wo_s = held.tile([P, 2 * N], U8, name="wo_s", align_bytes=64)
         wo_bf = {}
-        gb_place = {(0, 0): WA_STAGE, (256, 0): WA_STAGE + 4 * H, (512, 0): MESSAGES, (768, 0): MESSAGES + 16 * PAIR}
+        gb_place = {(0, 1): WA_STAGE, (256, 1): WA_STAGE + 4 * H, (512, 1): MESSAGES, (768, 1): MESSAGES + 4 * H}
 
         def round_wa(b):
             for t in range(4):
@@ -172,7 +173,9 @@ def tile_list_triangle_edge_update_kernel(
 
         def quantize_wo(b):
             cols = slice(b * N, (b + 1) * N)
-            quantize(wo_w[:, cols], wo_s[:, cols], wo_bf[b][:].rearrange("p n t -> p (n t)"))
+            if b == 0:
+                wo_w[0] = reuse.tile([P, 2 * N], U32, name="wo_w", align_bytes=64, offset=STAGE + 6 * H)
+            quantize(wo_w[0][:, cols], wo_s[:, cols], wo_bf[b][:].rearrange("p n t -> p (n t)"))
 
         def lone_pass(dst, codes, scales, rhs):
             nc.tensor.matmul_mx(
@@ -195,7 +198,7 @@ def tile_list_triangle_edge_update_kernel(
             nc.scalar.activation(gate[tok0, b, s][:], bank.rearrange("p u n -> p n u"), ACT.Sigmoid)
 
         def gate_times_b(tok0, b, s, on_gpsimd=False):
-            bank = next_bank("ring", 2)
+            bank = next_bank("ring" if on_gpsimd or tok0 >= RING_FROM else "a", 2)
             for u in range(2):
                 c0 = b * PASS + (2 * s + u) * P
                 lone_pass(
@@ -209,7 +212,7 @@ def tile_list_triangle_edge_update_kernel(
                     gb[tok0, b] = work.tile([P, 2, PAIR, 2], F32, name="gb", bufs=5)
             if on_gpsimd:
                 place = len(b_outs)
-                b_out = reuse.tile([P, PAIR, 2], F32, name=f"b_out{place}", align_bytes=64, offset=STAGE + place * 2 * H)
+                b_out = reuse.tile([P, PAIR, 2], F32, name=f"b_out{place}", align_bytes=64, offset=STAGE + (place + place // 4) * 2 * H)
                 b_outs.append(b_out)
                 nc.scalar.copy(b_out[:], bank.rearrange("p u n -> p n u"))
                 nc.gpsimd.tensor_tensor(gb[tok0, b][:, s], b_out[:], gate[tok0, b, s][:], ALU.mult)
@@ -266,7 +269,7 @@ def tile_list_triangle_edge_update_kernel(
             for c in cs:
                 cols = slice(b * N + c * P, b * N + (c + 1) * P)
                 nc.tensor.matmul_mx(
-                    out=y_bank[tok0, cs[0]][:, c - cs[0], :], lhsT=wo_w[:, cols].bitcast(FP8X4), lhsT_scale=wo_s[:, cols],
+                    out=y_bank[tok0, cs[0]][:, c - cs[0], :], lhsT=wo_w[0][:, cols].bitcast(FP8X4), lhsT_scale=wo_s[:, cols],
                     rhs=h_w[tok0][:, b * ntok : (b + 1) * ntok].bitcast(FP8X4), rhs_scale=h_s[tok0][:, b * ntok : (b + 1) * ntok],
                     start=False, stop=(b == 1 and c == cs[-1]),
                 )
@@ -298,7 +301,7 @@ def tile_list_triangle_edge_update_kernel(
         round_wa(0)
         pick_scales(JK, JK, 0)
         rows_to_plane(planes[JK], picked_s[JK][:].bitcast(I32))
-        deal_columns(wg_w[:], wg_raw[:])
+        deal_columns(wg_w[:], wg_raw[:], nc.gpsimd)
         for i in (IJ, JK):
             picked_w = held.tile([P, HALF], U32, name=f"picked_w{i}", align_bytes=64)
             gather_words(i, 0, picked_w[:])
@@ -308,7 +311,6 @@ def tile_list_triangle_edge_update_kernel(
             gather_words(i, h, late_w[:, n * HALF : (n + 1) * HALF])
         round_wa_on_gpsimd(1)
         wa_w = held.tile([P, H], U32, name="wa_w", align_bytes=64)
-        quantize(wa_w[:], wa_s[:], wa_bf[:].rearrange("p b t m j -> p (b t m j)"))
 
         def gates(tok0, b):
             for s in range(2):
@@ -347,52 +349,50 @@ def tile_list_triangle_edge_update_kernel(
             for cs in ([0, 1], [2, 3]):
                 close_y(GROUPS[q], cs)
 
-        gates(0, 1)
         gates(0, 0)
         gates(256, 0)
-        products(0, 0, True)
-        products(256, 0, True)
+        gates(0, 1)
+        products(0, 0)
+        quantize(wa_w[:], wa_s[:], wa_bf[:].rearrange("p b t m j -> p (b t m j)"))
+        products(0, 1, True)
         gates(256, 1)
-        products(0, 1)
-        products(256, 1)
+        products(256, 1, True)
+        products(256, 0)
         round_wo_pass(0, 10)
-        round_wo_pass(1, 12)
         dealt["ring"] = [0, 1, 2]
-        messages(0, 1)
         gates(512, 0)
+        round_wo_pass(1, 12)
         messages(0, 0)
+        messages(256, 0)
+        messages(0, 1)
+        products(512, 0)
+        gates(512, 1)
         messages(256, 1)
         quantize_wo(0)
         quantize_wo(1)
         quantize_h(GROUPS[0], [0, 1])
-        products(512, 0, True)
-        gates(512, 1)
-        messages(256, 0)
+        products(512, 1, True)
         gates(768, 0)
-        products(512, 1)
-        quantize_h(GROUPS[1], [0, 1])
-        products(768, 0, True)
         gates(768, 1)
-        messages(512, 1)
+        products(768, 1, True)
         messages(512, 0)
-        products(768, 1)
-        open_quarter(0)
-        close_quarter(0)
-        open_quarter(1)
-        close_quarter(1)
-        open_quarter(2, "ring")
-        quantize_h(GROUPS[2], [0, 1])
-        tail = GROUPS[4]
+        products(768, 0)
+        messages(512, 1)
+        for c in range(4):
+            whole_y(GROUPS[0], [c])
+        open_quarter(1, "ring")
+        tail = GROUPS[3]
         tail_banks = ([0, 1], [2, 3])
         message(768, 0, 0)
-        message(768, 1, 0)
-        close_quarter(2)
-        open_y(GROUPS[3], [0, 1, 2, 3])
         message(768, 0, 1)
-        quantize_h(GROUPS[3], [0, 1])
-        close_y(GROUPS[3], [0, 1, 2, 3])
-        message(768, 1, 1)
+        quantize_h(GROUPS[1], [0, 1])
+        message(768, 1, 0)
+        close_quarter(1)
         quantize_h(tail, [0])
+        open_y(GROUPS[2], [0, 1, 2, 3])
+        quantize_h(GROUPS[2], [0, 1])
+        message(768, 1, 1)
+        close_y(GROUPS[2], [0, 1, 2, 3])
         for cs in tail_banks:
             open_y(tail, cs, "ring")
             add_to_y(tail, cs, 0)

@@ -37,7 +37,7 @@ def tile_list_triangle_edge_update_kernel(
         reuse = ctx.enter_context(tc.tile_pool(name="reuse", bufs=1))
         psum = ctx.enter_context(tc.psum_pool(name="psum", bufs=1))
         banks = [psum.tile([P, 512], F32, name=f"bank{i}") for i in range(8)]
-        dealt = {"ring": [0, 1, 2, 6, 7], "a": [3, 4, 5], "y": [6, 7]}
+        dealt = {"ring": [0, 1, 2, 6], "a": [3, 4, 5, 7], "y": [6, 7]}
         turns = {"ring": 0, "a": 0, "y": 0}
 
         def next_bank(kind, rows):
@@ -49,12 +49,11 @@ def tile_list_triangle_edge_update_kernel(
         lists = [held.tile([P, S // 16], U16, name=f"list{i}") for i in range(3)]
         tab_w = held.tile([P, T], I32, name="tab_w", align_bytes=64)
         tab_s = held.tile([P, T // 4], I32, name="tab_s", align_bytes=64)
-        raw_s = [held.tile([P, H // 4], I32, name=f"raw_s{i}", align_bytes=64) for i in range(2)]
-        dealt_s = held.tile([P, (2 * H + N) // 4], I32, name="dealt_s", align_bytes=64)
-        w_plane = held.tile([P, (2 * H + N) // 4], I32, name="w_plane", align_bytes=64)
-        planes = {IJ: held.tile([P, S // 4], I32, name="plane_ij", align_bytes=64), JK: held.tile([P, S // 2], I32, name="plane_jk_ik", align_bytes=64)}
+        raw_s = [reuse.tile([P, H // 4], I32, name=f"raw_s{i}", align_bytes=64, offset=(62 + 2 * i) * H) for i in range(2)]
+        dealt_s = held.tile([P, H // 2], I32, name="dealt_s", align_bytes=64)
+        w_plane = held.tile([P, H // 2], I32, name="w_plane", align_bytes=64)
         wg_raw = held.tile([P, H // 2], I32, name="wg_raw")
-        wb_raw = reuse.tile([P, H], I32, name="wb_raw", align_bytes=64, offset=54 * H)
+        wb_raw = reuse.tile([P, H], I32, name="wb_raw", align_bytes=64, offset=52 * H)
         wr_w = held.tile([P, 2 * N], U8, name="wr_w", align_bytes=64)
         bias = held.tile([P, N // P], F32, name="bias")
         wa_raw = [held.tile([P, 4, PASS], F32, name=f"wa_raw{b}") for b in range(2)]
@@ -65,41 +64,27 @@ def tile_list_triangle_edge_update_kernel(
         def load_wa(b):
             nc.sync.dma_start(wa_raw[b][:], wa.rearrange("(p j) c -> p j c", j=4)[:, :, b * PASS : (b + 1) * PASS])
 
-        def rows_to_plane(plane, rows):
+        def rows_to_plane(plane, rows, queue):
             for q in range(4):
-                nc.scalar.dma_start(plane[32 * q : 32 * q + 4, :], rows[P - 16 + 4 * q : P - 12 + 4 * q, :])
+                queue.dma_start(plane[32 * q : 32 * q + 4, :], rows[P - 16 + 4 * q : P - 12 + 4 * q, :])
 
-        nc.scalar.dma_start(tab_s[ROWS, :], tab_scales[0].bitcast(I32))
         nc.scalar.dma_start(raw_s[0][ROWS, :], wg_scales[0].bitcast(I32))
         nc.scalar.dma_start(raw_s[1][ROWS, :], wb_scales[0].bitcast(I32))
-        nc.vector.memset(tab_s[REST, :], 0)
-        nc.vector.memset(planes[IJ][:], 0)
+        nc.scalar.dma_start(tab_s[ROWS, :], tab_scales[0].bitcast(I32))
         for i in range(2):
             nc.vector.memset(raw_s[i][REST, :], 0)
+        nc.vector.memset(tab_s[REST, :], 0)
         warm = held.tile([P, 2], F32, name="warm")
         nc.vector.memset(warm[:, 0:1], 0.0)
         nc.scalar.activation(warm[:, 1:2], warm[:, 0:1], ACT.Sigmoid)
         nc.vector.memset(w_plane[:], 0)
-        nc.vector.memset(planes[JK][:], 0)
         nc.sync.dma_start(lists[IJ][:], offs)
         nc.sync.dma_start(lists[IK][:], offs2)
-        nc.sync.dma_start(dealt_s[ROWS, H // 2 :], wr_scales[0].bitcast(I32))
-        load_wa(0)
         nc.sync.dma_start(lists[JK][:], offs3)
+        load_wa(0)
         nc.sync.dma_start(wg_raw[:], wg_words[0].bitcast(I32))
-        nc.sync.dma_start(tab_w[:], tab_words[0].rearrange("p t i -> p (t i)").bitcast(I32))
-        nc.sync.dma_start(wb_raw[:], wb_words[0].rearrange("p c i -> p (c i)").bitcast(I32))
-        load_wa(1)
-        wo_rows = wo.rearrange("(b g t e) n -> b t g e n", b=2, t=4, e=8)
-        for b in range(2):
-            for t in range(4):
-                nc.sync.dma_start(wo_raw[b][:, t, :], wo_rows[b, t])
-        nc.sync.dma_start(wr_w[:].bitcast(I32), wr_words[0].bitcast(I32))
-        with nc.allow_non_contiguous_dma(reason="one bias value a partition"):
-            nc.sync.dma_start(bias[:], bo.rearrange("(c p) -> p c", p=P))
         wg_s = w_plane[:].bitcast(U8)[:, 0:H]
         wb_s = w_plane[:].bitcast(U8)[:, H : 2 * H]
-        wr_s = w_plane[:].bitcast(U8)[:, 2 * H :]
 
         v_w = {}
         v_s = {}
@@ -292,21 +277,41 @@ def tile_list_triangle_edge_update_kernel(
                 add_to_y(group, cs, b)
             store_y(group, cs)
 
-        pick_scales(IJ, IJ, 0)
-        rows_to_plane(planes[IJ], picked_s[IJ][:].bitcast(I32))
         for i in range(2):
             deal_columns(dealt_s[:, i * H // 4 : (i + 1) * H // 4], raw_s[i][:])
-        rows_to_plane(w_plane, dealt_s[:])
-        pick_scales(IK, JK, 1)
+        rows_to_plane(w_plane, dealt_s[:], nc.sync)
+        nc.sync.dma_start(tab_w[:], tab_words[0].rearrange("p t i -> p (t i)").bitcast(I32))
+        planes = {
+            IJ: reuse.tile([P, S // 4], I32, name="plane_ij", align_bytes=64, offset=61 * H + 64),
+            JK: reuse.tile([P, S // 2], I32, name="plane_jk_ik", align_bytes=64, offset=62 * H + 64),
+        }
+        wr_plane = reuse.tile([P, N // 4], I32, name="wr_plane", align_bytes=64, offset=64 * H + 64)
+        for plane in (planes[IJ], planes[JK], wr_plane):
+            nc.gpsimd.memset(plane[:], 0)
+        wr_s = wr_plane[:].bitcast(U8)
+        pick_scales(IJ, IJ, 0)
+        rows_to_plane(planes[IJ], picked_s[IJ][:].bitcast(I32), nc.sync)
+        nc.sync.dma_start(wb_raw[:], wb_words[0].rearrange("p c i -> p (c i)").bitcast(I32))
+        load_wa(1)
         round_wa(0)
+        pick_scales(IK, JK, 1)
         pick_scales(JK, JK, 0)
-        rows_to_plane(planes[JK], picked_s[JK][:].bitcast(I32))
+        rows_to_plane(planes[JK], picked_s[JK][:].bitcast(I32), nc.sync)
+        wo_rows = wo.rearrange("(b g t e) n -> b t g e n", b=2, t=4, e=8)
+        for b in range(2):
+            for t in range(4):
+                nc.sync.dma_start(wo_raw[b][:, t, :], wo_rows[b, t])
+        nc.sync.dma_start(wr_w[:].bitcast(I32), wr_words[0].bitcast(I32))
+        for r in range(4):
+            nc.sync.dma_start(wr_plane[r:P:32, :], wr_scales[0, r:16:4, :].bitcast(I32))
+        with nc.allow_non_contiguous_dma(reason="one bias value a partition"):
+            nc.sync.dma_start(bias[:], bo.rearrange("(c p) -> p c", p=P))
         deal_columns(wg_w[:], wg_raw[:], nc.gpsimd)
         for i in (IJ, JK):
             picked_w = held.tile([P, HALF], U32, name=f"picked_w{i}", align_bytes=64)
             gather_words(i, 0, picked_w[:])
         deal_columns(wb_w[:], wb_raw[:])
-        late_w = reuse.tile([P, 4 * HALF], U32, name="late_w", align_bytes=64, offset=54 * H)
+        late_w = reuse.tile([P, 4 * HALF], U32, name="late_w", align_bytes=64, offset=52 * H)
         for n, (i, h) in enumerate(((IJ, 1), (IK, 0), (JK, 1), (IK, 1))):
             gather_words(i, h, late_w[:, n * HALF : (n + 1) * HALF])
         round_wa_on_gpsimd(1)
@@ -352,10 +357,10 @@ def tile_list_triangle_edge_update_kernel(
         gates(0, 0)
         gates(256, 0)
         gates(0, 1)
-        products(0, 0)
-        quantize(wa_w[:], wa_s[:], wa_bf[:].rearrange("p b t m j -> p (b t m j)"))
-        products(0, 1, True)
         gates(256, 1)
+        quantize(wa_w[:], wa_s[:], wa_bf[:].rearrange("p b t m j -> p (b t m j)"))
+        products(0, 0)
+        products(0, 1, True)
         products(256, 1, True)
         products(256, 0)
         round_wo_pass(0, 10)
@@ -364,33 +369,36 @@ def tile_list_triangle_edge_update_kernel(
         round_wo_pass(1, 12)
         messages(0, 0)
         messages(256, 0)
+        dealt["a"] = [3, 4, 5]
+        turns["a"] = 0
         messages(0, 1)
-        products(512, 0)
         gates(512, 1)
         messages(256, 1)
         quantize_wo(0)
+        quantize_h(GROUPS[0], [0])
         quantize_wo(1)
-        quantize_h(GROUPS[0], [0, 1])
+        quantize_h(GROUPS[0], [1])
         products(512, 1, True)
+        products(512, 0)
         gates(768, 0)
         gates(768, 1)
         products(768, 1, True)
         messages(512, 0)
         products(768, 0)
         messages(512, 1)
+        message(768, 0, 0)
         for c in range(4):
             whole_y(GROUPS[0], [c])
         open_quarter(1, "ring")
         tail = GROUPS[3]
         tail_banks = ([0, 1], [2, 3])
-        message(768, 0, 0)
-        message(768, 0, 1)
         quantize_h(GROUPS[1], [0, 1])
         message(768, 1, 0)
+        message(768, 0, 1)
         close_quarter(1)
-        quantize_h(tail, [0])
         open_y(GROUPS[2], [0, 1, 2, 3])
         quantize_h(GROUPS[2], [0, 1])
+        quantize_h(tail, [0])
         message(768, 1, 1)
         close_y(GROUPS[2], [0, 1, 2, 3])
         for cs in tail_banks:

@@ -37,7 +37,7 @@ def tile_list_triangle_edge_update_kernel(
         reuse = ctx.enter_context(tc.tile_pool(name="reuse", bufs=1))
         psum = ctx.enter_context(tc.psum_pool(name="psum", bufs=1))
         banks = [psum.tile([P, 512], F32, name=f"bank{i}") for i in range(8)]
-        dealt = {"ring": [0, 1, 2, 6], "a": [3, 4, 5, 7], "y": [6, 7]}
+        dealt = {"ring": [0, 1, 2, 6], "a": [3, 4, 5, 7], "y": [7, 2, 6, 0, 1]}
         turns = {"ring": 0, "a": 0, "y": 0}
 
         def next_bank(kind, rows):
@@ -118,24 +118,25 @@ def tile_list_triangle_edge_update_kernel(
                 src.rearrange("p (b g t e) -> p b t g e", b=2, t=4, g=16),
             )
 
-        wa_bf = reuse.tile([P, 2, 4, P, 4], BF16, name="wa_bf", align_bytes=64, offset=WA_STAGE)
+        wa_bf = [held.tile([P, 4, P, 4], BF16, name="wa_bf0", align_bytes=64), reuse.tile([P, 4, P, 4], BF16, name="wa_bf1", align_bytes=64, offset=WA_STAGE)]
         wa_s = held.tile([P, H], U8, name="wa_s", align_bytes=64)
         wo_w = {}
         wo_s = held.tile([P, 2 * N], U8, name="wo_s", align_bytes=64)
         wo_bf = {}
-        gb_place = {(0, 1): WA_STAGE, (256, 1): WA_STAGE + 4 * H, (512, 1): MESSAGES, (768, 1): MESSAGES + 4 * H}
+        gb_place = {(256, 1): WA_STAGE, (768, 1): MESSAGES}
+        B_PLACES = [0, 4, 6, 8, 10, 14, 18, 48]
 
         def round_wa(b):
             for t in range(4):
                 nc.scalar.copy(
-                    wa_bf[:, b, t].rearrange("p (g e i) j -> p g e j i", e=2, i=4),
+                    wa_bf[b][:, t].rearrange("p (g e i) j -> p g e j i", e=2, i=4),
                     wa_raw[b][:].rearrange("p j (g t e i) -> p t g e j i", t=4, e=2, i=4)[:, t],
                 )
 
         def round_wa_on_gpsimd(b):
             for t in range(4):
                 nc.gpsimd.tensor_scalar(
-                    wa_bf[:, b, t].rearrange("p (g e) j -> p g e j", e=8),
+                    wa_bf[b][:, t].rearrange("p (g e) j -> p g e j", e=8),
                     wa_raw[b][:].rearrange("p j (g t e) -> p t g e j", t=4, e=8)[:, t],
                     1.0, 0.0, ALU.mult, ALU.add,
                 )
@@ -156,11 +157,16 @@ def tile_list_triangle_edge_update_kernel(
         def quantize(codes, scales, values):
             nc.vector.quantize_mx(out=codes.bitcast(FP8X4), scales=scales, in_=values)
 
-        def quantize_wo(b):
+        wa_w = {}
+
+        def quantize_wa(b, offset):
+            wa_w[b] = reuse.tile([P, PASS], U32, name=f"wa_w{b}", align_bytes=64, offset=offset)
+            quantize(wa_w[b][:], wa_s[:, b * PASS : (b + 1) * PASS], wa_bf[b][:].rearrange("p t m j -> p (t m j)"))
+
+        def quantize_wo(b, offset):
             cols = slice(b * N, (b + 1) * N)
-            if b == 0:
-                wo_w[0] = reuse.tile([P, 2 * N], U32, name="wo_w", align_bytes=64, offset=STAGE + 6 * H)
-            quantize(wo_w[0][:, cols], wo_s[:, cols], wo_bf[b][:].rearrange("p n t -> p (n t)"))
+            wo_w[b] = reuse.tile([P, N], U32, name=f"wo_w{b}", align_bytes=64, offset=offset)
+            quantize(wo_w[b][:], wo_s[:, cols], wo_bf[b][:].rearrange("p n t -> p (n t)"))
 
         def lone_pass(dst, codes, scales, rhs):
             nc.tensor.matmul_mx(
@@ -194,10 +200,10 @@ def tile_list_triangle_edge_update_kernel(
                 if (tok0, b) in gb_place:
                     gb[tok0, b] = reuse.tile([P, 2, PAIR, 2], F32, name=f"gb{tok0}", align_bytes=64, offset=gb_place[tok0, b])
                 else:
-                    gb[tok0, b] = work.tile([P, 2, PAIR, 2], F32, name="gb", bufs=5)
+                    gb[tok0, b] = work.tile([P, 2, PAIR, 2], F32, name="gb", bufs=7)
             if on_gpsimd:
                 place = len(b_outs)
-                b_out = reuse.tile([P, PAIR, 2], F32, name=f"b_out{place}", align_bytes=64, offset=STAGE + (place + place // 4) * 2 * H)
+                b_out = reuse.tile([P, PAIR, 2], F32, name=f"b_out{place}", align_bytes=64, offset=B_PLACES[place] * H)
                 b_outs.append(b_out)
                 nc.scalar.copy(b_out[:], bank.rearrange("p u n -> p n u"))
                 nc.gpsimd.tensor_tensor(gb[tok0, b][:, s], b_out[:], gate[tok0, b, s][:], ALU.mult)
@@ -219,7 +225,7 @@ def tile_list_triangle_edge_update_kernel(
             bank = next_bank("a", 4)
             for t in range(4):
                 c0 = b * PASS + t * P
-                lone_pass(bank[:, t, :], wa_w[:, c0 : c0 + P].bitcast(FP8X4), wa_s[:, c0 : c0 + P], picked(IK, tok, TOK))
+                lone_pass(bank[:, t, :], wa_w[b][:, t * P : (t + 1) * P].bitcast(FP8X4), wa_s[:, c0 : c0 + P], picked(IK, tok, TOK))
             first = max(g0 for g0, ntok in GROUPS if g0 <= tok)
             nc.vector.tensor_tensor(
                 h_bf[first][:, b, tok - first : tok - first + TOK, :].rearrange("p n (s u) -> p n s u", s=2),
@@ -254,7 +260,7 @@ def tile_list_triangle_edge_update_kernel(
             for c in cs:
                 cols = slice(b * N + c * P, b * N + (c + 1) * P)
                 nc.tensor.matmul_mx(
-                    out=y_bank[tok0, cs[0]][:, c - cs[0], :], lhsT=wo_w[0][:, cols].bitcast(FP8X4), lhsT_scale=wo_s[:, cols],
+                    out=y_bank[tok0, cs[0]][:, c - cs[0], :], lhsT=wo_w[b][:, c * P : (c + 1) * P].bitcast(FP8X4), lhsT_scale=wo_s[:, cols],
                     rhs=h_w[tok0][:, b * ntok : (b + 1) * ntok].bitcast(FP8X4), rhs_scale=h_s[tok0][:, b * ntok : (b + 1) * ntok],
                     start=False, stop=(b == 1 and c == cs[-1]),
                 )
@@ -311,11 +317,11 @@ def tile_list_triangle_edge_update_kernel(
             picked_w = held.tile([P, HALF], U32, name=f"picked_w{i}", align_bytes=64)
             gather_words(i, 0, picked_w[:])
         deal_columns(wb_w[:], wb_raw[:])
-        late_w = reuse.tile([P, 4 * HALF], U32, name="late_w", align_bytes=64, offset=52 * H)
+        quantize_wa(0, 50 * H + 64)
+        late_w = reuse.tile([P, 4 * HALF], U32, name="late_w", align_bytes=64, offset=52 * H + 64)
         for n, (i, h) in enumerate(((IJ, 1), (IK, 0), (JK, 1), (IK, 1))):
             gather_words(i, h, late_w[:, n * HALF : (n + 1) * HALF])
         round_wa_on_gpsimd(1)
-        wa_w = held.tile([P, H], U32, name="wa_w", align_bytes=64)
 
         def gates(tok0, b):
             for s in range(2):
@@ -358,51 +364,50 @@ def tile_list_triangle_edge_update_kernel(
         gates(256, 0)
         gates(0, 1)
         gates(256, 1)
-        quantize(wa_w[:], wa_s[:], wa_bf[:].rearrange("p b t m j -> p (b t m j)"))
         products(0, 0)
         products(0, 1, True)
-        products(256, 1, True)
         products(256, 0)
+        quantize_wa(1, 2 * H + 64)
+        products(256, 1, True)
         round_wo_pass(0, 10)
-        dealt["ring"] = [0, 1, 2]
+        gates(512, 1)
+        products(512, 1, True)
         gates(512, 0)
         round_wo_pass(1, 12)
+        gates(768, 1)
+        gates(768, 0)
         messages(0, 0)
         messages(256, 0)
         dealt["a"] = [3, 4, 5]
         turns["a"] = 0
         messages(0, 1)
-        gates(512, 1)
         messages(256, 1)
-        quantize_wo(0)
-        quantize_h(GROUPS[0], [0])
-        quantize_wo(1)
-        quantize_h(GROUPS[0], [1])
-        products(512, 1, True)
         products(512, 0)
-        gates(768, 0)
-        gates(768, 1)
+        quantize_wo(0, 12 * H + 64)
+        quantize_h(GROUPS[0], [0])
+        quantize_wo(1, 14 * H + 64)
+        quantize_h(GROUPS[0], [1])
+        turns["ring"] = 2
         products(768, 1, True)
+        messages(512, 1)
         messages(512, 0)
         products(768, 0)
-        messages(512, 1)
-        message(768, 0, 0)
-        for c in range(4):
-            whole_y(GROUPS[0], [c])
-        open_quarter(1, "ring")
+        quantize_h(GROUPS[1], [0, 1])
         tail = GROUPS[3]
         tail_banks = ([0, 1], [2, 3])
-        quantize_h(GROUPS[1], [0, 1])
+        message(768, 0, 0)
         message(768, 1, 0)
         message(768, 0, 1)
+        for c in range(4):
+            whole_y(GROUPS[0], [c])
+        open_quarter(1)
         close_quarter(1)
-        open_y(GROUPS[2], [0, 1, 2, 3])
         quantize_h(GROUPS[2], [0, 1])
         quantize_h(tail, [0])
         message(768, 1, 1)
-        close_y(GROUPS[2], [0, 1, 2, 3])
+        whole_y(GROUPS[2], [0, 1, 2, 3])
         for cs in tail_banks:
-            open_y(tail, cs, "ring")
+            open_y(tail, cs)
             add_to_y(tail, cs, 0)
         quantize_h(tail, [1])
         for cs in tail_banks:

@@ -19,11 +19,12 @@ ALU = mybir.AluOpType
 P = 128
 PASS = 512
 HALF = 512
-PAIR = 256
+QUARTER = 256
 TOK = 128
 IJ, IK, JK = 0, 1, 2
-RING_FROM = 1024
-GROUPS = [(0, 512), (512, 256), (768, 128), (896, 128)]
+GROUPS = [(0, 256), (256, 256), (512, 256), (768, 128), (896, 128)]
+H_OVER = {256: "wo_bf1"}
+SIZE = {F32: 4, I32: 4, U32: 4, BF16: 2, U8: 1}
 
 
 def tile_list_triangle_edge_update_kernel(
@@ -33,218 +34,223 @@ def tile_list_triangle_edge_update_kernel(
     nc = tc.nc
     with ExitStack() as ctx:
         held = ctx.enter_context(tc.tile_pool(name="held", bufs=1))
-        work = ctx.enter_context(tc.tile_pool(name="work", bufs=16))
-        reuse = ctx.enter_context(tc.tile_pool(name="reuse", bufs=1))
+        shared = ctx.enter_context(tc.tile_pool(name="shared", bufs=1))
         psum = ctx.enter_context(tc.psum_pool(name="psum", bufs=1))
         banks = [psum.tile([P, 512], F32, name=f"bank{i}") for i in range(8)]
-        dealt = {"ring": [0, 1, 2, 6], "a": [3, 4, 5, 7], "y": [7, 2, 6, 0, 1]}
-        turns = {"ring": 0, "a": 0, "y": 0}
+        rings = {"scalar": [0, 1, 2], "vector": [3, 4, 5], "y": [6, 7]}
+        turns = {"scalar": 0, "vector": 0, "y": 0}
 
-        def next_bank(kind, rows):
-            bank = banks[dealt[kind][turns[kind] % len(dealt[kind])]]
-            turns[kind] = turns[kind] + 1
+        def next_bank(ring, rows):
+            bank = banks[rings[ring][turns[ring] % len(rings[ring])]]
+            turns[ring] = turns[ring] + 1
             return bank[:].rearrange("p (r n) -> p r n", r=rows)
 
+        places = {"free": (0, 0)}
 
-        lists = [held.tile([P, S // 16], U16, name=f"list{i}") for i in range(3)]
-        tab_w = held.tile([P, T], I32, name="tab_w", align_bytes=64)
-        tab_s = held.tile([P, T // 4], I32, name="tab_s", align_bytes=64)
-        raw_s = [reuse.tile([P, H // 4], I32, name=f"raw_s{i}", align_bytes=64, offset=(62 + 2 * i) * H) for i in range(2)]
-        dealt_s = held.tile([P, H // 2], I32, name="dealt_s", align_bytes=64)
-        w_plane = held.tile([P, H // 2], I32, name="w_plane", align_bytes=64)
-        wg_raw = held.tile([P, H // 2], I32, name="wg_raw")
-        wb_raw = reuse.tile([P, H], I32, name="wb_raw", align_bytes=64, offset=52 * H)
-        wr_w = held.tile([P, 2 * N], U8, name="wr_w", align_bytes=64)
-        bias = held.tile([P, N // P], F32, name="bias")
-        wa_raw = [held.tile([P, 4, PASS], F32, name=f"wa_raw{b}") for b in range(2)]
-        wo_raw = [held.tile([P, 4, N], F32, name=f"wo_raw{b}") for b in range(2)]
+        def place(name, shape, dtype, over=None, at=0, room=0):
+            size = SIZE[dtype]
+            for extent in shape[1:]:
+                size = size * extent
+            if over is None:
+                start = places["free"][0]
+                places["free"] = (start + size + room, 0)
+                places[name] = (start, size + room)
+            else:
+                start = places[over][0] + at
+                assert at + size <= places[over][1], name
+                places[name] = (start, places[over][1] - at)
+            return shared.tile(shape, dtype, name=name, align_bytes=64, offset=start)
+
         ROWS = slice(P - 16, P)
         REST = slice(0, P - 16)
-
-        def load_wa(b):
-            nc.sync.dma_start(wa_raw[b][:], wa.rearrange("(p j) c -> p j c", j=4)[:, :, b * PASS : (b + 1) * PASS])
+        lists = [held.tile([P, S // 16], U16, name=f"list{i}") for i in range(3)]
+        tab_w = held.tile([P, T], I32, name="tab_w", align_bytes=64)
+        tab_s = place("tab_s", [P, T // 4], I32)
+        raw_s = place("raw_s", [P, H // 2], I32)
+        dealt_s = place("dealt_s", [P, H // 2], I32)
+        w_plane = held.tile([P, H // 2], I32, name="w_plane", align_bytes=64)
+        planes = [held.tile([P, S // 4], I32, name=f"plane{i}", align_bytes=64) for i in range(3)]
+        wr_plane = held.tile([P, N // 4], I32, name="wr_plane", align_bytes=64)
+        wg_raw = place("wg_raw", [P, H // 2], I32)
+        wb_raw = place("wb_raw", [P, H], I32)
+        wg_w = held.tile([P, H // 2], I32, name="wg_w", align_bytes=64)
+        wb_w = held.tile([P, H], I32, name="wb_w", align_bytes=64)
+        wr_w = held.tile([P, 2 * N], U8, name="wr_w", align_bytes=64)
+        bias = held.tile([P, N // P], F32, name="bias")
+        wa_raw = [place(f"wa_raw{b}", [P, 4, PASS], F32) for b in range(2)]
+        wo_raw = [place(f"wo_raw{b}", [P, 4, N], F32) for b in range(2)]
+        wg_s = w_plane[:].bitcast(U8)[:, 0:H]
+        wb_s = w_plane[:].bitcast(U8)[:, H : 2 * H]
+        wr_s = wr_plane[:].bitcast(U8)
 
         def rows_to_plane(plane, rows, queue):
             for q in range(4):
                 queue.dma_start(plane[32 * q : 32 * q + 4, :], rows[P - 16 + 4 * q : P - 12 + 4 * q, :])
 
-        nc.scalar.dma_start(raw_s[0][ROWS, :], wg_scales[0].bitcast(I32))
-        nc.scalar.dma_start(raw_s[1][ROWS, :], wb_scales[0].bitcast(I32))
-        nc.scalar.dma_start(tab_s[ROWS, :], tab_scales[0].bitcast(I32))
-        for i in range(2):
-            nc.vector.memset(raw_s[i][REST, :], 0)
-        nc.vector.memset(tab_s[REST, :], 0)
-        warm = held.tile([P, 2], F32, name="warm")
-        nc.vector.memset(warm[:, 0:1], 0.0)
-        nc.scalar.activation(warm[:, 1:2], warm[:, 0:1], ACT.Sigmoid)
-        nc.vector.memset(w_plane[:], 0)
-        nc.sync.dma_start(lists[IJ][:], offs)
-        nc.sync.dma_start(lists[IK][:], offs2)
-        nc.sync.dma_start(lists[JK][:], offs3)
-        load_wa(0)
-        nc.sync.dma_start(wg_raw[:], wg_words[0].bitcast(I32))
-        wg_s = w_plane[:].bitcast(U8)[:, 0:H]
-        wb_s = w_plane[:].bitcast(U8)[:, H : 2 * H]
+        def deal_columns(dst, src, engine, passes=2):
+            engine.tensor_copy(
+                dst.rearrange("p (b t g e) -> p b t g e", b=passes, t=4, g=16),
+                src.rearrange("p (b g t e) -> p b t g e", b=passes, t=4, g=16),
+            )
 
         v_w = {}
-        v_s = {}
 
-        picked_s = {
-            IJ: held.tile([P, S], U8, name="picked_ij", align_bytes=64),
-            JK: held.tile([P, 2 * S], U8, name="picked_jk_ik", align_bytes=64),
-        }
+        def pick_scales(i, over=None):
+            rows = place(f"rows{i}", [P, S], U8, over)
+            nc.vector.tensor_copy(rows[:], tab_s[:].bitcast(U8).indirect(lists[i][:]))
+            return rows[:].bitcast(I32)
 
-        def pick_scales(i, first, n):
-            nc.vector.tensor_copy(picked_s[first][:, n * S : (n + 1) * S], tab_s[:].bitcast(U8).indirect(lists[i][:]))
-            v_s[i] = planes[first][:].bitcast(U8)[:, n * S : (n + 1) * S]
-
-        def gather_words(i, h, dst):
-            v_w[i, h] = dst
-            nc.vector.tensor_copy(dst, tab_w[:].bitcast(U32).indirect(lists[i][:, 32 * h : 32 * h + 32]))
+        def pick_words(i, h, over=None, at=0):
+            v_w[i, h] = place(f"v_w{i}{h}", [P, HALF], U32, over, at)
+            nc.vector.tensor_copy(v_w[i, h][:], tab_w[:].bitcast(U32).indirect(lists[i][:, 32 * h : 32 * h + 32]))
 
         def picked(i, tok0, ntok):
             h, lo = divmod(tok0, HALF)
-            return v_w[i, h][:, lo : lo + ntok].bitcast(FP8X4), v_s[i][:, tok0 : tok0 + ntok]
+            return v_w[i, h][:, lo : lo + ntok].bitcast(FP8X4), planes[i][:].bitcast(U8)[:, tok0 : tok0 + ntok]
 
-        STAGE = 0
-        MESSAGES = 28 * H
-        WA_STAGE = 44 * H
-        wg_w = held.tile([P, H // 2], I32, name="wg_w", align_bytes=64)
-        wb_w = held.tile([P, H], I32, name="wb_w", align_bytes=64)
-
-        def deal_columns(dst, src, engine=nc.vector):
-            engine.tensor_copy(
-                dst.rearrange("p (b t g e) -> p b t g e", b=2, t=4, g=16),
-                src.rearrange("p (b g t e) -> p b t g e", b=2, t=4, g=16),
-            )
-
-        wa_bf = [held.tile([P, 4, P, 4], BF16, name="wa_bf0", align_bytes=64), reuse.tile([P, 4, P, 4], BF16, name="wa_bf1", align_bytes=64, offset=WA_STAGE)]
-        wa_s = held.tile([P, H], U8, name="wa_s", align_bytes=64)
-        wo_w = {}
-        wo_s = held.tile([P, 2 * N], U8, name="wo_s", align_bytes=64)
+        wa_bf = {}
         wo_bf = {}
-        gb_place = {(256, 1): WA_STAGE, (768, 1): MESSAGES}
-        B_PLACES = [0, 4, 6, 8, 10, 14, 18, 48]
+        wa_w = {}
+        wo_w = {}
+        wa_s = held.tile([P, H], U8, name="wa_s", align_bytes=64)
+        wo_s = held.tile([P, 2 * N], U8, name="wo_s", align_bytes=64)
 
-        def round_wa(b):
+        def load_wa(b):
+            nc.sync.dma_start(wa_raw[b][:], wa.rearrange("(p j) c -> p j c", j=4)[:, :, b * PASS : (b + 1) * PASS])
+
+        def load_wo(b):
+            rows = wo.rearrange("(b g t e) n -> b t g e n", b=2, t=4, e=8)
             for t in range(4):
-                nc.scalar.copy(
-                    wa_bf[b][:, t].rearrange("p (g e i) j -> p g e j i", e=2, i=4),
-                    wa_raw[b][:].rearrange("p j (g t e i) -> p t g e j i", t=4, e=2, i=4)[:, t],
-                )
+                nc.sync.dma_start(wo_raw[b][:, t, :], rows[b, t])
 
-        def round_wa_on_gpsimd(b):
+        def round_wa(b, on_gpsimd, over=None):
+            wa_bf[b] = place(f"wa_bf{b}", [P, 4, P, 4], BF16, over, room=4096)
             for t in range(4):
-                nc.gpsimd.tensor_scalar(
-                    wa_bf[b][:, t].rearrange("p (g e) j -> p g e j", e=8),
-                    wa_raw[b][:].rearrange("p j (g t e) -> p t g e j", t=4, e=8)[:, t],
-                    1.0, 0.0, ALU.mult, ALU.add,
-                )
+                if on_gpsimd:
+                    nc.gpsimd.tensor_scalar(
+                        wa_bf[b][:, t].rearrange("p (g e) j -> p g e j", e=8),
+                        wa_raw[b][:].rearrange("p j (g t e) -> p t g e j", t=4, e=8)[:, t],
+                        1.0, 0.0, ALU.mult, ALU.add,
+                    )
+                else:
+                    nc.scalar.copy(
+                        wa_bf[b][:, t].rearrange("p (g e i) j -> p g e j i", e=2, i=4),
+                        wa_raw[b][:].rearrange("p j (g t e i) -> p t g e j i", t=4, e=2, i=4)[:, t],
+                    )
 
-        def round_wo_on_gpsimd(b, c):
-            cols = slice(c * P, (c + 1) * P)
-            nc.gpsimd.tensor_scalar(
-                wo_bf[b][:, cols, :], wo_raw[b][:, :, cols].rearrange("p t n -> p n t"), 1.0, 0.0, ALU.mult, ALU.add
-            )
-
-        def round_wo(b, c):
-            cols = slice(c * P, (c + 1) * P)
-            nc.scalar.copy(
-                wo_bf[b][:, cols, :].rearrange("p (m i) t -> p m t i", i=4),
-                wo_raw[b][:, :, cols].rearrange("p t (m i) -> p m t i", i=4),
-            )
+        def round_wo(b, on_gpsimd, over=None, at=0, pieces=2):
+            wo_bf[b] = place(f"wo_bf{b}", [P, N, 4], BF16, over, at)
+            for c in range(pieces):
+                cols = slice(c * N // pieces, (c + 1) * N // pieces)
+                if on_gpsimd:
+                    nc.gpsimd.tensor_scalar(
+                        wo_bf[b][:, cols, :], wo_raw[b][:, :, cols].rearrange("p t n -> p n t"), 1.0, 0.0, ALU.mult, ALU.add
+                    )
+                else:
+                    nc.scalar.copy(
+                        wo_bf[b][:, cols, :].rearrange("p (m i) t -> p m t i", i=4),
+                        wo_raw[b][:, :, cols].rearrange("p t (m i) -> p m t i", i=4),
+                    )
 
         def quantize(codes, scales, values):
             nc.vector.quantize_mx(out=codes.bitcast(FP8X4), scales=scales, in_=values)
 
-        wa_w = {}
-
-        def quantize_wa(b, offset):
-            wa_w[b] = reuse.tile([P, PASS], U32, name=f"wa_w{b}", align_bytes=64, offset=offset)
+        def quantize_wa(b, over=None, at=0):
+            wa_w[b] = place(f"wa_w{b}", [P, PASS], U32, over, at)
             quantize(wa_w[b][:], wa_s[:, b * PASS : (b + 1) * PASS], wa_bf[b][:].rearrange("p t m j -> p (t m j)"))
 
-        def quantize_wo(b, offset):
-            cols = slice(b * N, (b + 1) * N)
-            wo_w[b] = reuse.tile([P, N], U32, name=f"wo_w{b}", align_bytes=64, offset=offset)
-            quantize(wo_w[b][:], wo_s[:, cols], wo_bf[b][:].rearrange("p n t -> p (n t)"))
+        def quantize_wo(b, over=None, at=0):
+            wo_w[b] = place(f"wo_w{b}", [P, N], U32, over, at)
+            quantize(wo_w[b][:], wo_s[:, b * N : (b + 1) * N], wo_bf[b][:].rearrange("p n t -> p (n t)"))
 
         def lone_pass(dst, codes, scales, rhs):
             nc.tensor.matmul_mx(
                 out=dst, lhsT=codes, lhsT_scale=scales, rhs=rhs[0], rhs_scale=rhs[1], start=True, stop=True
             )
 
-        b_outs = []
         gate = {}
+        b_out = {}
         gb = {}
 
-        def gate_pair(tok0, b, s):
-            bank = next_bank("ring", 2)
-            for u in range(2):
-                c0 = b * PASS + (2 * s + u) * P
-                lone_pass(
-                    bank[:, u, :], wg_w[:].bitcast(U8)[:, 2 * c0 : 2 * c0 + 2 * P].bitcast(FP4X4),
-                    wg_s[:, c0 : c0 + P], picked(IJ, tok0, PAIR),
-                )
-            gate[tok0, b, s] = work.tile([P, PAIR, 2], F32, name="gate")
-            nc.scalar.activation(gate[tok0, b, s][:], bank.rearrange("p u n -> p n u"), ACT.Sigmoid)
+        def gates(q, b, over=None):
+            gate[q, b] = place(f"gate{q}{b}", [P, 2, QUARTER, 2], F32, over)
+            for s in range(2):
+                bank = next_bank("scalar", 2)
+                for u in range(2):
+                    c0 = b * PASS + (2 * s + u) * P
+                    lone_pass(
+                        bank[:, u, :], wg_w[:].bitcast(U8)[:, 2 * c0 : 2 * c0 + 2 * P].bitcast(FP4X4),
+                        wg_s[:, c0 : c0 + P], picked(IJ, q * QUARTER, QUARTER),
+                    )
+                nc.scalar.activation(gate[q, b][:, s], bank.rearrange("p u n -> p n u"), ACT.Sigmoid)
 
-        def gate_times_b(tok0, b, s, on_gpsimd=False):
-            bank = next_bank("ring" if on_gpsimd or tok0 >= RING_FROM else "a", 2)
+        def b_pair(q, b, s, ring):
+            bank = next_bank(ring, 2)
             for u in range(2):
                 c0 = b * PASS + (2 * s + u) * P
                 lone_pass(
-                    bank[:, u, :], wb_w[:, c0 : c0 + P].bitcast(FP8X4),
-                    wb_s[:, c0 : c0 + P], picked(JK, tok0, PAIR),
+                    bank[:, u, :], wb_w[:, c0 : c0 + P].bitcast(FP8X4), wb_s[:, c0 : c0 + P], picked(JK, q * QUARTER, QUARTER)
                 )
-            if s == 0:
-                if (tok0, b) in gb_place:
-                    gb[tok0, b] = reuse.tile([P, 2, PAIR, 2], F32, name=f"gb{tok0}", align_bytes=64, offset=gb_place[tok0, b])
-                else:
-                    gb[tok0, b] = work.tile([P, 2, PAIR, 2], F32, name="gb", bufs=7)
-            if on_gpsimd:
-                place = len(b_outs)
-                b_out = reuse.tile([P, PAIR, 2], F32, name=f"b_out{place}", align_bytes=64, offset=B_PLACES[place] * H)
-                b_outs.append(b_out)
-                nc.scalar.copy(b_out[:], bank.rearrange("p u n -> p n u"))
-                nc.gpsimd.tensor_tensor(gb[tok0, b][:, s], b_out[:], gate[tok0, b, s][:], ALU.mult)
-            else:
-                nc.vector.tensor_tensor(
-                    gb[tok0, b][:, s], bank.rearrange("p u n -> p n u"), gate[tok0, b, s][:], ALU.mult
-                )
+            return bank.rearrange("p u n -> p n u")
+
+        def products_on_vector(q, b, over=None, at=0):
+            both = place(f"gb{q}{b}", [P, 2, QUARTER, 2], F32, over, at)
+            for s in range(2):
+                nc.vector.tensor_tensor(both[:, s], b_pair(q, b, s, "vector"), gate[q, b][:, s], ALU.mult)
+            for k in range(2):
+                gb[q, b, k] = both[:, :, k * TOK : (k + 1) * TOK, :]
+
+        def copy_b(q, b):
+            b_out[q, b] = place(f"b_out{q}{b}", [P, 2, QUARTER, 2], F32)
+            for s in range(2):
+                nc.scalar.copy(b_out[q, b][:, s], b_pair(q, b, s, "scalar"))
+
+        def product_on_gpsimd(q, b, k, over=None, at=0):
+            cols = slice(k * TOK, (k + 1) * TOK)
+            gb[q, b, k] = place(f"gb{q}{b}{k}", [P, 2, TOK, 2], F32, over, at)[:]
+            nc.gpsimd.tensor_tensor(
+                gb[q, b, k].rearrange("p s n u -> p s (n u)"), b_out[q, b][:, :, cols, :].rearrange("p s n u -> p s (n u)"),
+                gate[q, b][:, :, cols, :].rearrange("p s n u -> p s (n u)"), ALU.mult,
+            )
 
         h_bf = {}
         h_w = {}
         h_s = {}
-        for tok0, ntok in GROUPS:
-            h_bf[tok0] = reuse.tile([P, 2, ntok, 4], BF16, name=f"h_bf{tok0}", align_bytes=64, offset=MESSAGES + 16 * tok0)
-            h_w[tok0] = held.tile([P, 2 * ntok], U32, name=f"h_w{tok0}", align_bytes=64)
-            h_s[tok0] = held.tile([P, 2 * ntok], U8, name=f"h_s{tok0}", align_bytes=64)
 
-        def message(tok0, b, k):
-            tok = tok0 + k * TOK
-            bank = next_bank("a", 4)
+        def message(tok, b):
+            q, k = divmod(tok // TOK, 2)
+            first, ntok = max(group for group in GROUPS if group[0] <= tok)
+            if first not in h_bf:
+                h_bf[first] = place(f"h_bf{first}", [P, 2, ntok, 4], BF16, H_OVER.get(first))
+            bank = next_bank("vector", 4)
             for t in range(4):
                 c0 = b * PASS + t * P
                 lone_pass(bank[:, t, :], wa_w[b][:, t * P : (t + 1) * P].bitcast(FP8X4), wa_s[:, c0 : c0 + P], picked(IK, tok, TOK))
-            first = max(g0 for g0, ntok in GROUPS if g0 <= tok)
             nc.vector.tensor_tensor(
                 h_bf[first][:, b, tok - first : tok - first + TOK, :].rearrange("p n (s u) -> p n s u", s=2),
                 bank.rearrange("p (s u) n -> p n s u", s=2),
-                gb[tok0, b][:, :, k * TOK : (k + 1) * TOK, :].rearrange("p s n u -> p n s u"),
+                gb[q, b, k].rearrange("p s n u -> p n s u"),
                 ALU.mult,
             )
 
-        def quantize_h(group, passes):
+        def messages(q, b):
+            for k in range(2):
+                message(q * QUARTER + k * TOK, b)
+
+        def quantize_h(group, passes, over=None):
             tok0, ntok = group
+            if tok0 not in h_w:
+                h_w[tok0] = place(f"h_w{tok0}", [P, 2 * ntok], U32, over)
+                h_s[tok0] = held.tile([P, 2 * ntok], U8, name=f"h_s{tok0}", align_bytes=64)
             cols = slice(passes[0] * ntok, (passes[-1] + 1) * ntok)
             values = h_bf[tok0][:].rearrange("p b n t -> p (b n t)")[:, 4 * cols.start : 4 * cols.stop]
             quantize(h_w[tok0][:, cols], h_s[tok0][:, cols], values)
 
         y_bank = {}
 
-        def open_y(group, cs, kind="y"):
+        def open_y(group, cs):
             tok0, ntok = group
-            y_bank[tok0, cs[0]] = next_bank(kind, 512 // ntok)
+            y_bank[tok0, cs[0]] = next_bank("y", 512 // ntok)
             width = ntok if ntok == HALF else TOK
             for c in cs:
                 for lo in range(0, ntok, width):
@@ -258,16 +264,16 @@ def tile_list_triangle_edge_update_kernel(
         def add_to_y(group, cs, b):
             tok0, ntok = group
             for c in cs:
-                cols = slice(b * N + c * P, b * N + (c + 1) * P)
                 nc.tensor.matmul_mx(
-                    out=y_bank[tok0, cs[0]][:, c - cs[0], :], lhsT=wo_w[b][:, c * P : (c + 1) * P].bitcast(FP8X4), lhsT_scale=wo_s[:, cols],
+                    out=y_bank[tok0, cs[0]][:, c - cs[0], :],
+                    lhsT=wo_w[b][:, c * P : (c + 1) * P].bitcast(FP8X4), lhsT_scale=wo_s[:, b * N + c * P : b * N + (c + 1) * P],
                     rhs=h_w[tok0][:, b * ntok : (b + 1) * ntok].bitcast(FP8X4), rhs_scale=h_s[tok0][:, b * ntok : (b + 1) * ntok],
                     start=False, stop=(b == 1 and c == cs[-1]),
                 )
 
         def store_y(group, cs, on_vector=False):
             tok0, ntok = group
-            y = work.tile([P, len(cs), ntok], F32, name="y", bufs=9)
+            y = held.tile([P, len(cs), ntok], F32, name=f"y{tok0}_{cs[0]}")
             for c in cs:
                 src = y_bank[tok0, cs[0]][:, c - cs[0], :]
                 if on_vector:
@@ -277,139 +283,124 @@ def tile_list_triangle_edge_update_kernel(
             dst = out.rearrange("(c p) s -> p c s", p=P)[:, cs[0] : cs[-1] + 1, tok0 : tok0 + ntok]
             nc.sync.dma_start(dst, y[:])
 
-        def whole_y(group, cs, kind="y"):
-            open_y(group, cs, kind)
-            for b in range(2):
-                add_to_y(group, cs, b)
-            store_y(group, cs)
-
-        for i in range(2):
-            deal_columns(dealt_s[:, i * H // 4 : (i + 1) * H // 4], raw_s[i][:])
-        rows_to_plane(w_plane, dealt_s[:], nc.sync)
-        nc.sync.dma_start(tab_w[:], tab_words[0].rearrange("p t i -> p (t i)").bitcast(I32))
-        planes = {
-            IJ: reuse.tile([P, S // 4], I32, name="plane_ij", align_bytes=64, offset=61 * H + 64),
-            JK: reuse.tile([P, S // 2], I32, name="plane_jk_ik", align_bytes=64, offset=62 * H + 64),
-        }
-        wr_plane = reuse.tile([P, N // 4], I32, name="wr_plane", align_bytes=64, offset=64 * H + 64)
-        for plane in (planes[IJ], planes[JK], wr_plane):
-            nc.gpsimd.memset(plane[:], 0)
-        wr_s = wr_plane[:].bitcast(U8)
-        pick_scales(IJ, IJ, 0)
-        rows_to_plane(planes[IJ], picked_s[IJ][:].bitcast(I32), nc.sync)
-        nc.sync.dma_start(wb_raw[:], wb_words[0].rearrange("p c i -> p (c i)").bitcast(I32))
-        load_wa(1)
-        round_wa(0)
-        pick_scales(IK, JK, 1)
-        pick_scales(JK, JK, 0)
-        rows_to_plane(planes[JK], picked_s[JK][:].bitcast(I32), nc.sync)
-        wo_rows = wo.rearrange("(b g t e) n -> b t g e n", b=2, t=4, e=8)
-        for b in range(2):
-            for t in range(4):
-                nc.sync.dma_start(wo_raw[b][:, t, :], wo_rows[b, t])
-        nc.sync.dma_start(wr_w[:].bitcast(I32), wr_words[0].bitcast(I32))
-        for r in range(4):
-            nc.sync.dma_start(wr_plane[r:P:32, :], wr_scales[0, r:16:4, :].bitcast(I32))
-        with nc.allow_non_contiguous_dma(reason="one bias value a partition"):
-            nc.sync.dma_start(bias[:], bo.rearrange("(c p) -> p c", p=P))
-        deal_columns(wg_w[:], wg_raw[:], nc.gpsimd)
-        for i in (IJ, JK):
-            picked_w = held.tile([P, HALF], U32, name=f"picked_w{i}", align_bytes=64)
-            gather_words(i, 0, picked_w[:])
-        deal_columns(wb_w[:], wb_raw[:])
-        quantize_wa(0, 50 * H + 64)
-        late_w = reuse.tile([P, 4 * HALF], U32, name="late_w", align_bytes=64, offset=52 * H + 64)
-        for n, (i, h) in enumerate(((IJ, 1), (IK, 0), (JK, 1), (IK, 1))):
-            gather_words(i, h, late_w[:, n * HALF : (n + 1) * HALF])
-        round_wa_on_gpsimd(1)
-
-        def gates(tok0, b):
-            for s in range(2):
-                gate_pair(tok0, b, s)
-
-        def products(tok0, b, on_gpsimd=False):
-            for s in range(2):
-                gate_times_b(tok0, b, s, on_gpsimd)
-
-        def messages(tok0, b):
-            for k in range(2):
-                message(tok0, b, k)
-
-        def round_wo_on_vector(b):
-            wo_bf[b] = held.tile([P, N, 4], BF16, name=f"wo_bf{b}", align_bytes=64)
-            nc.vector.tensor_copy(
-                wo_bf[b][:].rearrange("p (m i) t -> p m t i", i=4), wo_raw[b][:].rearrange("p t (m i) -> p m t i", i=4)
-            )
-
-        def round_wo_pass(b, place):
-            wo_bf[b] = reuse.tile([P, N, 4], BF16, name=f"wo_bf{b}", align_bytes=64, offset=STAGE + place * 2 * H)
-            for c in range(4):
-                round_wo(b, c)
-
-
-        def open_quarter(q, kind="y"):
-            for cs in ([0, 1], [2, 3]):
-                open_y(GROUPS[q], cs, kind)
-
         def close_y(group, cs):
             for b in range(2):
                 add_to_y(group, cs, b)
             store_y(group, cs)
+
+        def whole_y(group, cs):
+            open_y(group, cs)
+            close_y(group, cs)
+
+        nc.scalar.dma_start(raw_s[ROWS, 0 : H // 4], wg_scales[0].bitcast(I32))
+        nc.scalar.dma_start(raw_s[ROWS, H // 4 : H // 2], wb_scales[0].bitcast(I32))
+        nc.scalar.dma_start(tab_s[ROWS, :], tab_scales[0].bitcast(I32))
+        nc.sync.dma_start(lists[IJ][:], offs)
+        nc.sync.dma_start(lists[JK][:], offs3)
+        nc.sync.dma_start(wg_raw[:], wg_words[0].bitcast(I32))
+        nc.sync.dma_start(tab_w[:], tab_words[0].rearrange("p t i -> p (t i)").bitcast(I32))
+        nc.sync.dma_start(wb_raw[:], wb_words[0].rearrange("p c i -> p (c i)").bitcast(I32))
+        nc.sync.dma_start(lists[IK][:], offs2)
+        load_wa(0)
+        load_wa(1)
+        nc.sync.dma_start(wr_w[:].bitcast(I32), wr_words[0].bitcast(I32))
+        load_wo(0)
+        nc.vector.memset(raw_s[REST, :], 0)
+        nc.vector.memset(tab_s[REST, :], 0)
+        warm = held.tile([P, 2], F32, name="warm")
+        nc.vector.memset(warm[:, 0:1], 0.0)
+        nc.scalar.activation(warm[:, 1:2], warm[:, 0:1], ACT.Sigmoid)
+        for plane in [w_plane] + planes + [wr_plane]:
+            nc.vector.memset(plane[:], 0)
+        deal_columns(dealt_s[:], raw_s[:], nc.vector, passes=4)
+        deal_columns(wg_w[:], wg_raw[:], nc.vector)
+        rows_to_plane(w_plane, dealt_s[:], nc.scalar)
+        for i in (IJ, JK):
+            rows_to_plane(planes[i], pick_scales(i), nc.scalar)
+        pick_words(IJ, 0)
+        pick_words(JK, 0)
+        deal_columns(wb_w[:], wb_raw[:], nc.vector)
+        ik_rows = pick_scales(IK, "wb_raw")
+        load_wo(1)
+        for r in range(4):
+            nc.gpsimd.dma_start(wr_plane[r:P:32, :], wr_scales[0, r:16:4, :].bitcast(I32))
+        with nc.allow_non_contiguous_dma(reason="one bias value a partition"):
+            nc.sync.dma_start(bias[:], bo.rearrange("(c p) -> p c", p=P))
+
+        def open_quarter(q):
+            for cs in ([0, 1], [2, 3]):
+                open_y(GROUPS[q], cs)
 
         def close_quarter(q):
             for cs in ([0, 1], [2, 3]):
                 close_y(GROUPS[q], cs)
 
         gates(0, 0)
-        gates(256, 0)
         gates(0, 1)
-        gates(256, 1)
-        products(0, 0)
-        products(0, 1, True)
-        products(256, 0)
-        quantize_wa(1, 2 * H + 64)
-        products(256, 1, True)
-        round_wo_pass(0, 10)
-        gates(512, 1)
-        products(512, 1, True)
-        gates(512, 0)
-        round_wo_pass(1, 12)
-        gates(768, 1)
-        gates(768, 0)
+        copy_b(0, 1)
+        rows_to_plane(planes[IK], ik_rows, nc.scalar)
+        round_wa(0, True)
+        round_wa(1, False)
+        pick_words(IJ, 1, "tab_s")
+        pick_words(IK, 0, "tab_s", 2048)
+        product_on_gpsimd(0, 1, 0)
+        product_on_gpsimd(0, 1, 1)
+        products_on_vector(0, 0)
+        pick_words(JK, 1, "gate00")
+        quantize_wa(0, "b_out01")
+        quantize_wa(1, "b_out01", 2048)
+        round_wo(0, True, "wa_bf1")
+        gates(1, 1)
+        copy_b(1, 1)
+        gates(1, 0)
+        open_quarter(0)
         messages(0, 0)
-        messages(256, 0)
-        dealt["a"] = [3, 4, 5]
-        turns["a"] = 0
         messages(0, 1)
-        messages(256, 1)
-        products(512, 0)
-        quantize_wo(0, 12 * H + 64)
-        quantize_h(GROUPS[0], [0])
-        quantize_wo(1, 14 * H + 64)
-        quantize_h(GROUPS[0], [1])
-        turns["ring"] = 2
-        products(768, 1, True)
-        messages(512, 1)
-        messages(512, 0)
-        products(768, 0)
-        quantize_h(GROUPS[1], [0, 1])
-        tail = GROUPS[3]
-        tail_banks = ([0, 1], [2, 3])
-        message(768, 0, 0)
-        message(768, 1, 0)
-        message(768, 0, 1)
-        for c in range(4):
-            whole_y(GROUPS[0], [c])
+        product_on_gpsimd(1, 1, 0, "wo_raw0")
+        round_wo(1, False)
+        products_on_vector(1, 0)
+        quantize_wo(0, "gate10")
+        quantize_h(GROUPS[0], [0, 1], "gb011")
+        quantize_wo(1, "gb010")
+        gates(2, 1)
+        copy_b(2, 1)
+        product_on_gpsimd(1, 1, 1, "wo_bf0")
+        product_on_gpsimd(2, 1, 0, "wo_bf0", 2048)
+        messages(1, 0)
+        messages(1, 1)
+        gates(2, 0)
+        close_quarter(0)
         open_quarter(1)
+        pick_words(IK, 1, "gb111")
+        quantize_h(GROUPS[1], [0, 1])
+        product_on_gpsimd(2, 1, 1, "h_bf256")
+        gates(3, 1)
+        copy_b(3, 1)
+        product_on_gpsimd(3, 1, 0)
+        product_on_gpsimd(3, 1, 1)
+        products_on_vector(2, 0)
+        gates(3, 0)
+        messages(2, 0)
+        messages(2, 1)
+        products_on_vector(3, 0)
         close_quarter(1)
+        rings["y"] = [0, 1, 2, 6, 7]
+        turns["y"] = 0
+        tail = GROUPS[4]
+        message(768, 0)
         quantize_h(GROUPS[2], [0, 1])
+        message(768, 1)
+        message(896, 0)
+        quantize_h(GROUPS[3], [0, 1])
         quantize_h(tail, [0])
-        message(768, 1, 1)
-        whole_y(GROUPS[2], [0, 1, 2, 3])
-        for cs in tail_banks:
+        message(896, 1)
+        for cs in ([0, 1], [2, 3]):
+            whole_y(GROUPS[2], cs)
+        whole_y(GROUPS[3], [0, 1, 2, 3])
+        for cs in ([0, 1], [2, 3]):
             open_y(tail, cs)
             add_to_y(tail, cs, 0)
         quantize_h(tail, [1])
-        for cs in tail_banks:
+        for cs in ([0, 1], [2, 3]):
             add_to_y(tail, cs, 1)
             store_y(tail, cs, on_vector=(cs[0] == 0))

@@ -22,8 +22,8 @@ HALF = 512
 QUARTER = 256
 TOK = 128
 IJ, IK, JK = 0, 1, 2
-GROUPS = [(0, 256), (256, 256), (512, 256), (768, 128), (896, 128)]
-H_OVER = {256: "wo_bf1"}
+GROUPS = [(0, 512), (512, 256), (768, 128), (896, 128)]
+H_PLACE = {}
 SIZE = {F32: 4, I32: 4, U32: 4, BF16: 2, U8: 1}
 
 
@@ -45,20 +45,20 @@ def tile_list_triangle_edge_update_kernel(
             turns[ring] = turns[ring] + 1
             return bank[:].rearrange("p (r n) -> p r n", r=rows)
 
-        places = {"free": (0, 0)}
+        places = {"free": (0, 0, 0)}
 
-        def place(name, shape, dtype, over=None, at=0, room=0):
+        def place(name, shape, dtype, over=None, at=0, room=0, lead=0):
             size = SIZE[dtype]
             for extent in shape[1:]:
                 size = size * extent
             if over is None:
-                start = places["free"][0]
-                places["free"] = (start + size + room, 0)
-                places[name] = (start, size + room)
+                start = places["free"][0] + lead
+                places["free"] = (start + size + room, 0, 0)
+                places[name] = (start, size + room, lead)
             else:
                 start = places[over][0] + at
-                assert at + size <= places[over][1], name
-                places[name] = (start, places[over][1] - at)
+                assert -at <= places[over][2] and at + size <= places[over][1], name
+                places[name] = (start, places[over][1] - at, places[over][2] + at)
             return shared.tile(shape, dtype, name=name, align_bytes=64, offset=start)
 
         ROWS = slice(P - 16, P)
@@ -67,9 +67,11 @@ def tile_list_triangle_edge_update_kernel(
         tab_w = held.tile([P, T], I32, name="tab_w", align_bytes=64)
         tab_s = place("tab_s", [P, T // 4], I32)
         raw_s = place("raw_s", [P, H // 2], I32)
-        dealt_s = place("dealt_s", [P, H // 2], I32)
-        w_plane = held.tile([P, H // 2], I32, name="w_plane", align_bytes=64)
-        planes = [held.tile([P, S // 4], I32, name=f"plane{i}", align_bytes=64) for i in range(3)]
+        early_rows = place("early_rows", [P, 3 * H // 4], I32)
+        early_plane = held.tile([P, 3 * H // 4], I32, name="early_plane", align_bytes=64)
+        side_plane = {i: held.tile([P, S // 4], I32, name=f"side_plane{i}", align_bytes=64) for i in (JK, IK)}
+        early = early_plane[:].bitcast(U8)
+        v_s = {IJ: early[:, 2 * H : 2 * H + S], JK: side_plane[JK][:].bitcast(U8), IK: side_plane[IK][:].bitcast(U8)}
         wr_plane = held.tile([P, N // 4], I32, name="wr_plane", align_bytes=64)
         wg_raw = place("wg_raw", [P, H // 2], I32)
         wb_raw = place("wb_raw", [P, H], I32)
@@ -79,8 +81,8 @@ def tile_list_triangle_edge_update_kernel(
         bias = held.tile([P, N // P], F32, name="bias")
         wa_raw = [place(f"wa_raw{b}", [P, 4, PASS], F32) for b in range(2)]
         wo_raw = [place(f"wo_raw{b}", [P, 4, N], F32) for b in range(2)]
-        wg_s = w_plane[:].bitcast(U8)[:, 0:H]
-        wb_s = w_plane[:].bitcast(U8)[:, H : 2 * H]
+        wg_s = early[:, 0:H]
+        wb_s = early[:, H : 2 * H]
         wr_s = wr_plane[:].bitcast(U8)
 
         def rows_to_plane(plane, rows, queue):
@@ -95,10 +97,8 @@ def tile_list_triangle_edge_update_kernel(
 
         v_w = {}
 
-        def pick_scales(i, over=None):
-            rows = place(f"rows{i}", [P, S], U8, over)
-            nc.vector.tensor_copy(rows[:], tab_s[:].bitcast(U8).indirect(lists[i][:]))
-            return rows[:].bitcast(I32)
+        def pick_scales(i, rows):
+            nc.vector.tensor_copy(rows, tab_s[:].bitcast(U8).indirect(lists[i][:]))
 
         def pick_words(i, h, over=None, at=0):
             v_w[i, h] = place(f"v_w{i}{h}", [P, HALF], U32, over, at)
@@ -106,7 +106,7 @@ def tile_list_triangle_edge_update_kernel(
 
         def picked(i, tok0, ntok):
             h, lo = divmod(tok0, HALF)
-            return v_w[i, h][:, lo : lo + ntok].bitcast(FP8X4), planes[i][:].bitcast(U8)[:, tok0 : tok0 + ntok]
+            return v_w[i, h][:, lo : lo + ntok].bitcast(FP8X4), v_s[i][:, tok0 : tok0 + ntok]
 
         wa_bf = {}
         wo_bf = {}
@@ -138,8 +138,8 @@ def tile_list_triangle_edge_update_kernel(
                         wa_raw[b][:].rearrange("p j (g t e i) -> p t g e j i", t=4, e=2, i=4)[:, t],
                     )
 
-        def round_wo(b, on_gpsimd, over=None, at=0, pieces=2):
-            wo_bf[b] = place(f"wo_bf{b}", [P, N, 4], BF16, over, at)
+        def round_wo(b, on_gpsimd, pieces=2, **where):
+            wo_bf[b] = place(f"wo_bf{b}", [P, N, 4], BF16, **where)
             for c in range(pieces):
                 cols = slice(c * N // pieces, (c + 1) * N // pieces)
                 if on_gpsimd:
@@ -217,12 +217,12 @@ def tile_list_triangle_edge_update_kernel(
         h_w = {}
         h_s = {}
 
-        def message(tok, b):
+        def message(tok, b, ring="vector"):
             q, k = divmod(tok // TOK, 2)
             first, ntok = max(group for group in GROUPS if group[0] <= tok)
             if first not in h_bf:
-                h_bf[first] = place(f"h_bf{first}", [P, 2, ntok, 4], BF16, H_OVER.get(first))
-            bank = next_bank("vector", 4)
+                h_bf[first] = place(f"h_bf{first}", [P, 2, ntok, 4], BF16, **H_PLACE.get(first, {}))
+            bank = next_bank(ring, 4)
             for t in range(4):
                 c0 = b * PASS + t * P
                 lone_pass(bank[:, t, :], wa_w[b][:, t * P : (t + 1) * P].bitcast(FP8X4), wa_s[:, c0 : c0 + P], picked(IK, tok, TOK))
@@ -233,9 +233,9 @@ def tile_list_triangle_edge_update_kernel(
                 ALU.mult,
             )
 
-        def messages(q, b):
+        def messages(q, b, ring="vector"):
             for k in range(2):
-                message(q * QUARTER + k * TOK, b)
+                message(q * QUARTER + k * TOK, b, ring)
 
         def quantize_h(group, passes, over=None):
             tok0, ntok = group
@@ -292,111 +292,106 @@ def tile_list_triangle_edge_update_kernel(
             open_y(group, cs)
             close_y(group, cs)
 
-        nc.scalar.dma_start(raw_s[ROWS, 0 : H // 4], wg_scales[0].bitcast(I32))
-        nc.scalar.dma_start(raw_s[ROWS, H // 4 : H // 2], wb_scales[0].bitcast(I32))
         nc.scalar.dma_start(tab_s[ROWS, :], tab_scales[0].bitcast(I32))
+        nc.scalar.dma_start(raw_s[ROWS, H // 4 : H // 2], wb_scales[0].bitcast(I32))
         nc.sync.dma_start(lists[IJ][:], offs)
         nc.sync.dma_start(lists[JK][:], offs3)
+        nc.sync.dma_start(raw_s[ROWS, 0 : H // 4], wg_scales[0].bitcast(I32))
         nc.sync.dma_start(wg_raw[:], wg_words[0].bitcast(I32))
         nc.sync.dma_start(tab_w[:], tab_words[0].rearrange("p t i -> p (t i)").bitcast(I32))
-        nc.sync.dma_start(wb_raw[:], wb_words[0].rearrange("p c i -> p (c i)").bitcast(I32))
-        nc.sync.dma_start(lists[IK][:], offs2)
-        load_wa(0)
-        load_wa(1)
-        nc.sync.dma_start(wr_w[:].bitcast(I32), wr_words[0].bitcast(I32))
-        load_wo(0)
-        nc.vector.memset(raw_s[REST, :], 0)
         nc.vector.memset(tab_s[REST, :], 0)
+        nc.vector.memset(raw_s[REST, :], 0)
         warm = held.tile([P, 2], F32, name="warm")
         nc.vector.memset(warm[:, 0:1], 0.0)
         nc.scalar.activation(warm[:, 1:2], warm[:, 0:1], ACT.Sigmoid)
-        for plane in [w_plane] + planes + [wr_plane]:
-            nc.vector.memset(plane[:], 0)
-        deal_columns(dealt_s[:], raw_s[:], nc.vector, passes=4)
-        deal_columns(wg_w[:], wg_raw[:], nc.vector)
-        rows_to_plane(w_plane, dealt_s[:], nc.scalar)
-        for i in (IJ, JK):
-            rows_to_plane(planes[i], pick_scales(i), nc.scalar)
+        for plane in (early_plane, side_plane[JK], side_plane[IK], wr_plane):
+            nc.gpsimd.memset(plane[:], 0)
+        deal_columns(wg_w[:], wg_raw[:], nc.gpsimd)
+        ij_rows = place("ij_rows", [P, S], U8)
+        pick_scales(IJ, ij_rows[:])
+        deal_columns(early_rows[:, 0 : H // 2], raw_s[:], nc.vector, passes=4)
+        nc.vector.tensor_copy(early_rows[:, H // 2 : 3 * H // 4], ij_rows[:].bitcast(I32))
+        rows_to_plane(early_plane, early_rows[:], nc.sync)
+        nc.sync.dma_start(wb_raw[:], wb_words[0].rearrange("p c i -> p (c i)").bitcast(I32))
+        nc.sync.dma_start(lists[IK][:], offs2)
+        load_wa(0)
+        jk_rows = place("jk_rows", [P, S], U8, "raw_s")
+        pick_scales(JK, jk_rows[:])
+        rows_to_plane(side_plane[JK], jk_rows[:].bitcast(I32), nc.sync)
+        load_wa(1)
         pick_words(IJ, 0)
         pick_words(JK, 0)
         deal_columns(wb_w[:], wb_raw[:], nc.vector)
-        ik_rows = pick_scales(IK, "wb_raw")
+        ik_rows = place("ik_rows", [P, S], U8, "wb_raw")
+        pick_scales(IK, ik_rows[:])
+        load_wo(0)
+        rows_to_plane(side_plane[IK], ik_rows[:].bitcast(I32), nc.sync)
         load_wo(1)
+        nc.sync.dma_start(wr_w[:].bitcast(I32), wr_words[0].bitcast(I32))
         for r in range(4):
-            nc.gpsimd.dma_start(wr_plane[r:P:32, :], wr_scales[0, r:16:4, :].bitcast(I32))
+            nc.sync.dma_start(wr_plane[r:P:32, :], wr_scales[0, r:16:4, :].bitcast(I32))
         with nc.allow_non_contiguous_dma(reason="one bias value a partition"):
             nc.sync.dma_start(bias[:], bo.rearrange("(c p) -> p c", p=P))
 
-        def open_quarter(q):
-            for cs in ([0, 1], [2, 3]):
-                open_y(GROUPS[q], cs)
-
-        def close_quarter(q):
-            for cs in ([0, 1], [2, 3]):
-                close_y(GROUPS[q], cs)
-
         gates(0, 0)
         gates(0, 1)
+        gates(1, 0)
         copy_b(0, 1)
-        rows_to_plane(planes[IK], ik_rows, nc.scalar)
+        turns["scalar"] = turns["scalar"] + 1
         round_wa(0, True)
-        round_wa(1, False)
-        pick_words(IJ, 1, "tab_s")
-        pick_words(IK, 0, "tab_s", 2048)
+        pick_words(IK, 0, "tab_s")
+        pick_words(IJ, 1, "tab_s", 2048)
         product_on_gpsimd(0, 1, 0)
         product_on_gpsimd(0, 1, 1)
         products_on_vector(0, 0)
         pick_words(JK, 1, "gate00")
-        quantize_wa(0, "b_out01")
-        quantize_wa(1, "b_out01", 2048)
-        round_wo(0, True, "wa_bf1")
+        round_wa(1, False)
         gates(1, 1)
         copy_b(1, 1)
-        gates(1, 0)
-        open_quarter(0)
-        messages(0, 0)
+        quantize_wa(0, "b_out01")
+        quantize_wa(1, "b_out01", 2048)
+        product_on_gpsimd(1, 1, 0, "wa_bf1")
+        product_on_gpsimd(1, 1, 1, "wa_bf1", 2048)
+        round_wo(1, True, over="gate11")
+        products_on_vector(1, 0, "wa_bf0")
+        messages(0, 0, "scalar")
+        round_wo(0, False)
         messages(0, 1)
-        product_on_gpsimd(1, 1, 0, "wo_raw0")
-        round_wo(1, False)
-        products_on_vector(1, 0)
-        quantize_wo(0, "gate10")
-        quantize_h(GROUPS[0], [0, 1], "gb011")
-        quantize_wo(1, "gb010")
-        gates(2, 1)
-        copy_b(2, 1)
-        product_on_gpsimd(1, 1, 1, "wo_bf0")
-        product_on_gpsimd(2, 1, 0, "wo_bf0", 2048)
         messages(1, 0)
         messages(1, 1)
+        gates(2, 1)
+        copy_b(2, 1)
         gates(2, 0)
-        close_quarter(0)
-        open_quarter(1)
-        pick_words(IK, 1, "gb111")
-        quantize_h(GROUPS[1], [0, 1])
-        product_on_gpsimd(2, 1, 1, "h_bf256")
         gates(3, 1)
         copy_b(3, 1)
-        product_on_gpsimd(3, 1, 0)
-        product_on_gpsimd(3, 1, 1)
-        products_on_vector(2, 0)
         gates(3, 0)
+        quantize_wo(0, "gb110")
+        quantize_wo(1, "gb10")
+        quantize_h(GROUPS[0], [0, 1])
+        pick_words(IK, 1, "gb111")
+        product_on_gpsimd(2, 1, 0, "h_bf0")
+        product_on_gpsimd(2, 1, 1, "h_bf0", 2048)
+        product_on_gpsimd(3, 1, 0, "h_bf0", 4096)
+        product_on_gpsimd(3, 1, 1, "h_bf0", 6144)
+        products_on_vector(2, 0)
+        message(512, 1)
         messages(2, 0)
-        messages(2, 1)
+        message(640, 1)
         products_on_vector(3, 0)
-        close_quarter(1)
-        rings["y"] = [0, 1, 2, 6, 7]
-        turns["y"] = 0
-        tail = GROUPS[4]
+        tail = GROUPS[3]
         message(768, 0)
-        quantize_h(GROUPS[2], [0, 1])
+        quantize_h(GROUPS[1], [0, 1])
         message(768, 1)
         message(896, 0)
-        quantize_h(GROUPS[3], [0, 1])
+        quantize_h(GROUPS[2], [0, 1])
         quantize_h(tail, [0])
         message(896, 1)
+        rings["y"] = [6, 7, 0, 1, 2]
+        for c in range(4):
+            whole_y(GROUPS[0], [c])
         for cs in ([0, 1], [2, 3]):
-            whole_y(GROUPS[2], cs)
-        whole_y(GROUPS[3], [0, 1, 2, 3])
+            whole_y(GROUPS[1], cs)
+        whole_y(GROUPS[2], [0, 1, 2, 3])
         for cs in ([0, 1], [2, 3]):
             open_y(tail, cs)
             add_to_y(tail, cs, 0)

@@ -79,7 +79,7 @@ def tile_list_triangle_edge_update_kernel(
         wb_w = held.tile([P, H], I32, name="wb_w", align_bytes=64)
         wr_w = held.tile([P, 2 * N], U8, name="wr_w", align_bytes=64)
         bias = held.tile([P, N // P], F32, name="bias")
-        wa_raw = [place(f"wa_raw{b}", [P, 4, PASS], F32) for b in range(2)]
+        wa_raw = [place(f"wa_raw{b}", [P, 4, PASS], F32, lead=4096 * b, room=64 * b) for b in range(2)]
         wo_raw = [place(f"wo_raw{b}", [P, 4, N], F32) for b in range(2)]
         wg_s = early[:, 0:H]
         wb_s = early[:, H : 2 * H]
@@ -124,12 +124,12 @@ def tile_list_triangle_edge_update_kernel(
                 nc.sync.dma_start(wo_raw[b][:, t, :], rows[b, t])
 
         def round_wa(b, on_gpsimd, over=None):
-            wa_bf[b] = place(f"wa_bf{b}", [P, 4, P, 4], BF16, over, room=4096)
+            wa_bf[b] = place(f"wa_bf{b}", [P, 4, P, 4], BF16, over, room=4096, lead=4096)
             for t in range(4):
                 if on_gpsimd:
                     nc.gpsimd.tensor_scalar(
-                        wa_bf[b][:, t].rearrange("p (g e) j -> p g e j", e=8),
-                        wa_raw[b][:].rearrange("p j (g t e) -> p t g e j", t=4, e=8)[:, t],
+                        wa_bf[b][:, t].rearrange("p (g e) j -> p g j e", e=8),
+                        wa_raw[b][:].rearrange("p j (g t e) -> p t g j e", t=4, e=8)[:, t],
                         1.0, 0.0, ALU.mult, ALU.add,
                     )
                 else:
@@ -144,13 +144,21 @@ def tile_list_triangle_edge_update_kernel(
                 cols = slice(c * N // pieces, (c + 1) * N // pieces)
                 if on_gpsimd:
                     nc.gpsimd.tensor_scalar(
-                        wo_bf[b][:, cols, :], wo_raw[b][:, :, cols].rearrange("p t n -> p n t"), 1.0, 0.0, ALU.mult, ALU.add
+                        wo_bf[b][:, cols, :].rearrange("p (m i) t -> p m t i", i=2),
+                        wo_raw[b][:, :, cols].rearrange("p t (m i) -> p m t i", i=2),
+                        1.0, 0.0, ALU.mult, ALU.add,
                     )
                 else:
                     nc.scalar.copy(
                         wo_bf[b][:, cols, :].rearrange("p (m i) t -> p m t i", i=4),
                         wo_raw[b][:, :, cols].rearrange("p t (m i) -> p m t i", i=4),
                     )
+
+        def round_wo_on_vector(b, **where):
+            wo_bf[b] = place(f"wo_bf{b}", [P, N, 4], BF16, **where)
+            nc.vector.tensor_copy(
+                wo_bf[b][:].rearrange("p (m i) t -> p m t i", i=4), wo_raw[b][:].rearrange("p t (m i) -> p m t i", i=4)
+            )
 
         def quantize(codes, scales, values):
             nc.vector.quantize_mx(out=codes.bitcast(FP8X4), scales=scales, in_=values)
@@ -172,8 +180,8 @@ def tile_list_triangle_edge_update_kernel(
         b_out = {}
         gb = {}
 
-        def gates(q, b, over=None):
-            gate[q, b] = place(f"gate{q}{b}", [P, 2, QUARTER, 2], F32, over)
+        def gates(q, b, over=None, at=0):
+            gate[q, b] = place(f"gate{q}{b}", [P, 2, QUARTER, 2], F32, over, at)
             for s in range(2):
                 bank = next_bank("scalar", 2)
                 for u in range(2):
@@ -200,8 +208,8 @@ def tile_list_triangle_edge_update_kernel(
             for k in range(2):
                 gb[q, b, k] = both[:, :, k * TOK : (k + 1) * TOK, :]
 
-        def copy_b(q, b):
-            b_out[q, b] = place(f"b_out{q}{b}", [P, 2, QUARTER, 2], F32)
+        def copy_b(q, b, over=None, at=0):
+            b_out[q, b] = place(f"b_out{q}{b}", [P, 2, QUARTER, 2], F32, over, at)
             for s in range(2):
                 nc.scalar.copy(b_out[q, b][:, s], b_pair(q, b, s, "scalar"))
 
@@ -212,6 +220,12 @@ def tile_list_triangle_edge_update_kernel(
                 gb[q, b, k].rearrange("p s n u -> p s (n u)"), b_out[q, b][:, :, cols, :].rearrange("p s n u -> p s (n u)"),
                 gate[q, b][:, :, cols, :].rearrange("p s n u -> p s (n u)"), ALU.mult,
             )
+
+        def products_on_gpsimd(q, b, over=None, at=0):
+            both = place(f"gb{q}{b}", [P, 2, QUARTER, 2], F32, over, at)
+            nc.gpsimd.tensor_tensor(both[:], b_out[q, b][:], gate[q, b][:], ALU.mult)
+            for k in range(2):
+                gb[q, b, k] = both[:, :, k * TOK : (k + 1) * TOK, :]
 
         h_bf = {}
         h_w = {}
@@ -237,10 +251,10 @@ def tile_list_triangle_edge_update_kernel(
             for k in range(2):
                 message(q * QUARTER + k * TOK, b, ring)
 
-        def quantize_h(group, passes, over=None):
+        def quantize_h(group, passes, over=None, at=0):
             tok0, ntok = group
             if tok0 not in h_w:
-                h_w[tok0] = place(f"h_w{tok0}", [P, 2 * ntok], U32, over)
+                h_w[tok0] = place(f"h_w{tok0}", [P, 2 * ntok], U32, over, at)
                 h_s[tok0] = held.tile([P, 2 * ntok], U8, name=f"h_s{tok0}", align_bytes=64)
             cols = slice(passes[0] * ntok, (passes[-1] + 1) * ntok)
             values = h_bf[tok0][:].rearrange("p b n t -> p (b n t)")[:, 4 * cols.start : 4 * cols.stop]
@@ -341,21 +355,20 @@ def tile_list_triangle_edge_update_kernel(
         round_wa(0, True)
         pick_words(IK, 0, "tab_s")
         pick_words(IJ, 1, "tab_s", 2048)
-        product_on_gpsimd(0, 1, 0)
-        product_on_gpsimd(0, 1, 1)
+        products_on_gpsimd(0, 1, "wa_raw0")
         products_on_vector(0, 0)
         pick_words(JK, 1, "gate00")
+        pick_words(IK, 1, "gate00", 2048)
         round_wa(1, False)
-        gates(1, 1)
-        copy_b(1, 1)
+        gates(1, 1, "wa_raw1", 64)
+        copy_b(1, 1, "wa_raw1", 64 + 4096)
         quantize_wa(0, "b_out01")
         quantize_wa(1, "b_out01", 2048)
-        product_on_gpsimd(1, 1, 0, "wa_bf1")
-        product_on_gpsimd(1, 1, 1, "wa_bf1", 2048)
-        round_wo(1, True, over="gate11")
-        products_on_vector(1, 0, "wa_bf0")
+        products_on_gpsimd(1, 1, "wa_bf1", 64)
+        round_wo(1, True, pieces=1, over="gate11")
+        products_on_vector(1, 0, "wa_bf1", 64 - 4096)
         messages(0, 0, "scalar")
-        round_wo(0, False)
+        round_wo(0, False, over="wa_raw1", at=64 - 4096)
         messages(0, 1)
         messages(1, 0)
         messages(1, 1)
@@ -365,19 +378,17 @@ def tile_list_triangle_edge_update_kernel(
         gates(3, 1)
         copy_b(3, 1)
         gates(3, 0)
-        quantize_wo(0, "gb110")
-        quantize_wo(1, "gb10")
-        quantize_h(GROUPS[0], [0, 1])
-        pick_words(IK, 1, "gb111")
-        product_on_gpsimd(2, 1, 0, "h_bf0")
-        product_on_gpsimd(2, 1, 1, "h_bf0", 2048)
-        product_on_gpsimd(3, 1, 0, "h_bf0", 4096)
-        product_on_gpsimd(3, 1, 1, "h_bf0", 6144)
-        products_on_vector(2, 0)
-        message(512, 1)
+        quantize_wo(0, "wo_raw1")
+        quantize_h(GROUPS[0], [0, 1], "wo_raw1", 2048)
+        quantize_wo(1, "wo_raw1", 6144)
+        product_on_gpsimd(2, 1, 0, "wo_bf1")
+        product_on_gpsimd(2, 1, 1, "wo_bf1", 2048)
+        product_on_gpsimd(3, 1, 0, "gate21")
+        product_on_gpsimd(3, 1, 1, "gate21", 2048)
+        products_on_vector(2, 0, "h_bf0")
+        products_on_vector(3, 0, "h_bf0", 4096)
         messages(2, 0)
-        message(640, 1)
-        products_on_vector(3, 0)
+        messages(2, 1)
         tail = GROUPS[3]
         message(768, 0)
         quantize_h(GROUPS[1], [0, 1])

@@ -104,11 +104,17 @@ def tile_list_triangle_edge_update_kernel(
             v_w[i, h] = place(f"v_w{i}{h}", [P, HALF], U32, over, at)
             nc.vector.tensor_copy(v_w[i, h][:], tab_w[:].bitcast(U32).indirect(lists[i][:, 32 * h : 32 * h + 32]))
 
+        def pick_all_words(i):
+            whole = place(f"v_w{i}", [P, S], U32)
+            nc.vector.tensor_copy(whole[:], tab_w[:].bitcast(U32).indirect(lists[i][:]))
+            v_w[i, 0], v_w[i, 1] = whole[:, 0:HALF], whole[:, HALF:S]
+
         def picked(i, tok0, ntok):
             h, lo = divmod(tok0, HALF)
             return v_w[i, h][:, lo : lo + ntok].bitcast(FP8X4), v_s[i][:, tok0 : tok0 + ntok]
 
-        wa_bf = {}
+        wa_both = place("wa_bf", [P, 2, 4, P, 4], BF16)
+        wa_bf = [wa_both[:, b] for b in range(2)]
         wo_bf = {}
         wa_w = {}
         wo_w = {}
@@ -123,8 +129,7 @@ def tile_list_triangle_edge_update_kernel(
             for t in range(4):
                 nc.sync.dma_start(wo_raw[b][:, t, :], rows[b, t])
 
-        def round_wa(b, on_gpsimd, over=None):
-            wa_bf[b] = place(f"wa_bf{b}", [P, 4, P, 4], BF16, over, room=4096, lead=4096)
+        def round_wa(b, on_gpsimd):
             for t in range(4):
                 if on_gpsimd:
                     nc.gpsimd.tensor_scalar(
@@ -138,10 +143,11 @@ def tile_list_triangle_edge_update_kernel(
                         wa_raw[b][:].rearrange("p j (g t e i) -> p t g e j i", t=4, e=2, i=4)[:, t],
                     )
 
-        def round_wo(b, on_gpsimd, pieces=2, **where):
-            wo_bf[b] = place(f"wo_bf{b}", [P, N, 4], BF16, **where)
-            for c in range(pieces):
-                cols = slice(c * N // pieces, (c + 1) * N // pieces)
+        def round_wo(b, on_gpsimd, pieces=((0, N),), **where):
+            if b not in wo_bf:
+                wo_bf[b] = place(f"wo_bf{b}", [P, N, 4], BF16, **where)
+            for lo, hi in pieces:
+                cols = slice(lo, hi)
                 if on_gpsimd:
                     nc.gpsimd.tensor_scalar(
                         wo_bf[b][:, cols, :].rearrange("p (m i) t -> p m t i", i=2),
@@ -163,9 +169,10 @@ def tile_list_triangle_edge_update_kernel(
         def quantize(codes, scales, values):
             nc.vector.quantize_mx(out=codes.bitcast(FP8X4), scales=scales, in_=values)
 
-        def quantize_wa(b, over=None, at=0):
-            wa_w[b] = place(f"wa_w{b}", [P, PASS], U32, over, at)
-            quantize(wa_w[b][:], wa_s[:, b * PASS : (b + 1) * PASS], wa_bf[b][:].rearrange("p t m j -> p (t m j)"))
+        def quantize_wa(over):
+            codes = place("wa_w", [P, H], U32, over)
+            quantize(codes[:], wa_s[:], wa_both[:].rearrange("p b t m j -> p (b t m j)"))
+            wa_w[0], wa_w[1] = codes[:, 0:PASS], codes[:, PASS:H]
 
         def quantize_wo(b, over=None, at=0):
             wo_w[b] = place(f"wo_w{b}", [P, N], U32, over, at)
@@ -336,7 +343,7 @@ def tile_list_triangle_edge_update_kernel(
         pick_words(IJ, 0)
         pick_words(JK, 0)
         deal_columns(wb_w[:], wb_raw[:], nc.vector)
-        ik_rows = place("ik_rows", [P, S], U8, "wb_raw")
+        ik_rows = place("ik_rows", [P, S], U8)
         pick_scales(IK, ik_rows[:])
         load_wo(0)
         rows_to_plane(side_plane[IK], ik_rows[:].bitcast(I32), nc.sync)
@@ -353,31 +360,30 @@ def tile_list_triangle_edge_update_kernel(
         copy_b(0, 1)
         turns["scalar"] = turns["scalar"] + 1
         round_wa(0, True)
-        pick_words(IK, 0, "tab_s")
-        pick_words(IJ, 1, "tab_s", 2048)
+        pick_all_words(IK)
+        pick_words(IJ, 1, "tab_s")
+        pick_words(JK, 1, "tab_s", 2048)
         products_on_gpsimd(0, 1, "wa_raw0")
         products_on_vector(0, 0)
-        pick_words(JK, 1, "gate00")
-        pick_words(IK, 1, "gate00", 2048)
         round_wa(1, False)
         gates(1, 1, "wa_raw1", 64)
         copy_b(1, 1, "wa_raw1", 64 + 4096)
-        quantize_wa(0, "b_out01")
-        quantize_wa(1, "b_out01", 2048)
-        products_on_gpsimd(1, 1, "wa_bf1", 64)
-        round_wo(1, True, pieces=1, over="gate11")
-        products_on_vector(1, 0, "wa_bf1", 64 - 4096)
-        messages(0, 0, "scalar")
+        quantize_wa("b_out01")
+        products_on_gpsimd(1, 1, "wa_bf")
+        round_wo(1, True, ((128, N),), over="gate11")
+        products_on_vector(1, 0, "wa_bf", 4096)
+        messages(0, 0, "y")
         round_wo(0, False, over="wa_raw1", at=64 - 4096)
         messages(0, 1)
         messages(1, 0)
         messages(1, 1)
         gates(2, 1)
         copy_b(2, 1)
+        round_wo(1, False, ((0, 128),))
         gates(2, 0)
+        gates(3, 0)
         gates(3, 1)
         copy_b(3, 1)
-        gates(3, 0)
         quantize_wo(0, "wo_raw1")
         quantize_h(GROUPS[0], [0, 1], "wo_raw1", 2048)
         quantize_wo(1, "wo_raw1", 6144)
@@ -398,6 +404,7 @@ def tile_list_triangle_edge_update_kernel(
         quantize_h(tail, [0])
         message(896, 1)
         rings["y"] = [6, 7, 0, 1, 2]
+        turns["y"] = 0
         for c in range(4):
             whole_y(GROUPS[0], [c])
         for cs in ([0, 1], [2, 3]):

from contextlib import ExitStack

import concourse.mybir as mybir

K, H, N, T, S = 512, 1024, 512, 4096, 1024
FLOPS = 2 * S * (3 * K * H + K * N + H * N)

F32 = mybir.dt.float32
BF16 = mybir.dt.bfloat16
I32 = mybir.dt.int32
U32 = mybir.dt.uint32
U16 = mybir.dt.uint16
U8 = mybir.dt.uint8
FP8X4 = mybir.dt.float8_e4m3fn_x4
FP4X4 = mybir.dt.float4_e2m1fn_x4
ACT = mybir.ActivationFunctionType
ALU = mybir.AluOpType

P = 128
PASS = 512
HALF = 512
QUARTER = 256
TOK = 128
IJ, IK, JK = 0, 1, 2
GROUPS = [(0, 512), (512, 256), (768, 128), (896, 128)]
H_PLACE = {}
SIZE = {F32: 4, I32: 4, U32: 4, BF16: 2, U8: 1}


def tile_list_triangle_edge_update_kernel(
    tc, tab_words, tab_scales, offs, offs2, offs3, wg_words, wg_scales, wa, wb_words, wb_scales,
    wr_words, wr_scales, wo, bo, out,
):
    nc = tc.nc
    with ExitStack() as ctx:
        held = ctx.enter_context(tc.tile_pool(name="held", bufs=1))
        shared = ctx.enter_context(tc.tile_pool(name="shared", bufs=1))
        psum = ctx.enter_context(tc.psum_pool(name="psum", bufs=1))
        banks = [psum.tile([P, 512], F32, name=f"bank{i}") for i in range(8)]
        rings = {"scalar": [0, 1, 2], "vector": [3, 4, 5], "y": [6, 7]}
        turns = {"scalar": 0, "vector": 0, "y": 0}

        def next_bank(ring, rows):
            bank = banks[rings[ring][turns[ring] % len(rings[ring])]]
            turns[ring] = turns[ring] + 1
            return bank[:].rearrange("p (r n) -> p r n", r=rows)

        places = {"free": (0, 0, 0)}

        def place(name, shape, dtype, over=None, at=0, room=0, lead=0):
            size = SIZE[dtype]
            for extent in shape[1:]:
                size = size * extent
            if over is None:
                start = places["free"][0] + lead
                places["free"] = (start + size + room, 0, 0)
                places[name] = (start, size + room, lead)
            else:
                start = places[over][0] + at
                assert -at <= places[over][2] and at + size <= places[over][1], name
                places[name] = (start, places[over][1] - at, places[over][2] + at)
            return shared.tile(shape, dtype, name=name, align_bytes=64, offset=start)

        ROWS = slice(P - 16, P)
        REST = slice(0, P - 16)
        lists = [held.tile([P, S // 16], U16, name=f"list{i}") for i in range(3)]
        tab_w = held.tile([P, T], I32, name="tab_w", align_bytes=64)
        tab_s = place("tab_s", [P, T // 4], I32)
        raw_s = place("raw_s", [P, H // 2], I32)
        early_rows = place("early_rows", [P, 3 * H // 4], I32)
        early_plane = held.tile([P, 3 * H // 4], I32, name="early_plane", align_bytes=64)
        side_plane = {i: held.tile([P, S // 4], I32, name=f"side_plane{i}", align_bytes=64) for i in (JK, IK)}
        early = early_plane[:].bitcast(U8)
        v_s = {IJ: early[:, 2 * H : 2 * H + S], JK: side_plane[JK][:].bitcast(U8), IK: side_plane[IK][:].bitcast(U8)}
        wr_plane = held.tile([P, N // 4], I32, name="wr_plane", align_bytes=64)
        wg_raw = place("wg_raw", [P, H // 2], I32)
        wb_raw = place("wb_raw", [P, H], I32)
        wg_w = held.tile([P, H // 2], I32, name="wg_w", align_bytes=64)
        wb_w = held.tile([P, H], I32, name="wb_w", align_bytes=64)
        wr_w = held.tile([P, 2 * N], U8, name="wr_w", align_bytes=64)
        bias = held.tile([P, N // P], F32, name="bias")
        wa_raw = [place(f"wa_raw{b}", [P, 4, PASS], F32, lead=4096 * b, room=64 * b) for b in range(2)]
        wo_raw = [place(f"wo_raw{b}", [P, 4, N], F32) for b in range(2)]
        wg_s = early[:, 0:H]
        wb_s = early[:, H : 2 * H]
        wr_s = wr_plane[:].bitcast(U8)

        def rows_to_plane(plane, rows, queue):
            for q in range(4):
                queue.dma_start(plane[32 * q : 32 * q + 4, :], rows[P - 16 + 4 * q : P - 12 + 4 * q, :])

        def deal_columns(dst, src, engine, passes=2):
            engine.tensor_copy(
                dst.rearrange("p (b t g e) -> p b t g e", b=passes, t=4, g=16),
                src.rearrange("p (b g t e) -> p b t g e", b=passes, t=4, g=16),
            )

        v_w = {}

        def pick_scales(i, rows):
            nc.vector.tensor_copy(rows, tab_s[:].bitcast(U8).indirect(lists[i][:]))

        def pick_words(i, h, over=None, at=0):
            v_w[i, h] = place(f"v_w{i}{h}", [P, HALF], U32, over, at)
            nc.vector.tensor_copy(v_w[i, h][:], tab_w[:].bitcast(U32).indirect(lists[i][:, 32 * h : 32 * h + 32]))

        def pick_all_words(i):
            whole = place(f"v_w{i}", [P, S], U32)
            nc.vector.tensor_copy(whole[:], tab_w[:].bitcast(U32).indirect(lists[i][:]))
            v_w[i, 0], v_w[i, 1] = whole[:, 0:HALF], whole[:, HALF:S]

        def picked(i, tok0, ntok):
            h, lo = divmod(tok0, HALF)
            return v_w[i, h][:, lo : lo + ntok].bitcast(FP8X4), v_s[i][:, tok0 : tok0 + ntok]

        wa_both = place("wa_bf", [P, 2, 4, P, 4], BF16)
        wa_bf = [wa_both[:, b] for b in range(2)]
        wo_bf = {}
        wa_w = {}
        wo_w = {}
        wa_s = held.tile([P, H], U8, name="wa_s", align_bytes=64)
        wo_s = held.tile([P, 2 * N], U8, name="wo_s", align_bytes=64)

        def load_wa(b):
            nc.sync.dma_start(wa_raw[b][:], wa.rearrange("(p j) c -> p j c", j=4)[:, :, b * PASS : (b + 1) * PASS])

        def load_wo(b):
            rows = wo.rearrange("(b g t e) n -> b t g e n", b=2, t=4, e=8)
            for t in range(4):
                nc.sync.dma_start(wo_raw[b][:, t, :], rows[b, t])

        def round_wa(b, on_gpsimd):
            for t in range(4):
                if on_gpsimd:
                    nc.gpsimd.tensor_scalar(
                        wa_bf[b][:, t].rearrange("p (g e) j -> p g j e", e=8),
                        wa_raw[b][:].rearrange("p j (g t e) -> p t g j e", t=4, e=8)[:, t],
                        1.0, 0.0, ALU.mult, ALU.add,
                    )
                else:
                    nc.scalar.copy(
                        wa_bf[b][:, t].rearrange("p (g e i) j -> p g e j i", e=2, i=4),
                        wa_raw[b][:].rearrange("p j (g t e i) -> p t g e j i", t=4, e=2, i=4)[:, t],
                    )

        def round_wo(b, on_gpsimd, pieces=((0, N),), **where):
            if b not in wo_bf:
                wo_bf[b] = place(f"wo_bf{b}", [P, N, 4], BF16, **where)
            for lo, hi in pieces:
                cols = slice(lo, hi)
                if on_gpsimd:
                    nc.gpsimd.tensor_scalar(
                        wo_bf[b][:, cols, :].rearrange("p (m i) t -> p m t i", i=2),
                        wo_raw[b][:, :, cols].rearrange("p t (m i) -> p m t i", i=2),
                        1.0, 0.0, ALU.mult, ALU.add,
                    )
                else:
                    nc.scalar.copy(
                        wo_bf[b][:, cols, :].rearrange("p (m i) t -> p m t i", i=4),
                        wo_raw[b][:, :, cols].rearrange("p t (m i) -> p m t i", i=4),
                    )

        def round_wo_on_vector(b, **where):
            wo_bf[b] = place(f"wo_bf{b}", [P, N, 4], BF16, **where)
            nc.vector.tensor_copy(
                wo_bf[b][:].rearrange("p (m i) t -> p m t i", i=4), wo_raw[b][:].rearrange("p t (m i) -> p m t i", i=4)
            )

        def quantize(codes, scales, values):
            nc.vector.quantize_mx(out=codes.bitcast(FP8X4), scales=scales, in_=values)

        def quantize_wa(over):
            codes = place("wa_w", [P, H], U32, over)
            quantize(codes[:], wa_s[:], wa_both[:].rearrange("p b t m j -> p (b t m j)"))
            wa_w[0], wa_w[1] = codes[:, 0:PASS], codes[:, PASS:H]

        def quantize_wo(b, over=None, at=0):
            wo_w[b] = place(f"wo_w{b}", [P, N], U32, over, at)
            quantize(wo_w[b][:], wo_s[:, b * N : (b + 1) * N], wo_bf[b][:].rearrange("p n t -> p (n t)"))

        def lone_pass(dst, codes, scales, rhs):
            nc.tensor.matmul_mx(
                out=dst, lhsT=codes, lhsT_scale=scales, rhs=rhs[0], rhs_scale=rhs[1], start=True, stop=True
            )

        gate = {}
        b_out = {}
        gb = {}

        def gates(q, b, over=None, at=0):
            gate[q, b] = place(f"gate{q}{b}", [P, 2, QUARTER, 2], F32, over, at)
            for s in range(2):
                bank = next_bank("scalar", 2)
                for u in range(2):
                    c0 = b * PASS + (2 * s + u) * P
                    lone_pass(
                        bank[:, u, :], wg_w[:].bitcast(U8)[:, 2 * c0 : 2 * c0 + 2 * P].bitcast(FP4X4),
                        wg_s[:, c0 : c0 + P], picked(IJ, q * QUARTER, QUARTER),
                    )
                nc.scalar.activation(gate[q, b][:, s], bank.rearrange("p u n -> p n u"), ACT.Sigmoid)

        def b_pair(q, b, s, ring):
            bank = next_bank(ring, 2)
            for u in range(2):
                c0 = b * PASS + (2 * s + u) * P
                lone_pass(
                    bank[:, u, :], wb_w[:, c0 : c0 + P].bitcast(FP8X4), wb_s[:, c0 : c0 + P], picked(JK, q * QUARTER, QUARTER)
                )
            return bank.rearrange("p u n -> p n u")

        def products_on_vector(q, b, over=None, at=0):
            both = place(f"gb{q}{b}", [P, 2, QUARTER, 2], F32, over, at)
            for s in range(2):
                nc.vector.tensor_tensor(both[:, s], b_pair(q, b, s, "vector"), gate[q, b][:, s], ALU.mult)
            for k in range(2):
                gb[q, b, k] = both[:, :, k * TOK : (k + 1) * TOK, :]

        def copy_b(q, b, over=None, at=0):
            b_out[q, b] = place(f"b_out{q}{b}", [P, 2, QUARTER, 2], F32, over, at)
            for s in range(2):
                nc.scalar.copy(b_out[q, b][:, s], b_pair(q, b, s, "scalar"))

        def product_on_gpsimd(q, b, k, over=None, at=0):
            cols = slice(k * TOK, (k + 1) * TOK)
            gb[q, b, k] = place(f"gb{q}{b}{k}", [P, 2, TOK, 2], F32, over, at)[:]
            nc.gpsimd.tensor_tensor(
                gb[q, b, k].rearrange("p s n u -> p s (n u)"), b_out[q, b][:, :, cols, :].rearrange("p s n u -> p s (n u)"),
                gate[q, b][:, :, cols, :].rearrange("p s n u -> p s (n u)"), ALU.mult,
            )

        def products_on_gpsimd(q, b, over=None, at=0):
            both = place(f"gb{q}{b}", [P, 2, QUARTER, 2], F32, over, at)
            nc.gpsimd.tensor_tensor(both[:], b_out[q, b][:], gate[q, b][:], ALU.mult)
            for k in range(2):
                gb[q, b, k] = both[:, :, k * TOK : (k + 1) * TOK, :]

        h_bf = {}
        h_w = {}
        h_s = {}

        def message(tok, b, ring="vector"):
            q, k = divmod(tok // TOK, 2)
            first, ntok = max(group for group in GROUPS if group[0] <= tok)
            if first not in h_bf:
                h_bf[first] = place(f"h_bf{first}", [P, 2, ntok, 4], BF16, **H_PLACE.get(first, {}))
            bank = next_bank(ring, 4)
            for t in range(4):
                c0 = b * PASS + t * P
                lone_pass(bank[:, t, :], wa_w[b][:, t * P : (t + 1) * P].bitcast(FP8X4), wa_s[:, c0 : c0 + P], picked(IK, tok, TOK))
            nc.vector.tensor_tensor(
                h_bf[first][:, b, tok - first : tok - first + TOK, :].rearrange("p n (s u) -> p n s u", s=2),
                bank.rearrange("p (s u) n -> p n s u", s=2),
                gb[q, b, k].rearrange("p s n u -> p n s u"),
                ALU.mult,
            )

        def messages(q, b, ring="vector"):
            for k in range(2):
                message(q * QUARTER + k * TOK, b, ring)

        def quantize_h(group, passes, over=None, at=0):
            tok0, ntok = group
            if tok0 not in h_w:
                h_w[tok0] = place(f"h_w{tok0}", [P, 2 * ntok], U32, over, at)
                h_s[tok0] = held.tile([P, 2 * ntok], U8, name=f"h_s{tok0}", align_bytes=64)
            cols = slice(passes[0] * ntok, (passes[-1] + 1) * ntok)
            values = h_bf[tok0][:].rearrange("p b n t -> p (b n t)")[:, 4 * cols.start : 4 * cols.stop]
            quantize(h_w[tok0][:, cols], h_s[tok0][:, cols], values)

        y_bank = {}

        def open_y(group, cs):
            tok0, ntok = group
            y_bank[tok0, cs[0]] = next_bank("y", 512 // ntok)
            width = ntok if ntok == HALF else TOK
            for c in cs:
                for lo in range(0, ntok, width):
                    rhs = picked(IJ, tok0 + lo, width)
                    nc.tensor.matmul_mx(
                        out=y_bank[tok0, cs[0]][:, c - cs[0], lo : lo + width],
                        lhsT=wr_w[:, 2 * c * P : 2 * (c + 1) * P].bitcast(FP4X4), lhsT_scale=wr_s[:, c * P : (c + 1) * P],
                        rhs=rhs[0], rhs_scale=rhs[1], start=(c == cs[0] and lo == 0), stop=False,
                    )

        def add_to_y(group, cs, b):
            tok0, ntok = group
            for c in cs:
                nc.tensor.matmul_mx(
                    out=y_bank[tok0, cs[0]][:, c - cs[0], :],
                    lhsT=wo_w[b][:, c * P : (c + 1) * P].bitcast(FP8X4), lhsT_scale=wo_s[:, b * N + c * P : b * N + (c + 1) * P],
                    rhs=h_w[tok0][:, b * ntok : (b + 1) * ntok].bitcast(FP8X4), rhs_scale=h_s[tok0][:, b * ntok : (b + 1) * ntok],
                    start=False, stop=(b == 1 and c == cs[-1]),
                )

        def store_y(group, cs, on_vector=False):
            tok0, ntok = group
            y = held.tile([P, len(cs), ntok], F32, name=f"y{tok0}_{cs[0]}")
            for c in cs:
                src = y_bank[tok0, cs[0]][:, c - cs[0], :]
                if on_vector:
                    nc.vector.tensor_scalar(y[:, c - cs[0], :], src, bias[:, c : c + 1], None, ALU.add)
                else:
                    nc.scalar.activation(y[:, c - cs[0], :], src, ACT.Identity, bias=bias[:, c : c + 1])
            dst = out.rearrange("(c p) s -> p c s", p=P)[:, cs[0] : cs[-1] + 1, tok0 : tok0 + ntok]
            nc.sync.dma_start(dst, y[:])

        def close_y(group, cs):
            for b in range(2):
                add_to_y(group, cs, b)
            store_y(group, cs)

        def whole_y(group, cs):
            open_y(group, cs)
            close_y(group, cs)

        nc.scalar.dma_start(tab_s[ROWS, :], tab_scales[0].bitcast(I32))
        nc.scalar.dma_start(raw_s[ROWS, H // 4 : H // 2], wb_scales[0].bitcast(I32))
        nc.sync.dma_start(lists[IJ][:], offs)
        nc.sync.dma_start(lists[JK][:], offs3)
        nc.sync.dma_start(raw_s[ROWS, 0 : H // 4], wg_scales[0].bitcast(I32))
        nc.sync.dma_start(wg_raw[:], wg_words[0].bitcast(I32))
        nc.sync.dma_start(tab_w[:], tab_words[0].rearrange("p t i -> p (t i)").bitcast(I32))
        nc.vector.memset(tab_s[REST, :], 0)
        nc.vector.memset(raw_s[REST, :], 0)
        warm = held.tile([P, 2], F32, name="warm")
        nc.vector.memset(warm[:, 0:1], 0.0)
        nc.scalar.activation(warm[:, 1:2], warm[:, 0:1], ACT.Sigmoid)
        for plane in (early_plane, side_plane[JK], side_plane[IK], wr_plane):
            nc.gpsimd.memset(plane[:], 0)
        deal_columns(wg_w[:], wg_raw[:], nc.gpsimd)
        ij_rows = place("ij_rows", [P, S], U8)
        pick_scales(IJ, ij_rows[:])
        deal_columns(early_rows[:, 0 : H // 2], raw_s[:], nc.vector, passes=4)
        nc.vector.tensor_copy(early_rows[:, H // 2 : 3 * H // 4], ij_rows[:].bitcast(I32))
        rows_to_plane(early_plane, early_rows[:], nc.sync)
        nc.sync.dma_start(wb_raw[:], wb_words[0].rearrange("p c i -> p (c i)").bitcast(I32))
        nc.sync.dma_start(lists[IK][:], offs2)
        load_wa(0)
        jk_rows = place("jk_rows", [P, S], U8, "raw_s")
        pick_scales(JK, jk_rows[:])
        rows_to_plane(side_plane[JK], jk_rows[:].bitcast(I32), nc.sync)
        load_wa(1)
        pick_words(IJ, 0)
        pick_words(JK, 0)
        deal_columns(wb_w[:], wb_raw[:], nc.vector)
        ik_rows = place("ik_rows", [P, S], U8)
        pick_scales(IK, ik_rows[:])
        load_wo(0)
        rows_to_plane(side_plane[IK], ik_rows[:].bitcast(I32), nc.sync)
        load_wo(1)
        nc.sync.dma_start(wr_w[:].bitcast(I32), wr_words[0].bitcast(I32))
        for r in range(4):
            nc.sync.dma_start(wr_plane[r:P:32, :], wr_scales[0, r:16:4, :].bitcast(I32))
        with nc.allow_non_contiguous_dma(reason="one bias value a partition"):
            nc.sync.dma_start(bias[:], bo.rearrange("(c p) -> p c", p=P))

        gates(0, 0)
        gates(0, 1)
        gates(1, 0)
        copy_b(0, 1)
        turns["scalar"] = turns["scalar"] + 1
        round_wa(0, True)
        pick_all_words(IK)
        pick_words(IJ, 1, "tab_s")
        pick_words(JK, 1, "tab_s", 2048)
        products_on_gpsimd(0, 1, "wa_raw0")
        products_on_vector(0, 0)
        round_wa(1, False)
        gates(1, 1, "wa_raw1", 64)
        copy_b(1, 1, "wa_raw1", 64 + 4096)
        quantize_wa("b_out01")
        products_on_gpsimd(1, 1, "wa_bf")
        round_wo(1, True, ((128, N),), over="gate11")
        products_on_vector(1, 0, "wa_bf", 4096)
        messages(0, 0, "y")
        round_wo(0, False, over="wa_raw1", at=64 - 4096)
        messages(0, 1)
        messages(1, 0)
        messages(1, 1)
        gates(2, 1)
        copy_b(2, 1)
        round_wo(1, False, ((0, 128),))
        gates(2, 0)
        gates(3, 0)
        gates(3, 1)
        copy_b(3, 1)
        quantize_wo(0, "wo_raw1")
        quantize_h(GROUPS[0], [0, 1], "wo_raw1", 2048)
        quantize_wo(1, "wo_raw1", 6144)
        product_on_gpsimd(2, 1, 0, "wo_bf1")
        product_on_gpsimd(2, 1, 1, "wo_bf1", 2048)
        product_on_gpsimd(3, 1, 0, "gate21")
        product_on_gpsimd(3, 1, 1, "gate21", 2048)
        products_on_vector(2, 0, "h_bf0")
        products_on_vector(3, 0, "h_bf0", 4096)
        messages(2, 0)
        messages(2, 1)
        tail = GROUPS[3]
        message(768, 0)
        quantize_h(GROUPS[1], [0, 1])
        message(768, 1)
        message(896, 0)
        quantize_h(GROUPS[2], [0, 1])
        quantize_h(tail, [0])
        message(896, 1)
        rings["y"] = [6, 7, 0, 1, 2]
        turns["y"] = 0
        for c in range(4):
            whole_y(GROUPS[0], [c])
        for cs in ([0, 1], [2, 3]):
            whole_y(GROUPS[1], cs)
        whole_y(GROUPS[2], [0, 1, 2, 3])
        for cs in ([0, 1], [2, 3]):
            open_y(tail, cs)
            add_to_y(tail, cs, 0)
        quantize_h(tail, [1])
        for cs in ([0, 1], [2, 3]):
            add_to_y(tail, cs, 1)
            store_y(tail, cs, on_vector=(cs[0] == 0))
